import numpy as np
import ml_dtypes


def mxq(x, axis, fmt="e4m3"):
    dtype, down = {"e4m3": (ml_dtypes.float8_e4m3fn, 7), "e5m2": (ml_dtypes.float8_e5m2, 14)}[fmt]
    v = np.moveaxis(np.asarray(x, np.float32).astype(ml_dtypes.bfloat16).astype(np.float64), axis, -1)
    blocks = v.reshape(v.shape[:-1] + (-1, 32))
    amax = np.abs(blocks).max(-1, keepdims=True)
    byte = np.maximum(np.where(amax > 0, np.frexp(amax)[1] - 1 + 127, 0) - down, 1)
    scale = np.exp2(byte - 127.0)
    codes = (blocks / scale).astype(np.float32).astype(dtype).astype(np.float64)
    return np.moveaxis((codes * scale).reshape(v.shape), -1, axis)


WIDE = False


def mx_kscale(k):
    if not WIDE:
        return np.ones(k)
    levels = np.array([10, -10, 5, -5, 0])
    if k % 512:
        return np.exp2(np.random.permutation(np.resize(levels, k // 32))).repeat(32)
    a = np.empty((k // 512, 16))
    for p in range(k // 512):
        a[p, :8] = np.random.permutation(np.resize(levels, 8))
        for g in range(8):
            far = levels[np.abs(levels - a[p, g]) >= 10]
            a[p, g + 8] = far[np.random.randint(len(far))]
    return np.exp2(a.ravel()).repeat(32)


def f64(x):
    return np.asarray(x).astype(np.float64)


def striped(idx):
    return np.tile(idx.reshape(-1, 16).T, (8, 1)).astype(np.uint16)


def unstriped(offs):
    return offs[:16].T.reshape(-1).astype(np.int64)


E2M1 = np.array([0.0, 0.5, 1.0, 1.5, 2.0, 3.0, 4.0, 6.0, -0.0, -0.5, -1.0, -1.5, -2.0, -3.0, -4.0, -6.0])


def pack_weight(w, fmt):
    k, n = w.shape
    w = f64(np.asarray(w, np.float32).astype(ml_dtypes.bfloat16)).reshape(k // 32, 32, n)
    amax = np.abs(w).max(1)
    if fmt == "e4m3":
        byte = np.frexp(amax)[1] - 1 + 127 - 7
    else:
        mant, ex = np.frexp(amax / 6.0)
        byte = np.where(mant > 0.5, ex, ex - 1) + 127
    byte = np.clip(np.where(amax > 0, byte, 1), 1, 254)
    scaled = (w * np.exp2(127.0 - byte)[:, None, :]).reshape(k, n).astype(np.float32)
    by_word = np.ascontiguousarray(scaled.reshape(k // 512, 128, 4, n).transpose(0, 1, 3, 2))
    if fmt == "e4m3":
        words = by_word.astype(ml_dtypes.float8_e4m3fn).view(np.uint8)
    else:
        c = by_word.astype(ml_dtypes.float4_e2m1fn).view(np.uint8) & 0xF
        words = (c[..., 0::2] | (c[..., 1::2] << 4)).reshape(k // 512, 128, 2 * n)
    return np.ascontiguousarray(words), np.ascontiguousarray(byte.astype(np.uint8).reshape(k // 512, 16, n))


def unpack_weight(words, scales, fmt):
    g, _, n = scales.shape
    words = np.ascontiguousarray(words).reshape(g, 128, n, -1)
    if fmt == "e4m3":
        vals = words.view(ml_dtypes.float8_e4m3fn).astype(np.float64)
    else:
        nib = np.empty((g, 128, n, 4), np.uint8)
        nib[..., 0::2] = words & 0xF
        nib[..., 1::2] = words >> 4
        vals = E2M1[nib]
    vals = vals * np.repeat(np.exp2(scales.astype(np.float64) - 127.0), 8, axis=1)[..., None]
    return vals.transpose(0, 1, 3, 2).reshape(g * 512, n)


K, T, E, C, H, N, TOP = 1024, 768, 9, 256, 512, 128, 3


def by_expert(wq, xq):
    return np.concatenate([wq[e].T @ xq[:, e * C:(e + 1) * C] for e in range(E)], axis=1)


def setup_inputs():
    n = np.random.standard_normal
    s = mx_kscale(K)
    u = mx_kscale(H)
    deal = np.repeat(np.arange(E), C).reshape(TOP, T)[:, np.random.permutation(T)]
    deal = np.take_along_axis(deal, np.argsort(np.random.rand(TOP, T), axis=0), axis=0)
    for _ in range(8):
        s_, t_ = np.random.permutation(T).reshape(2, -1); r = np.random.randint(TOP, size=T // 2); x, y = deal[r, s_].copy(), deal[r, t_].copy()
        ok = ~((deal[:, s_] == y).any(0) | (deal[:, t_] == x).any(0)); deal[r[ok], s_[ok]] = y[ok]; deal[r[ok], t_[ok]] = x[ok]
    order = np.lexsort((np.random.rand(TOP * T), deal.reshape(-1)))
    slot_token = order % T; pos = np.empty(TOP * T, np.int64); pos[order] = np.arange(TOP * T); pos = pos.reshape(TOP, T)
    g = np.random.uniform(0.5, 1.5, (TOP, T)); g = g / g.sum(0)
    x = pack_weight(n((K, T)) * s[:, None], "e4m3")
    w = pack_weight(n((K, N)) / np.sqrt(K) / s[:, None], "e2m1")
    wa = [pack_weight(m, "e2m1") for m in n((E, K, H)) / np.sqrt(K) / s[None, :, None] * u]
    wb = [pack_weight(m, "e2m1") for m in n((E, H, N)) / np.sqrt(H) / u[None, :, None]]
    return {
        "x_words": x[0],
        "x_scales": x[1],
        "w_words": w[0],
        "w_scales": w[1],
        "wa_words": np.stack([m[0] for m in wa]),
        "wa_scales": np.stack([m[1] for m in wa]),
        "wb_words": np.stack([m[0] for m in wb]),
        "wb_scales": np.stack([m[1] for m in wb]),
        "gate": np.stack([np.tile(r, (128, 1)) for r in g]).astype(np.float32),
        "offs": striped(slot_token),
        "pos1": striped(pos[0]),
        "pos2": striped(pos[1]),
        "pos3": striped(pos[2]),
    }


def reference(x_words, x_scales, w_words, w_scales, wa_words, wa_scales, wb_words, wb_scales, gate, offs, pos1, pos2, pos3):
    w = unpack_weight(w_words, w_scales, "e2m1")
    wa = np.stack([unpack_weight(wa_words[e], wa_scales[e], "e2m1") for e in range(E)])
    wb = np.stack([unpack_weight(wb_words[e], wb_scales[e], "e2m1") for e in range(E)])
    idx = unstriped(offs)
    x = unpack_weight(x_words, x_scales, "e4m3")
    base = w.T @ x
    h = by_expert(wa, x[:, idx])
    y = by_expert(wb, mxq(h, 0, "e4m3"))
    c = sum(f64(gate[r, :1]) * y[:, unstriped(p)] for r, p in enumerate((pos1, pos2, pos3)))
    return base + c

@@ -1,0 +1,253 @@
+from contextlib import ExitStack
+
+import concourse.mybir as mybir
+from concourse.masks import make_identity
+
+K, T, E, C, H, N, TOP = 1024, 768, 9, 256, 512, 128, 3
+FLOPS = 2 * K * N * T + 2 * E * C * (K * H + H * N)
+
+F32 = mybir.dt.float32
+BF16 = mybir.dt.bfloat16
+I32 = mybir.dt.int32
+U32 = mybir.dt.uint32
+U16 = mybir.dt.uint16
+U8 = mybir.dt.uint8
+FP8X4 = mybir.dt.float8_e4m3fn_x4
+FP4X4 = mybir.dt.float4_e2m1fn_x4
+COPY = mybir.ActivationFunctionType.Copy
+
+P = 128
+PASSES = K // 512
+SLOTS = E * C
+BANK = 512
+CHUNKS = [(0, 1), (1, 3), (3, 5), (5, 7), (7, 9)]
+EARLY = 3
+HALF = T // 2
+BLOCKS = T // P
+
+
+def tile_moe_adp_none_kernel(
+    tc, x_words, x_scales, w_words, w_scales, wa_words, wa_scales, wb_words, wb_scales, gate, offs, pos1, pos2, pos3, out
+):
+    nc = tc.nc
+    with ExitStack() as ctx:
+        keep = ctx.enter_context(tc.tile_pool(name="keep", bufs=1))
+        ring = ctx.enter_context(tc.tile_pool(name="ring", bufs=2))
+        psum = ctx.enter_context(tc.psum_pool(name="psum", bufs=2))
+
+        def zeroed_plane(cols, name, engine):
+            plane = keep.tile([P, cols], U8, name=name, align_bytes=64)
+            engine.memset(plane[:].bitcast(I32), 0)
+            return plane
+
+        def load_scale_rows(plane, rows, queues):
+            groups = rows.shape[0]
+            for q in range(4):
+                queues[q % len(queues)].dma_start(
+                    out=plane[32 * q : 32 * q + 4, :].rearrange("b (g n) -> b g n", g=groups).bitcast(I32),
+                    in_=rows[:, 4 * q : 4 * q + 4, :].rearrange("g b n -> b g n").bitcast(I32),
+                )
+
+        def shift_second_pass(dst, src, queue):
+            queue.dma_start(out=dst[0:112, :].bitcast(I32), in_=src[4:116, :].bitcast(I32))
+
+        offs_sb = keep.tile([P, SLOTS // 16], U16, name="offs_sb")
+        nc.sync.dma_start(offs_sb[:], offs)
+        xs = zeroed_plane(T, "xs", nc.gpsimd)
+        for q in range(4):
+            (nc.sync, nc.scalar)[q // 2].dma_start(
+                out=xs[32 * q : 32 * q + 8, :].bitcast(I32), in_=x_scales[:, 4 * q : 4 * q + 4, :].bitcast(I32)
+            )
+        xw = keep.tile([P, PASSES, T], I32, name="xw", align_bytes=64)
+        nc.sync.dma_start(out=xw[:], in_=x_words.rearrange("s p t d -> p s (t d)").bitcast(I32))
+        wa_rows = wa_scales.rearrange("e s b n -> (e s) b n")
+        was_early = zeroed_plane(EARLY * PASSES * H, "was_early", nc.vector)
+        slot_s1 = zeroed_plane(SLOTS, "slot_s1", nc.vector)
+        was_late = zeroed_plane((E - EARLY) * PASSES * H, "was_late", nc.vector)
+        wbs = zeroed_plane(E * N, "wbs", nc.vector)
+        ws = zeroed_plane(PASSES * N, "ws", nc.vector)
+        xs1 = zeroed_plane(T, "xs1", nc.vector)
+        ident = keep.tile([P, P], F32, name="ident")
+        make_identity(nc, ident[:])
+        gate_rows = keep.tile([P, P], F32, name="gate_rows")
+        nc.gpsimd.memset(gate_rows[:], 0.0)
+
+        y = keep.tile([P, SLOTS], F32, name="y")
+
+        def load_wa(first, last, queue):
+            waw = ring.tile([P, (last - first) * PASSES, 2 * H], U8, name="waw", align_bytes=64)
+            queue.dma_start(
+                out=waw[:].bitcast(I32), in_=wa_words[first:last].rearrange("e s p n -> p (e s) n").bitcast(I32)
+            )
+            return waw
+
+        def gather_scales(first, last, queue):
+            lo, hi = first * C, last * C
+            slot_s0 = ring.tile([P, hi - lo], U8, name="slot_s0", align_bytes=64)
+            nc.vector.tensor_copy(slot_s0[:], xs[:].indirect(offs_sb[:, lo // 16 : hi // 16]))
+            shift_second_pass(slot_s1[:, lo:hi], slot_s0[:], queue)
+            return slot_s0
+
+        def gather_words(e):
+            words = []
+            for s in range(PASSES):
+                slot_w = ring.tile([P, C], I32, name="slot_w", bufs=4, align_bytes=64)
+                nc.vector.tensor_copy(
+                    slot_w[:].bitcast(U32),
+                    xw[:, s, :].bitcast(U32).indirect(offs_sb[:, e * C // 16 : (e + 1) * C // 16]),
+                )
+                words.append(slot_w)
+            return words
+
+        def copy_out(on_vector, dst, src):
+            if on_vector:
+                nc.vector.tensor_copy(out=dst, in_=src)
+            else:
+                nc.scalar.copy(out=dst, in_=src)
+
+        def adapter(e, first, waw, slot_s0, words):
+            was, e0 = (was_early, 0) if e < EARLY else (was_late, EARLY)
+            turned = psum.tile([P, 2, 2, P], F32, name="turned")
+            for b in range(2):
+                h_t = psum.tile([P, H], F32, name="h_t", bufs=3)
+                for s in range(PASSES):
+                    col = e * C + b * P
+                    plane = slot_s0[:, col - first * C : col - first * C + P] if s == 0 else slot_s1[:, col : col + P]
+                    g = (e - e0) * PASSES + s
+                    nc.tensor.matmul_mx(
+                        out=h_t[:],
+                        lhsT=words[s][:, b * P : (b + 1) * P].bitcast(FP8X4),
+                        lhsT_scale=plane,
+                        rhs=waw[:, (e - first) * PASSES + s, :].bitcast(FP4X4),
+                        rhs_scale=was[:, g * H : (g + 1) * H],
+                        start=(s == 0),
+                        stop=(s == PASSES - 1),
+                    )
+                h_bf = ring.tile([P, H], BF16, name="h_bf", bufs=4)
+                dst = h_bf[:].rearrange("p (u m d) -> p u m d", u=2, d=2)
+                src = h_t[:].rearrange("p (m u d) -> p u m d", u=2, d=2)
+                if (e, b) in H_ON_VECTOR:
+                    nc.vector.tensor_copy(out=dst, in_=src)
+                else:
+                    nc.scalar.activation(out=dst, in_=src, func=COPY)
+                pairs = h_bf[:].bitcast(F32)
+                for u in range(2):
+                    nc.tensor.transpose(turned[:, b, u, :], pairs[:, u * P : (u + 1) * P], ident[:])
+            h_in = ring.tile([P, 4 * C], BF16, name="h_in", bufs=E, align_bytes=64)
+            copy_out(
+                e in TURN_ON_VECTOR,
+                h_in[:].bitcast(F32).rearrange("p (b j u) -> p b j u", b=2, u=2),
+                turned[:].rearrange("p b u j -> p b j u"),
+            )
+            return h_in
+
+        def second(e, h_in, wbw):
+            h_w = ring.tile([P, C], U32, name="h_w", align_bytes=64)
+            h_s = ring.tile([P, C], U8, name="h_s", align_bytes=64)
+            nc.vector.quantize_mx(out=h_w[:].bitcast(FP8X4), scales=h_s[:], in_=h_in[:])
+            y_e = psum.tile([P, BANK], F32, name="y_e", bufs=3)
+            nc.tensor.matmul_mx(
+                out=y_e[:, 0:C],
+                lhsT=wbw[:, e, :].bitcast(FP4X4),
+                lhsT_scale=wbs[:, e * N : (e + 1) * N],
+                rhs=h_w[:].bitcast(FP8X4),
+                rhs_scale=h_s[:],
+                start=True,
+                stop=True,
+            )
+            copy_out(e in Y_ON_VECTOR, y[:, e * C : (e + 1) * C], y_e[:, 0:C])
+
+        H_ON_VECTOR = {(8, 1)}
+        TURN_ON_VECTOR = set()
+        Y_ON_VECTOR = {0, 1, 2, 3, 4, 5}
+
+        waws = {0: load_wa(*CHUNKS[0], nc.scalar)}
+        load_scale_rows(was_early, wa_rows[0 : EARLY * PASSES], [nc.sync, nc.scalar])
+        waws[1] = load_wa(*CHUNKS[1], nc.sync)
+        load_scale_rows(was_late, wa_rows[EARLY * PASSES :], [nc.sync])
+        planes = {0: gather_scales(*CHUNKS[0], nc.scalar)}
+        hidden = []
+        for c, (first, last) in enumerate(CHUNKS):
+            for e in range(first, last):
+                if e == last - 1 and c + 1 < len(CHUNKS):
+                    planes[c + 1] = gather_scales(*CHUNKS[c + 1], nc.scalar if c == 0 else nc.sync)
+                hidden.append(adapter(e, first, waws[c], planes[c], gather_words(e)))
+            if c + 2 < len(CHUNKS):
+                waws[c + 2] = load_wa(*CHUNKS[c + 2], nc.sync)
+        load_scale_rows(wbs, wb_scales.rearrange("e o b n -> (e o) b n"), [nc.sync])
+        wbw = ring.tile([P, E, 2 * N], U8, name="waw", align_bytes=64)
+        nc.sync.dma_start(out=wbw[:].bitcast(I32), in_=wb_words.rearrange("e o p n -> p (e o) n").bitcast(I32))
+        for e in range(E):
+            second(e, hidden[e], wbw)
+
+        ww = ring.tile([P, PASSES, 2 * N], U8, name="waw", align_bytes=64)
+        nc.sync.dma_start(out=ww[:].bitcast(I32), in_=w_words.rearrange("s p n -> p s n").bitcast(I32))
+        load_scale_rows(ws, w_scales, [nc.sync])
+        shift_second_pass(xs1[:], xs[:], nc.sync)
+        base_t = keep.tile([P, BLOCKS, N], F32, name="base_t")
+        for b0 in range(0, BLOCKS, 3):
+            acc = psum.tile([P, BANK], F32, name="turned")
+            for j in range(3):
+                cols = slice((b0 + j) * P, (b0 + j + 1) * P)
+                for s in range(PASSES):
+                    nc.tensor.matmul_mx(
+                        out=acc[:, j * N : (j + 1) * N],
+                        lhsT=xw[:, s, cols].bitcast(FP8X4),
+                        lhsT_scale=(xs, xs1)[s][:, cols],
+                        rhs=ww[:, s, :].bitcast(FP4X4),
+                        rhs_scale=ws[:, s * N : (s + 1) * N],
+                        start=(s == 0),
+                        stop=(s == PASSES - 1),
+                    )
+            nc.scalar.copy(out=base_t[:, b0 : b0 + 3, :], in_=acc[:, 0 : 3 * N].rearrange("p (j n) -> p j n", j=3))
+
+        nc.sync.dma_start(
+            out=gate_rows[0 : TOP * BLOCKS, :], in_=gate[:, 0, :].rearrange("r (b t) -> r b t", t=P)
+        )
+        gate_ps = psum.tile([P, 2, 2, P], F32, name="turned")
+        nc.tensor.transpose(gate_ps[:, 0, 0, :], gate_rows[:], ident[:])
+        gate_t = keep.tile([P, TOP * BLOCKS], F32, name="gate_t")
+        nc.scalar.copy(out=gate_t[:], in_=gate_ps[:, 0, 0, 0 : TOP * BLOCKS])
+
+        lists = []
+        for r, pos in enumerate((pos1, pos2, pos3)):
+            pos_sb = keep.tile([P, T // 16], U16, name="pos%d_sb" % (r + 1))
+            nc.sync.dma_start(pos_sb[:], pos)
+            lists.append(pos_sb)
+
+        per_half = HALF // P
+        for half in range(2):
+            sums = []
+            for r in range(TOP):
+                picked = ring.tile([P, HALF], F32, name="picked", bufs=6)
+                nc.vector.tensor_copy(
+                    picked[:], y[:].indirect(lists[r][:, half * HALF // 16 : (half + 1) * HALF // 16])
+                )
+                picked_t = psum.tile([P, 2, 2, P], F32, name="turned")
+                flat_t = picked_t[:].rearrange("p b u j -> p (b u j)")
+                for j in range(per_half):
+                    nc.tensor.transpose(flat_t[:, j * P : (j + 1) * P], picked[:, j * P : (j + 1) * P], ident[:])
+                for j in range(per_half):
+                    block = half * per_half + j
+                    scaled = ring.tile([P, N], F32, name="scaled", bufs=6)
+                    col = r * BLOCKS + block
+                    nc.scalar.activation(
+                        out=scaled[:], in_=flat_t[:, j * P : (j + 1) * P], func=COPY, scale=gate_t[:, col : col + 1]
+                    )
+                    if r == 0:
+                        if block < 3:
+                            total = psum.tile([P, H], F32, name="h_t", bufs=3)
+                        else:
+                            total = psum.tile([P, BANK], F32, name="y_e", bufs=3)
+                        sums.append(total)
+                    nc.tensor.matmul(
+                        sums[j][:, 0:P], lhsT=scaled[:], rhs=ident[:], is_transpose=True, start=(r == 0), stop=(r == TOP - 1)
+                    )
+                    if r == 1:
+                        nc.tensor.matmul(
+                            sums[j][:, 0:P], lhsT=base_t[:, block, :], rhs=ident[:], is_transpose=True, start=False, stop=False
+                        )
+            result = ring.tile([P, HALF], F32, name="result")
+            for j in range(per_half):
+                copy_out(half == 1 and j != 1, result[:, j * P : (j + 1) * P], sums[j][:, 0:P])
+            nc.sync.dma_start(out=out[:, half * HALF : (half + 1) * HALF], in_=result[:])

@@ -14,6 +14,8 @@ U16 = mybir.dt.uint16
 U8 = mybir.dt.uint8
 FP8X4 = mybir.dt.float8_e4m3fn_x4
 FP4X4 = mybir.dt.float4_e2m1fn_x4
+MULT = mybir.AluOpType.mult
+ADD = mybir.AluOpType.add
 COPY = mybir.ActivationFunctionType.Copy
 
 P = 128
@@ -21,9 +23,11 @@ PASSES = K // 512
 SLOTS = E * C
 BANK = 512
 CHUNKS = [(0, 1), (1, 3), (3, 5), (5, 7), (7, 9)]
+SCALE_CHUNKS = [(0, 1), (1, 2), (2, 4), (4, 6), (6, 8), (8, 9)]
 EARLY = 3
 HALF = T // 2
 BLOCKS = T // P
+TURNED = TOP - 1
 
 
 def tile_moe_adp_none_kernel(
@@ -63,19 +67,17 @@ def tile_moe_adp_none_kernel(
         wa_rows = wa_scales.rearrange("e s b n -> (e s) b n")
         was_early = zeroed_plane(EARLY * PASSES * H, "was_early", nc.vector)
         slot_s1 = zeroed_plane(SLOTS, "slot_s1", nc.vector)
-        was_late = zeroed_plane((E - EARLY) * PASSES * H, "was_late", nc.vector)
         wbs = zeroed_plane(E * N, "wbs", nc.vector)
-        ws = zeroed_plane(PASSES * N, "ws", nc.vector)
-        xs1 = zeroed_plane(T, "xs1", nc.vector)
         ident = keep.tile([P, P], F32, name="ident")
         make_identity(nc, ident[:])
-        gate_rows = keep.tile([P, P], F32, name="gate_rows")
-        nc.gpsimd.memset(gate_rows[:], 0.0)
+        was_late = zeroed_plane((E - EARLY) * PASSES * H, "was_late", nc.gpsimd)
+        ws = zeroed_plane(PASSES * N, "ws", nc.gpsimd)
+        xs1 = zeroed_plane(T, "xs1", nc.gpsimd)
 
         y = keep.tile([P, SLOTS], F32, name="y")
 
         def load_wa(first, last, queue):
-            waw = ring.tile([P, (last - first) * PASSES, 2 * H], U8, name="waw", align_bytes=64)
+            waw = ring.tile([P, (last - first) * PASSES, 2 * H], U8, name="waw", bufs=3, align_bytes=64)
             queue.dma_start(
                 out=waw[:].bitcast(I32), in_=wa_words[first:last].rearrange("e s p n -> p (e s) n").bitcast(I32)
             )
@@ -83,7 +85,7 @@ def tile_moe_adp_none_kernel(
 
         def gather_scales(first, last, queue):
             lo, hi = first * C, last * C
-            slot_s0 = ring.tile([P, hi - lo], U8, name="slot_s0", align_bytes=64)
+            slot_s0 = ring.tile([P, hi - lo], U8, name="slot_s0", bufs=3, align_bytes=64)
             nc.vector.tensor_copy(slot_s0[:], xs[:].indirect(offs_sb[:, lo // 16 : hi // 16]))
             shift_second_pass(slot_s1[:, lo:hi], slot_s0[:], queue)
             return slot_s0
@@ -91,7 +93,7 @@ def tile_moe_adp_none_kernel(
         def gather_words(e):
             words = []
             for s in range(PASSES):
-                slot_w = ring.tile([P, C], I32, name="slot_w", bufs=4, align_bytes=64)
+                slot_w = ring.tile([P, C], I32, name="slot_w", bufs=6, align_bytes=64)
                 nc.vector.tensor_copy(
                     slot_w[:].bitcast(U32),
                     xw[:, s, :].bitcast(U32).indirect(offs_sb[:, e * C // 16 : (e + 1) * C // 16]),
@@ -105,14 +107,15 @@ def tile_moe_adp_none_kernel(
             else:
                 nc.scalar.copy(out=dst, in_=src)
 
-        def adapter(e, first, waw, slot_s0, words):
+        def adapter(e, first, waw, s_first, slot_s0, words):
             was, e0 = (was_early, 0) if e < EARLY else (was_late, EARLY)
             turned = psum.tile([P, 2, 2, P], F32, name="turned")
+            h_bf = ring.tile([P, 2, H], BF16, name="h_bf", bufs=3)
             for b in range(2):
                 h_t = psum.tile([P, H], F32, name="h_t", bufs=3)
                 for s in range(PASSES):
                     col = e * C + b * P
-                    plane = slot_s0[:, col - first * C : col - first * C + P] if s == 0 else slot_s1[:, col : col + P]
+                    plane = slot_s0[:, col - s_first * C : col - s_first * C + P] if s == 0 else slot_s1[:, col : col + P]
                     g = (e - e0) * PASSES + s
                     nc.tensor.matmul_mx(
                         out=h_t[:],
@@ -123,16 +126,16 @@ def tile_moe_adp_none_kernel(
                         start=(s == 0),
                         stop=(s == PASSES - 1),
                     )
-                h_bf = ring.tile([P, H], BF16, name="h_bf", bufs=4)
-                dst = h_bf[:].rearrange("p (u m d) -> p u m d", u=2, d=2)
+                dst = h_bf[:, b, :].rearrange("p (u m d) -> p u m d", u=2, d=2)
                 src = h_t[:].rearrange("p (m u d) -> p u m d", u=2, d=2)
                 if (e, b) in H_ON_VECTOR:
                     nc.vector.tensor_copy(out=dst, in_=src)
                 else:
                     nc.scalar.activation(out=dst, in_=src, func=COPY)
-                pairs = h_bf[:].bitcast(F32)
+            pairs = h_bf[:].bitcast(F32)
+            for b in range(2):
                 for u in range(2):
-                    nc.tensor.transpose(turned[:, b, u, :], pairs[:, u * P : (u + 1) * P], ident[:])
+                    nc.tensor.transpose(turned[:, b, u, :], pairs[:, b, u * P : (u + 1) * P], ident[:])
             h_in = ring.tile([P, 4 * C], BF16, name="h_in", bufs=E, align_bytes=64)
             copy_out(
                 e in TURN_ON_VECTOR,
@@ -142,8 +145,8 @@ def tile_moe_adp_none_kernel(
             return h_in
 
         def second(e, h_in, wbw):
-            h_w = ring.tile([P, C], U32, name="h_w", align_bytes=64)
-            h_s = ring.tile([P, C], U8, name="h_s", align_bytes=64)
+            h_w = ring.tile([P, C], U32, name="h_w", bufs=4, align_bytes=64)
+            h_s = ring.tile([P, C], U8, name="h_s", bufs=4, align_bytes=64)
             nc.vector.quantize_mx(out=h_w[:].bitcast(FP8X4), scales=h_s[:], in_=h_in[:])
             y_e = psum.tile([P, BANK], F32, name="y_e", bufs=3)
             nc.tensor.matmul_mx(
@@ -157,30 +160,38 @@ def tile_moe_adp_none_kernel(
             )
             copy_out(e in Y_ON_VECTOR, y[:, e * C : (e + 1) * C], y_e[:, 0:C])
 
-        H_ON_VECTOR = {(8, 1)}
-        TURN_ON_VECTOR = set()
-        Y_ON_VECTOR = {0, 1, 2, 3, 4, 5}
+        H_ON_VECTOR = {(8, 0)}
+        TURN_ON_VECTOR = {5, 6, 7}
+        Y_ON_VECTOR = set(range(E))
 
         waws = {0: load_wa(*CHUNKS[0], nc.scalar)}
         load_scale_rows(was_early, wa_rows[0 : EARLY * PASSES], [nc.sync, nc.scalar])
         waws[1] = load_wa(*CHUNKS[1], nc.sync)
-        load_scale_rows(was_late, wa_rows[EARLY * PASSES :], [nc.sync])
-        planes = {0: gather_scales(*CHUNKS[0], nc.scalar)}
+        planes = [gather_scales(*SCALE_CHUNKS[c], nc.scalar if c == 0 else nc.sync) for c in range(3)]
+        load_scale_rows(was_late, wa_rows[EARLY * PASSES :], [nc.sync, nc.scalar])
+        waws[2] = load_wa(*CHUNKS[2], nc.sync)
         hidden = []
         for c, (first, last) in enumerate(CHUNKS):
             for e in range(first, last):
-                if e == last - 1 and c + 1 < len(CHUNKS):
-                    planes[c + 1] = gather_scales(*CHUNKS[c + 1], nc.scalar if c == 0 else nc.sync)
-                hidden.append(adapter(e, first, waws[c], planes[c], gather_words(e)))
-            if c + 2 < len(CHUNKS):
-                waws[c + 2] = load_wa(*CHUNKS[c + 2], nc.sync)
-        load_scale_rows(wbs, wb_scales.rearrange("e o b n -> (e o) b n"), [nc.sync])
-        wbw = ring.tile([P, E, 2 * N], U8, name="waw", align_bytes=64)
-        nc.sync.dma_start(out=wbw[:].bitcast(I32), in_=wb_words.rearrange("e o p n -> p (e o) n").bitcast(I32))
-        for e in range(E):
+                if e == 4:
+                    load_scale_rows(wbs, wb_scales.rearrange("e o b n -> (e o) b n"), [nc.scalar, nc.sync])
+                if e == 6:
+                    wbw = ring.tile([P, E, 2 * N], U8, name="waw", bufs=3, align_bytes=64)
+                    nc.sync.dma_start(
+                        out=wbw[:].bitcast(I32), in_=wb_words.rearrange("e o p n -> p (e o) n").bitcast(I32)
+                    )
+                for done in {6: (0, 1, 2), 7: (3, 4, 5), 8: (6,)}.get(e, ()):
+                    second(done, hidden[done], wbw)
+                if e in (3, 4, 6):
+                    planes.append(gather_scales(*SCALE_CHUNKS[len(planes)], nc.sync))
+                sc = [k for k, (a, b) in enumerate(SCALE_CHUNKS) if a <= e < b][0]
+                hidden.append(adapter(e, first, waws[c], SCALE_CHUNKS[sc][0], planes[sc], gather_words(e)))
+            if c + 3 < len(CHUNKS):
+                waws[c + 3] = load_wa(*CHUNKS[c + 3], nc.sync)
+        for e in (7, 8):
             second(e, hidden[e], wbw)
 
-        ww = ring.tile([P, PASSES, 2 * N], U8, name="waw", align_bytes=64)
+        ww = ring.tile([P, PASSES, 2 * N], U8, name="waw", bufs=3, align_bytes=64)
         nc.sync.dma_start(out=ww[:].bitcast(I32), in_=w_words.rearrange("s p n -> p s n").bitcast(I32))
         load_scale_rows(ws, w_scales, [nc.sync])
         shift_second_pass(xs1[:], xs[:], nc.sync)
@@ -201,13 +212,17 @@ def tile_moe_adp_none_kernel(
                     )
             nc.scalar.copy(out=base_t[:, b0 : b0 + 3, :], in_=acc[:, 0 : 3 * N].rearrange("p (j n) -> p j n", j=3))
 
+        gate_rows = keep.tile([P, P], F32, name="gate_rows")
+        nc.gpsimd.memset(gate_rows[:], 0.0)
         nc.sync.dma_start(
-            out=gate_rows[0 : TOP * BLOCKS, :], in_=gate[:, 0, :].rearrange("r (b t) -> r b t", t=P)
+            out=gate_rows[0 : TURNED * BLOCKS, :], in_=gate[0:TURNED, 0, :].rearrange("r (b t) -> r b t", t=P)
         )
         gate_ps = psum.tile([P, 2, 2, P], F32, name="turned")
         nc.tensor.transpose(gate_ps[:, 0, 0, :], gate_rows[:], ident[:])
-        gate_t = keep.tile([P, TOP * BLOCKS], F32, name="gate_t")
-        nc.scalar.copy(out=gate_t[:], in_=gate_ps[:, 0, 0, 0 : TOP * BLOCKS])
+        gate_t = keep.tile([P, TURNED * BLOCKS], F32, name="gate_t")
+        nc.scalar.copy(out=gate_t[:], in_=gate_ps[:, 0, 0, 0 : TURNED * BLOCKS])
+        gate_last = keep.tile([P, T], F32, name="gate_last")
+        nc.sync.dma_start(out=gate_last[:], in_=gate[TOP - 1])
 
         lists = []
         for r, pos in enumerate((pos1, pos2, pos3)):
@@ -216,10 +231,15 @@ def tile_moe_adp_none_kernel(
             lists.append(pos_sb)
 
         per_half = HALF // P
+        sums = []
+        for block in range(BLOCKS):
+            sums.append(psum.tile([P, BANK], F32, name=("h_t", "y_e")[block // per_half], bufs=3))
+            nc.tensor.matmul(
+                sums[block][:, 0:P], lhsT=base_t[:, block, :], rhs=ident[:], is_transpose=True, start=True, stop=False
+            )
         for half in range(2):
-            sums = []
-            for r in range(TOP):
-                picked = ring.tile([P, HALF], F32, name="picked", bufs=6)
+            for r in range(TURNED):
+                picked = ring.tile([P, HALF], F32, name="picked", bufs=4)
                 nc.vector.tensor_copy(
                     picked[:], y[:].indirect(lists[r][:, half * HALF // 16 : (half + 1) * HALF // 16])
                 )
@@ -234,20 +254,18 @@ def tile_moe_adp_none_kernel(
                     nc.scalar.activation(
                         out=scaled[:], in_=flat_t[:, j * P : (j + 1) * P], func=COPY, scale=gate_t[:, col : col + 1]
                     )
-                    if r == 0:
-                        if block < 3:
-                            total = psum.tile([P, H], F32, name="h_t", bufs=3)
-                        else:
-                            total = psum.tile([P, BANK], F32, name="y_e", bufs=3)
-                        sums.append(total)
                     nc.tensor.matmul(
-                        sums[j][:, 0:P], lhsT=scaled[:], rhs=ident[:], is_transpose=True, start=(r == 0), stop=(r == TOP - 1)
+                        sums[block][:, 0:P], lhsT=scaled[:], rhs=ident[:], is_transpose=True, start=False, stop=(r == TURNED - 1)
                     )
-                    if r == 1:
-                        nc.tensor.matmul(
-                            sums[j][:, 0:P], lhsT=base_t[:, block, :], rhs=ident[:], is_transpose=True, start=False, stop=False
-                        )
+        for half in range(2):
+            cols = slice(half * HALF, (half + 1) * HALF)
+            third = ring.tile([P, HALF], F32, name="third")
+            nc.vector.tensor_tensor(
+                third[:], y[:].indirect(lists[TOP - 1][:, half * HALF // 16 : (half + 1) * HALF // 16]), gate_last[:, cols], MULT
+            )
             result = ring.tile([P, HALF], F32, name="result")
             for j in range(per_half):
-                copy_out(half == 1 and j != 1, result[:, j * P : (j + 1) * P], sums[j][:, 0:P])
-            nc.sync.dma_start(out=out[:, half * HALF : (half + 1) * HALF], in_=result[:])
+                nc.vector.tensor_tensor(
+                    result[:, j * P : (j + 1) * P], sums[half * per_half + j][:, 0:P], third[:, j * P : (j + 1) * P], ADD
+                )
+            nc.sync.dma_start(out=out[:, cols], in_=result[:])

@@ -23,7 +23,7 @@ PASSES = K // 512
 SLOTS = E * C
 BANK = 512
 CHUNKS = [(0, 1), (1, 3), (3, 5), (5, 7), (7, 9)]
-SCALE_CHUNKS = [(0, 1), (1, 2), (2, 4), (4, 6), (6, 8), (8, 9)]
+SCALE_CHUNKS = CHUNKS
 EARLY = 3
 HALF = T // 2
 BLOCKS = T // P
@@ -66,11 +66,11 @@ def tile_moe_adp_none_kernel(
         nc.sync.dma_start(out=xw[:], in_=x_words.rearrange("s p t d -> p s (t d)").bitcast(I32))
         wa_rows = wa_scales.rearrange("e s b n -> (e s) b n")
         was_early = zeroed_plane(EARLY * PASSES * H, "was_early", nc.vector)
-        slot_s1 = zeroed_plane(SLOTS, "slot_s1", nc.vector)
-        wbs = zeroed_plane(E * N, "wbs", nc.vector)
+        slot_s1 = zeroed_plane(SLOTS, "slot_s1", nc.gpsimd)
+        was_late = zeroed_plane((E - EARLY) * PASSES * H, "was_late", nc.vector)
+        wbs = zeroed_plane(E * N, "wbs", nc.gpsimd)
         ident = keep.tile([P, P], F32, name="ident")
         make_identity(nc, ident[:])
-        was_late = zeroed_plane((E - EARLY) * PASSES * H, "was_late", nc.gpsimd)
         ws = zeroed_plane(PASSES * N, "ws", nc.gpsimd)
         xs1 = zeroed_plane(T, "xs1", nc.gpsimd)
 
@@ -112,7 +112,7 @@ def tile_moe_adp_none_kernel(
             turned = psum.tile([P, 2, 2, P], F32, name="turned")
             h_bf = ring.tile([P, 2, H], BF16, name="h_bf", bufs=3)
             for b in range(2):
-                h_t = psum.tile([P, H], F32, name="h_t", bufs=3)
+                h_t = psum.tile([P, H], F32, name="h_t", bufs=4)
                 for s in range(PASSES):
                     col = e * C + b * P
                     plane = slot_s0[:, col - s_first * C : col - s_first * C + P] if s == 0 else slot_s1[:, col : col + P]
@@ -145,10 +145,10 @@ def tile_moe_adp_none_kernel(
             return h_in
 
         def second(e, h_in, wbw):
-            h_w = ring.tile([P, C], U32, name="h_w", bufs=4, align_bytes=64)
-            h_s = ring.tile([P, C], U8, name="h_s", bufs=4, align_bytes=64)
+            h_w = ring.tile([P, C], U32, name="h_w", bufs=3, align_bytes=64)
+            h_s = ring.tile([P, C], U8, name="h_s", bufs=3, align_bytes=64)
             nc.vector.quantize_mx(out=h_w[:].bitcast(FP8X4), scales=h_s[:], in_=h_in[:])
-            y_e = psum.tile([P, BANK], F32, name="y_e", bufs=3)
+            y_e = psum.tile([P, BANK], F32, name="y_e")
             nc.tensor.matmul_mx(
                 out=y_e[:, 0:C],
                 lhsT=wbw[:, e, :].bitcast(FP4X4),
@@ -160,41 +160,43 @@ def tile_moe_adp_none_kernel(
             )
             copy_out(e in Y_ON_VECTOR, y[:, e * C : (e + 1) * C], y_e[:, 0:C])
 
-        H_ON_VECTOR = {(8, 0)}
-        TURN_ON_VECTOR = {5, 6, 7}
-        Y_ON_VECTOR = set(range(E))
+        H_ON_VECTOR = set()
+        TURN_ON_VECTOR = {7}
+        Y_ON_VECTOR = {0, 1, 2, 3, 4, 5, 8}
 
-        waws = {0: load_wa(*CHUNKS[0], nc.scalar)}
-        load_scale_rows(was_early, wa_rows[0 : EARLY * PASSES], [nc.sync, nc.scalar])
+        planes = [gather_scales(*SCALE_CHUNKS[0], nc.scalar)]
+        waws = {0: load_wa(*CHUNKS[0], nc.sync)}
+        load_scale_rows(was_early, wa_rows[0 : EARLY * PASSES], [nc.scalar])
         waws[1] = load_wa(*CHUNKS[1], nc.sync)
-        planes = [gather_scales(*SCALE_CHUNKS[c], nc.scalar if c == 0 else nc.sync) for c in range(3)]
+        planes.append(gather_scales(*SCALE_CHUNKS[1], nc.scalar))
+        planes.append(gather_scales(*SCALE_CHUNKS[2], nc.sync))
         load_scale_rows(was_late, wa_rows[EARLY * PASSES :], [nc.sync, nc.scalar])
         waws[2] = load_wa(*CHUNKS[2], nc.sync)
         hidden = []
         for c, (first, last) in enumerate(CHUNKS):
             for e in range(first, last):
-                if e == 4:
-                    load_scale_rows(wbs, wb_scales.rearrange("e o b n -> (e o) b n"), [nc.scalar, nc.sync])
+                if e in (2, 4):
+                    planes.append(gather_scales(*SCALE_CHUNKS[len(planes)], nc.sync))
+                if e == 2:
+                    load_scale_rows(wbs, wb_scales.rearrange("e o b n -> (e o) b n"), [nc.sync])
                 if e == 6:
                     wbw = ring.tile([P, E, 2 * N], U8, name="waw", bufs=3, align_bytes=64)
                     nc.sync.dma_start(
                         out=wbw[:].bitcast(I32), in_=wb_words.rearrange("e o p n -> p (e o) n").bitcast(I32)
                     )
-                for done in {6: (0, 1, 2), 7: (3, 4, 5), 8: (6,)}.get(e, ()):
+                for done in {6: (0, 1), 7: (2, 3), 8: (4, 5)}.get(e, ()):
                     second(done, hidden[done], wbw)
-                if e in (3, 4, 6):
-                    planes.append(gather_scales(*SCALE_CHUNKS[len(planes)], nc.sync))
                 sc = [k for k, (a, b) in enumerate(SCALE_CHUNKS) if a <= e < b][0]
                 hidden.append(adapter(e, first, waws[c], SCALE_CHUNKS[sc][0], planes[sc], gather_words(e)))
             if c + 3 < len(CHUNKS):
                 waws[c + 3] = load_wa(*CHUNKS[c + 3], nc.sync)
-        for e in (7, 8):
+        for e in (6, 7, 8):
             second(e, hidden[e], wbw)
 
         ww = ring.tile([P, PASSES, 2 * N], U8, name="waw", bufs=3, align_bytes=64)
         nc.sync.dma_start(out=ww[:].bitcast(I32), in_=w_words.rearrange("s p n -> p s n").bitcast(I32))
         load_scale_rows(ws, w_scales, [nc.sync])
-        shift_second_pass(xs1[:], xs[:], nc.sync)
+        shift_second_pass(xs1[:], xs[:], nc.scalar)
         base_t = keep.tile([P, BLOCKS, N], F32, name="base_t")
         for b0 in range(0, BLOCKS, 3):
             acc = psum.tile([P, BANK], F32, name="turned")
@@ -233,7 +235,10 @@ def tile_moe_adp_none_kernel(
         per_half = HALF // P
         sums = []
         for block in range(BLOCKS):
-            sums.append(psum.tile([P, BANK], F32, name=("h_t", "y_e")[block // per_half], bufs=3))
+            if block < 4:
+                sums.append(psum.tile([P, BANK], F32, name="h_t", bufs=4))
+            else:
+                sums.append(psum.tile([P, BANK], F32, name="y_e"))
             nc.tensor.matmul(
                 sums[block][:, 0:P], lhsT=base_t[:, block, :], rhs=ident[:], is_transpose=True, start=True, stop=False
             )

@@ -22,12 +22,17 @@ P = 128
 PASSES = K // 512
 SLOTS = E * C
 BANK = 512
-CHUNKS = [(0, 1), (1, 3), (3, 5), (5, 7), (7, 9)]
-SCALE_CHUNKS = CHUNKS
-EARLY = 3
-HALF = T // 2
+PER_COLUMN = 16
 BLOCKS = T // P
+HALF = T // 2
 TURNED = TOP - 1
+
+CHUNKS = [(0, 1)] + [(e, e + 2) for e in range(1, E, 2)]
+AHEAD = 3
+EARLY = CHUNKS[1][1]
+H_BANKS = 4
+H_READY = 4
+WEAVE_FROM = E - 3
 
 
 def tile_moe_adp_none_kernel(
@@ -45,17 +50,26 @@ def tile_moe_adp_none_kernel(
             return plane
 
         def load_scale_rows(plane, rows, queues):
-            groups = rows.shape[0]
+            passes = rows.shape[0]
             for q in range(4):
                 queues[q % len(queues)].dma_start(
-                    out=plane[32 * q : 32 * q + 4, :].rearrange("b (g n) -> b g n", g=groups).bitcast(I32),
+                    out=plane[32 * q : 32 * q + 4, :].rearrange("b (g n) -> b g n", g=passes).bitcast(I32),
                     in_=rows[:, 4 * q : 4 * q + 4, :].rearrange("g b n -> b g n").bitcast(I32),
                 )
 
         def shift_second_pass(dst, src, queue):
             queue.dma_start(out=dst[0:112, :].bitcast(I32), in_=src[4:116, :].bitcast(I32))
 
-        offs_sb = keep.tile([P, SLOTS // 16], U16, name="offs_sb")
+        def entries(offsets, lo, hi):
+            return offsets[:, lo // PER_COLUMN : hi // PER_COLUMN]
+
+        def copy_out(on_vector, dst, src):
+            if on_vector:
+                nc.vector.tensor_copy(out=dst, in_=src)
+            else:
+                nc.scalar.copy(out=dst, in_=src)
+
+        offs_sb = keep.tile([P, SLOTS // PER_COLUMN], U16, name="offs_sb")
         nc.sync.dma_start(offs_sb[:], offs)
         xs = zeroed_plane(T, "xs", nc.gpsimd)
         for q in range(4):
@@ -64,9 +78,10 @@ def tile_moe_adp_none_kernel(
             )
         xw = keep.tile([P, PASSES, T], I32, name="xw", align_bytes=64)
         nc.sync.dma_start(out=xw[:], in_=x_words.rearrange("s p t d -> p s (t d)").bitcast(I32))
+
         wa_rows = wa_scales.rearrange("e s b n -> (e s) b n")
+        slot_s1 = zeroed_plane(SLOTS, "slot_s1", nc.vector)
         was_early = zeroed_plane(EARLY * PASSES * H, "was_early", nc.vector)
-        slot_s1 = zeroed_plane(SLOTS, "slot_s1", nc.gpsimd)
         was_late = zeroed_plane((E - EARLY) * PASSES * H, "was_late", nc.vector)
         wbs = zeroed_plane(E * N, "wbs", nc.gpsimd)
         ident = keep.tile([P, P], F32, name="ident")
@@ -76,51 +91,47 @@ def tile_moe_adp_none_kernel(
 
         y = keep.tile([P, SLOTS], F32, name="y")
 
-        def load_wa(first, last, queue):
-            waw = ring.tile([P, (last - first) * PASSES, 2 * H], U8, name="waw", bufs=3, align_bytes=64)
-            queue.dma_start(
+        def weight_tile(rows, row_bytes):
+            return ring.tile([P, rows, row_bytes], U8, name="waw", bufs=AHEAD, align_bytes=64)
+
+        def load_wa(first, last):
+            waw = weight_tile((last - first) * PASSES, 2 * H)
+            nc.sync.dma_start(
                 out=waw[:].bitcast(I32), in_=wa_words[first:last].rearrange("e s p n -> p (e s) n").bitcast(I32)
             )
             return waw
 
         def gather_scales(first, last, queue):
             lo, hi = first * C, last * C
-            slot_s0 = ring.tile([P, hi - lo], U8, name="slot_s0", bufs=3, align_bytes=64)
-            nc.vector.tensor_copy(slot_s0[:], xs[:].indirect(offs_sb[:, lo // 16 : hi // 16]))
+            slot_s0 = ring.tile([P, hi - lo], U8, name="slot_s0", bufs=AHEAD, align_bytes=64)
+            nc.vector.tensor_copy(slot_s0[:], xs[:].indirect(entries(offs_sb, lo, hi)))
             shift_second_pass(slot_s1[:, lo:hi], slot_s0[:], queue)
             return slot_s0
 
         def gather_words(e):
             words = []
             for s in range(PASSES):
-                slot_w = ring.tile([P, C], I32, name="slot_w", bufs=6, align_bytes=64)
+                slot_w = ring.tile([P, C], I32, name="slot_w", bufs=3 * PASSES, align_bytes=64)
                 nc.vector.tensor_copy(
-                    slot_w[:].bitcast(U32),
-                    xw[:, s, :].bitcast(U32).indirect(offs_sb[:, e * C // 16 : (e + 1) * C // 16]),
+                    slot_w[:].bitcast(U32), xw[:, s, :].bitcast(U32).indirect(entries(offs_sb, e * C, (e + 1) * C))
                 )
                 words.append(slot_w)
             return words
 
-        def copy_out(on_vector, dst, src):
-            if on_vector:
-                nc.vector.tensor_copy(out=dst, in_=src)
-            else:
-                nc.scalar.copy(out=dst, in_=src)
-
-        def adapter(e, first, waw, s_first, slot_s0, words):
-            was, e0 = (was_early, 0) if e < EARLY else (was_late, EARLY)
+        def first_product(e, first, waw, slot_s0, words):
+            was, was_first = (was_early, 0) if e < EARLY else (was_late, EARLY)
             turned = psum.tile([P, 2, 2, P], F32, name="turned")
             h_bf = ring.tile([P, 2, H], BF16, name="h_bf", bufs=3)
             for b in range(2):
-                h_t = psum.tile([P, H], F32, name="h_t", bufs=4)
+                h_t = psum.tile([P, H], F32, name="h_t", bufs=H_BANKS)
+                slot = e * C + b * P
+                planes = (slot_s0[:, slot - first * C : slot - first * C + P], slot_s1[:, slot : slot + P])
                 for s in range(PASSES):
-                    col = e * C + b * P
-                    plane = slot_s0[:, col - s_first * C : col - s_first * C + P] if s == 0 else slot_s1[:, col : col + P]
-                    g = (e - e0) * PASSES + s
+                    g = (e - was_first) * PASSES + s
                     nc.tensor.matmul_mx(
                         out=h_t[:],
                         lhsT=words[s][:, b * P : (b + 1) * P].bitcast(FP8X4),
-                        lhsT_scale=plane,
+                        lhsT_scale=planes[s],
                         rhs=waw[:, (e - first) * PASSES + s, :].bitcast(FP4X4),
                         rhs_scale=was[:, g * H : (g + 1) * H],
                         start=(s == 0),
@@ -128,7 +139,7 @@ def tile_moe_adp_none_kernel(
                     )
                 dst = h_bf[:, b, :].rearrange("p (u m d) -> p u m d", u=2, d=2)
                 src = h_t[:].rearrange("p (m u d) -> p u m d", u=2, d=2)
-                if (e, b) in H_ON_VECTOR:
+                if (e, b) == (E - 1, 0):
                     nc.vector.tensor_copy(out=dst, in_=src)
                 else:
                     nc.scalar.activation(out=dst, in_=src, func=COPY)
@@ -137,16 +148,15 @@ def tile_moe_adp_none_kernel(
                 for u in range(2):
                     nc.tensor.transpose(turned[:, b, u, :], pairs[:, b, u * P : (u + 1) * P], ident[:])
             h_in = ring.tile([P, 4 * C], BF16, name="h_in", bufs=E, align_bytes=64)
-            copy_out(
-                e in TURN_ON_VECTOR,
-                h_in[:].bitcast(F32).rearrange("p (b j u) -> p b j u", b=2, u=2),
-                turned[:].rearrange("p b u j -> p b j u"),
+            nc.scalar.copy(
+                out=h_in[:].bitcast(F32).rearrange("p (b j u) -> p b j u", b=2, u=2),
+                in_=turned[:].rearrange("p b u j -> p b j u"),
             )
             return h_in
 
-        def second(e, h_in, wbw):
-            h_w = ring.tile([P, C], U32, name="h_w", bufs=3, align_bytes=64)
-            h_s = ring.tile([P, C], U8, name="h_s", bufs=3, align_bytes=64)
+        def second_product(e, h_in, wbw):
+            h_w = ring.tile([P, C], U32, name="h_w", bufs=H_READY, align_bytes=64)
+            h_s = ring.tile([P, C], U8, name="h_s", bufs=H_READY, align_bytes=64)
             nc.vector.quantize_mx(out=h_w[:].bitcast(FP8X4), scales=h_s[:], in_=h_in[:])
             y_e = psum.tile([P, BANK], F32, name="y_e")
             nc.tensor.matmul_mx(
@@ -158,50 +168,48 @@ def tile_moe_adp_none_kernel(
                 start=True,
                 stop=True,
             )
-            copy_out(e in Y_ON_VECTOR, y[:, e * C : (e + 1) * C], y_e[:, 0:C])
+            copy_out(e not in (E - 3, E - 2), y[:, e * C : (e + 1) * C], y_e[:, 0:C])
 
-        H_ON_VECTOR = set()
-        TURN_ON_VECTOR = {7}
-        Y_ON_VECTOR = {0, 1, 2, 3, 4, 5, 8}
-
-        planes = [gather_scales(*SCALE_CHUNKS[0], nc.scalar)]
-        waws = {0: load_wa(*CHUNKS[0], nc.sync)}
+        slot_planes = [gather_scales(*CHUNKS[0], nc.scalar)]
+        waws = [load_wa(*CHUNKS[0])]
         load_scale_rows(was_early, wa_rows[0 : EARLY * PASSES], [nc.scalar])
-        waws[1] = load_wa(*CHUNKS[1], nc.sync)
-        planes.append(gather_scales(*SCALE_CHUNKS[1], nc.scalar))
-        planes.append(gather_scales(*SCALE_CHUNKS[2], nc.sync))
+        waws.append(load_wa(*CHUNKS[1]))
+        slot_planes.append(gather_scales(*CHUNKS[1], nc.scalar))
+        slot_planes.append(gather_scales(*CHUNKS[2], nc.sync))
         load_scale_rows(was_late, wa_rows[EARLY * PASSES :], [nc.sync, nc.scalar])
-        waws[2] = load_wa(*CHUNKS[2], nc.sync)
+        waws.append(load_wa(*CHUNKS[2]))
+
         hidden = []
         for c, (first, last) in enumerate(CHUNKS):
             for e in range(first, last):
-                if e in (2, 4):
-                    planes.append(gather_scales(*SCALE_CHUNKS[len(planes)], nc.sync))
-                if e == 2:
+                if e == last - 1 and AHEAD <= c + 2 < len(CHUNKS):
+                    slot_planes.append(gather_scales(*CHUNKS[c + 2], nc.sync))
+                if e == EARLY - 1:
                     load_scale_rows(wbs, wb_scales.rearrange("e o b n -> (e o) b n"), [nc.sync])
-                if e == 6:
-                    wbw = ring.tile([P, E, 2 * N], U8, name="waw", bufs=3, align_bytes=64)
+                if e == WEAVE_FROM:
+                    wbw = weight_tile(E, 2 * N)
                     nc.sync.dma_start(
                         out=wbw[:].bitcast(I32), in_=wb_words.rearrange("e o p n -> p (e o) n").bitcast(I32)
                     )
-                for done in {6: (0, 1), 7: (2, 3), 8: (4, 5)}.get(e, ()):
-                    second(done, hidden[done], wbw)
-                sc = [k for k, (a, b) in enumerate(SCALE_CHUNKS) if a <= e < b][0]
-                hidden.append(adapter(e, first, waws[c], SCALE_CHUNKS[sc][0], planes[sc], gather_words(e)))
-            if c + 3 < len(CHUNKS):
-                waws[c + 3] = load_wa(*CHUNKS[c + 3], nc.sync)
-        for e in (6, 7, 8):
-            second(e, hidden[e], wbw)
+                if e >= WEAVE_FROM:
+                    for done in range(2 * (e - WEAVE_FROM), 2 * (e - WEAVE_FROM + 1)):
+                        second_product(done, hidden[done], wbw)
+                hidden.append(first_product(e, first, waws[c], slot_planes[c], gather_words(e)))
+            if c + AHEAD < len(CHUNKS):
+                waws.append(load_wa(*CHUNKS[c + AHEAD]))
+        for e in range(2 * (E - WEAVE_FROM), E):
+            second_product(e, hidden[e], wbw)
 
-        ww = ring.tile([P, PASSES, 2 * N], U8, name="waw", bufs=3, align_bytes=64)
+        per_half = HALF // P
+        ww = weight_tile(PASSES, 2 * N)
         nc.sync.dma_start(out=ww[:].bitcast(I32), in_=w_words.rearrange("s p n -> p s n").bitcast(I32))
         load_scale_rows(ws, w_scales, [nc.sync])
-        shift_second_pass(xs1[:], xs[:], nc.scalar)
+        shift_second_pass(xs1[:], xs[:], nc.sync)
         base_t = keep.tile([P, BLOCKS, N], F32, name="base_t")
-        for b0 in range(0, BLOCKS, 3):
+        for half in range(2):
             acc = psum.tile([P, BANK], F32, name="turned")
-            for j in range(3):
-                cols = slice((b0 + j) * P, (b0 + j + 1) * P)
+            for j in range(per_half):
+                cols = slice(half * HALF + j * P, half * HALF + (j + 1) * P)
                 for s in range(PASSES):
                     nc.tensor.matmul_mx(
                         out=acc[:, j * N : (j + 1) * N],
@@ -212,7 +220,10 @@ def tile_moe_adp_none_kernel(
                         start=(s == 0),
                         stop=(s == PASSES - 1),
                     )
-            nc.scalar.copy(out=base_t[:, b0 : b0 + 3, :], in_=acc[:, 0 : 3 * N].rearrange("p (j n) -> p j n", j=3))
+            nc.scalar.copy(
+                out=base_t[:, half * per_half : (half + 1) * per_half, :],
+                in_=acc[:, 0 : per_half * N].rearrange("p (j n) -> p j n", j=per_half),
+            )
 
         gate_rows = keep.tile([P, P], F32, name="gate_rows")
         nc.gpsimd.memset(gate_rows[:], 0.0)
@@ -228,49 +239,46 @@ def tile_moe_adp_none_kernel(
 
         lists = []
         for r, pos in enumerate((pos1, pos2, pos3)):
-            pos_sb = keep.tile([P, T // 16], U16, name="pos%d_sb" % (r + 1))
+            pos_sb = keep.tile([P, T // PER_COLUMN], U16, name="pos%d_sb" % (r + 1))
             nc.sync.dma_start(pos_sb[:], pos)
             lists.append(pos_sb)
 
-        per_half = HALF // P
+        def add_turned(total, tile_t, start, stop):
+            nc.tensor.matmul(total[:, 0:P], lhsT=tile_t, rhs=ident[:], is_transpose=True, start=start, stop=stop)
+
         sums = []
         for block in range(BLOCKS):
-            if block < 4:
-                sums.append(psum.tile([P, BANK], F32, name="h_t", bufs=4))
+            if block < H_BANKS:
+                sums.append(psum.tile([P, BANK], F32, name="h_t", bufs=H_BANKS))
             else:
                 sums.append(psum.tile([P, BANK], F32, name="y_e"))
-            nc.tensor.matmul(
-                sums[block][:, 0:P], lhsT=base_t[:, block, :], rhs=ident[:], is_transpose=True, start=True, stop=False
-            )
+            add_turned(sums[block], base_t[:, block, :], True, False)
         for half in range(2):
             for r in range(TURNED):
-                picked = ring.tile([P, HALF], F32, name="picked", bufs=4)
-                nc.vector.tensor_copy(
-                    picked[:], y[:].indirect(lists[r][:, half * HALF // 16 : (half + 1) * HALF // 16])
-                )
+                picked = ring.tile([P, HALF], F32, name="picked", bufs=2 * TURNED)
+                nc.vector.tensor_copy(picked[:], y[:].indirect(entries(lists[r], half * HALF, (half + 1) * HALF)))
                 picked_t = psum.tile([P, 2, 2, P], F32, name="turned")
                 flat_t = picked_t[:].rearrange("p b u j -> p (b u j)")
                 for j in range(per_half):
                     nc.tensor.transpose(flat_t[:, j * P : (j + 1) * P], picked[:, j * P : (j + 1) * P], ident[:])
                 for j in range(per_half):
                     block = half * per_half + j
-                    scaled = ring.tile([P, N], F32, name="scaled", bufs=6)
+                    scaled = ring.tile([P, N], F32, name="scaled", bufs=2 * per_half)
                     col = r * BLOCKS + block
                     nc.scalar.activation(
                         out=scaled[:], in_=flat_t[:, j * P : (j + 1) * P], func=COPY, scale=gate_t[:, col : col + 1]
                     )
-                    nc.tensor.matmul(
-                        sums[block][:, 0:P], lhsT=scaled[:], rhs=ident[:], is_transpose=True, start=False, stop=(r == TURNED - 1)
-                    )
+                    add_turned(sums[block], scaled[:], False, r == TURNED - 1)
         for half in range(2):
             cols = slice(half * HALF, (half + 1) * HALF)
             third = ring.tile([P, HALF], F32, name="third")
             nc.vector.tensor_tensor(
-                third[:], y[:].indirect(lists[TOP - 1][:, half * HALF // 16 : (half + 1) * HALF // 16]), gate_last[:, cols], MULT
+                third[:], y[:].indirect(entries(lists[TOP - 1], cols.start, cols.stop)), gate_last[:, cols], MULT
             )
             result = ring.tile([P, HALF], F32, name="result")
             for j in range(per_half):
+                block_cols = slice(j * P, (j + 1) * P)
                 nc.vector.tensor_tensor(
-                    result[:, j * P : (j + 1) * P], sums[half * per_half + j][:, 0:P], third[:, j * P : (j + 1) * P], ADD
+                    result[:, block_cols], sums[half * per_half + j][:, 0:P], third[:, block_cols], ADD
                 )
             nc.sync.dma_start(out=out[:, cols], in_=result[:])

@@ -80,8 +80,8 @@ def tile_moe_adp_none_kernel(
         nc.sync.dma_start(out=xw[:], in_=x_words.rearrange("s p t d -> p s (t d)").bitcast(I32))
 
         wa_rows = wa_scales.rearrange("e s b n -> (e s) b n")
-        slot_s1 = zeroed_plane(SLOTS, "slot_s1", nc.vector)
         was_early = zeroed_plane(EARLY * PASSES * H, "was_early", nc.vector)
+        slot_s1 = zeroed_plane(SLOTS, "slot_s1", nc.gpsimd)
         was_late = zeroed_plane((E - EARLY) * PASSES * H, "was_late", nc.vector)
         wbs = zeroed_plane(E * N, "wbs", nc.gpsimd)
         ident = keep.tile([P, P], F32, name="ident")
@@ -118,11 +118,12 @@ def tile_moe_adp_none_kernel(
                 words.append(slot_w)
             return words
 
-        def first_product(e, first, waw, slot_s0, words):
+        def first_product(e, blocks, first, waw, slot_s0, words):
             was, was_first = (was_early, 0) if e < EARLY else (was_late, EARLY)
-            turned = psum.tile([P, 2, 2, P], F32, name="turned")
-            h_bf = ring.tile([P, 2, H], BF16, name="h_bf", bufs=3)
-            for b in range(2):
+            count = len(blocks)
+            turned = psum.tile([P, count, 2, P], F32, name="turned")
+            h_bf = ring.tile([P, count, H], BF16, name="h_bf", bufs=3)
+            for place, b in enumerate(blocks):
                 h_t = psum.tile([P, H], F32, name="h_t", bufs=H_BANKS)
                 slot = e * C + b * P
                 planes = (slot_s0[:, slot - first * C : slot - first * C + P], slot_s1[:, slot : slot + P])
@@ -137,30 +138,31 @@ def tile_moe_adp_none_kernel(
                         start=(s == 0),
                         stop=(s == PASSES - 1),
                     )
-                dst = h_bf[:, b, :].rearrange("p (u m d) -> p u m d", u=2, d=2)
+                dst = h_bf[:, place, :].rearrange("p (u m d) -> p u m d", u=2, d=2)
                 src = h_t[:].rearrange("p (m u d) -> p u m d", u=2, d=2)
                 if (e, b) == (E - 1, 0):
                     nc.vector.tensor_copy(out=dst, in_=src)
                 else:
                     nc.scalar.activation(out=dst, in_=src, func=COPY)
             pairs = h_bf[:].bitcast(F32)
-            for b in range(2):
+            for place in range(count):
                 for u in range(2):
-                    nc.tensor.transpose(turned[:, b, u, :], pairs[:, b, u * P : (u + 1) * P], ident[:])
-            h_in = ring.tile([P, 4 * C], BF16, name="h_in", bufs=E, align_bytes=64)
+                    nc.tensor.transpose(turned[:, place, u, :], pairs[:, place, u * P : (u + 1) * P], ident[:])
+            h_in = ring.tile([P, 4 * count * P], BF16, name="h_in", bufs=E + 1, align_bytes=64)
             nc.scalar.copy(
-                out=h_in[:].bitcast(F32).rearrange("p (b j u) -> p b j u", b=2, u=2),
+                out=h_in[:].bitcast(F32).rearrange("p (b j u) -> p b j u", b=count, u=2),
                 in_=turned[:].rearrange("p b u j -> p b j u"),
             )
             return h_in
 
-        def second_product(e, h_in, wbw):
-            h_w = ring.tile([P, C], U32, name="h_w", bufs=H_READY, align_bytes=64)
-            h_s = ring.tile([P, C], U8, name="h_s", bufs=H_READY, align_bytes=64)
+        def second_product(e, blocks, h_in, wbw):
+            slot, width = e * C + blocks[0] * P, len(blocks) * P
+            h_w = ring.tile([P, width], U32, name="h_w", bufs=H_READY, align_bytes=64)
+            h_s = ring.tile([P, width], U8, name="h_s", bufs=H_READY, align_bytes=64)
             nc.vector.quantize_mx(out=h_w[:].bitcast(FP8X4), scales=h_s[:], in_=h_in[:])
             y_e = psum.tile([P, BANK], F32, name="y_e")
             nc.tensor.matmul_mx(
-                out=y_e[:, 0:C],
+                out=y_e[:, 0:width],
                 lhsT=wbw[:, e, :].bitcast(FP4X4),
                 lhsT_scale=wbs[:, e * N : (e + 1) * N],
                 rhs=h_w[:].bitcast(FP8X4),
@@ -168,7 +170,7 @@ def tile_moe_adp_none_kernel(
                 start=True,
                 stop=True,
             )
-            copy_out(e not in (E - 3, E - 2), y[:, e * C : (e + 1) * C], y_e[:, 0:C])
+            copy_out(e not in (E - 3, E - 2), y[:, slot : slot + width], y_e[:, 0:width])
 
         slot_planes = [gather_scales(*CHUNKS[0], nc.scalar)]
         waws = [load_wa(*CHUNKS[0])]
@@ -193,12 +195,14 @@ def tile_moe_adp_none_kernel(
                     )
                 if e >= WEAVE_FROM:
                     for done in range(2 * (e - WEAVE_FROM), 2 * (e - WEAVE_FROM + 1)):
-                        second_product(done, hidden[done], wbw)
-                hidden.append(first_product(e, first, waws[c], slot_planes[c], gather_words(e)))
+                        second_product(*hidden[done], wbw)
+                words = gather_words(e)
+                for blocks in [(0, 1)] if e < E - 1 else [(0,), (1,)]:
+                    hidden.append((e, blocks, first_product(e, blocks, first, waws[c], slot_planes[c], words)))
             if c + AHEAD < len(CHUNKS):
                 waws.append(load_wa(*CHUNKS[c + AHEAD]))
-        for e in range(2 * (E - WEAVE_FROM), E):
-            second_product(e, hidden[e], wbw)
+        for left in hidden[2 * (E - WEAVE_FROM) :]:
+            second_product(*left, wbw)
 
         per_half = HALF // P
         ww = weight_tile(PASSES, 2 * N)

@@ -28,11 +28,8 @@ HALF = T // 2
 TURNED = TOP - 1
 
 CHUNKS = [(0, 1)] + [(e, e + 2) for e in range(1, E, 2)]
-AHEAD = 3
 EARLY = CHUNKS[1][1]
-H_BANKS = 4
-H_READY = 4
-WEAVE_FROM = E - 3
+H_BANKS = 3
 
 
 def tile_moe_adp_none_kernel(
@@ -44,10 +41,8 @@ def tile_moe_adp_none_kernel(
         ring = ctx.enter_context(tc.tile_pool(name="ring", bufs=2))
         psum = ctx.enter_context(tc.psum_pool(name="psum", bufs=2))
 
-        def zeroed_plane(cols, name, engine):
-            plane = keep.tile([P, cols], U8, name=name, align_bytes=64)
-            engine.memset(plane[:].bitcast(I32), 0)
-            return plane
+        def plane_tile(cols, name):
+            return keep.tile([P, cols], U8, name=name, align_bytes=64)
 
         def load_scale_rows(plane, rows, queues):
             passes = rows.shape[0]
@@ -71,153 +66,183 @@ def tile_moe_adp_none_kernel(
 
         offs_sb = keep.tile([P, SLOTS // PER_COLUMN], U16, name="offs_sb")
         nc.sync.dma_start(offs_sb[:], offs)
-        xs = zeroed_plane(T, "xs", nc.gpsimd)
+        xs = plane_tile(T, "xs")
+        nc.gpsimd.memset(xs[:].bitcast(I32), 0)
         for q in range(4):
             (nc.sync, nc.scalar)[q // 2].dma_start(
                 out=xs[32 * q : 32 * q + 8, :].bitcast(I32), in_=x_scales[:, 4 * q : 4 * q + 4, :].bitcast(I32)
             )
-        xw = keep.tile([P, PASSES, T], I32, name="xw", align_bytes=64)
-        nc.sync.dma_start(out=xw[:], in_=x_words.rearrange("s p t d -> p s (t d)").bitcast(I32))
+        xw_all = keep.tile([P, PASSES, T], I32, name="xw", align_bytes=64)
+        nc.sync.dma_start(out=xw_all[:], in_=x_words.rearrange("s p t d -> p s (t d)").bitcast(I32))
+        xw = [xw_all[:, s, :] for s in range(PASSES)]
 
         wa_rows = wa_scales.rearrange("e s b n -> (e s) b n")
-        was_early = zeroed_plane(EARLY * PASSES * H, "was_early", nc.vector)
-        slot_s1 = zeroed_plane(SLOTS, "slot_s1", nc.gpsimd)
-        was_late = zeroed_plane((E - EARLY) * PASSES * H, "was_late", nc.vector)
-        wbs = zeroed_plane(E * N, "wbs", nc.gpsimd)
-        ident = keep.tile([P, P], F32, name="ident")
-        make_identity(nc, ident[:])
-        ws = zeroed_plane(PASSES * N, "ws", nc.gpsimd)
-        xs1 = zeroed_plane(T, "xs1", nc.gpsimd)
+        was_early = plane_tile(EARLY * PASSES * H, "was_early")
+        slot_s1 = plane_tile(SLOTS, "slot_s1")
+        was_late = plane_tile((E - EARLY) * PASSES * H, "was_late")
+        wbs = plane_tile(E * N, "wbs")
+        ws = plane_tile(PASSES * N, "ws")
+        xs1 = plane_tile(T, "xs1")
 
         y = keep.tile([P, SLOTS], F32, name="y")
 
-        def weight_tile(rows, row_bytes):
-            return ring.tile([P, rows, row_bytes], U8, name="waw", bufs=AHEAD, align_bytes=64)
+        waw, slot_s0, words = {}, {}, {}
 
-        def load_wa(first, last):
-            waw = weight_tile((last - first) * PASSES, 2 * H)
-            nc.sync.dma_start(
-                out=waw[:].bitcast(I32), in_=wa_words[first:last].rearrange("e s p n -> p (e s) n").bitcast(I32)
+        def load_wa(c, queue):
+            first, last = CHUNKS[c]
+            tile = keep.tile([P, (last - first) * PASSES, 2 * H], U8, name="waw%d" % c, align_bytes=64)
+            queue.dma_start(
+                out=tile[:].bitcast(I32), in_=wa_words[first:last].rearrange("e s p n -> p (e s) n").bitcast(I32)
             )
-            return waw
+            for e in range(first, last):
+                waw[e] = tile[:, (e - first) * PASSES : (e - first + 1) * PASSES, :]
 
-        def gather_scales(first, last, queue):
-            lo, hi = first * C, last * C
-            slot_s0 = ring.tile([P, hi - lo], U8, name="slot_s0", bufs=AHEAD, align_bytes=64)
-            nc.vector.tensor_copy(slot_s0[:], xs[:].indirect(entries(offs_sb, lo, hi)))
-            shift_second_pass(slot_s1[:, lo:hi], slot_s0[:], queue)
-            return slot_s0
+        def gather_scales(c):
+            first, last = CHUNKS[c]
+            tile = ring.tile([P, (last - first) * C], U8, name="slot_s0", bufs=2, align_bytes=64)
+            nc.vector.tensor_copy(tile[:], xs[:].indirect(entries(offs_sb, first * C, last * C)))
+            for e in range(first, last):
+                slot_s0[e] = tile[:, (e - first) * C : (e - first + 1) * C]
+            return tile
+
+        def shift_scales(c, tile, queue):
+            first, last = CHUNKS[c]
+            shift_second_pass(slot_s1[:, first * C : last * C], tile[:], queue)
 
         def gather_words(e):
-            words = []
             for s in range(PASSES):
-                slot_w = ring.tile([P, C], I32, name="slot_w", bufs=3 * PASSES, align_bytes=64)
+                tile = ring.tile([P, C], I32, name="slot_w", bufs=3 * PASSES, align_bytes=64)
                 nc.vector.tensor_copy(
-                    slot_w[:].bitcast(U32), xw[:, s, :].bitcast(U32).indirect(entries(offs_sb, e * C, (e + 1) * C))
+                    tile[:].bitcast(U32), xw[s].bitcast(U32).indirect(entries(offs_sb, e * C, (e + 1) * C))
                 )
-                words.append(slot_w)
-            return words
+                words[e, s] = tile
 
-        def first_product(e, blocks, first, waw, slot_s0, words):
+        lists = []
+
+        def load_list(pos):
+            pos_sb = keep.tile([P, T // PER_COLUMN], U16, name="pos%d_sb" % (len(lists) + 1))
+            nc.sync.dma_start(pos_sb[:], pos)
+            lists.append(pos_sb)
+
+        load_scale_rows(was_early, wa_rows[0 : EARLY * PASSES], [nc.scalar, nc.sync, nc.sync, nc.sync])
+        load_wa(0, nc.scalar)
+        load_scale_rows(was_late, wa_rows[EARLY * PASSES :], [nc.scalar])
+        ident = keep.tile([P, P], F32, name="ident")
+        make_identity(nc, ident[:])
+        gate_rows = keep.tile([P, P], F32, name="gate_rows")
+        nc.gpsimd.memset(gate_rows[:], 0.0)
+        shift_scales(0, gather_scales(0), nc.sync)
+        load_wa(1, nc.sync)
+        shift_scales(1, gather_scales(1), nc.sync)
+        gather_words(0)
+        gather_words(1)
+        load_wa(2, nc.sync)
+        gather_words(2)
+        load_wa(3, nc.sync)
+
+        def product_bank():
+            return psum.tile([P, BANK], F32, name="product", bufs=H_BANKS)
+
+        def first_product(e):
             was, was_first = (was_early, 0) if e < EARLY else (was_late, EARLY)
-            count = len(blocks)
-            turned = psum.tile([P, count, 2, P], F32, name="turned")
-            h_bf = ring.tile([P, count, H], BF16, name="h_bf", bufs=3)
-            for place, b in enumerate(blocks):
-                h_t = psum.tile([P, H], F32, name="h_t", bufs=H_BANKS)
-                slot = e * C + b * P
-                planes = (slot_s0[:, slot - first * C : slot - first * C + P], slot_s1[:, slot : slot + P])
-                for s in range(PASSES):
+            h_bf = keep.tile([P, 2, H], BF16, name="h_bf%d" % e)
+            banks = [product_bank() for b in range(2)]
+            for s in range(PASSES):
+                for b in range(2):
+                    slot = e * C + b * P
+                    planes = (slot_s0[e][:, b * P : (b + 1) * P], slot_s1[:, slot : slot + P])
                     g = (e - was_first) * PASSES + s
                     nc.tensor.matmul_mx(
-                        out=h_t[:],
-                        lhsT=words[s][:, b * P : (b + 1) * P].bitcast(FP8X4),
+                        out=banks[b][:],
+                        lhsT=words[e, s][:, b * P : (b + 1) * P].bitcast(FP8X4),
                         lhsT_scale=planes[s],
-                        rhs=waw[:, (e - first) * PASSES + s, :].bitcast(FP4X4),
+                        rhs=waw[e][:, s, :].bitcast(FP4X4),
                         rhs_scale=was[:, g * H : (g + 1) * H],
                         start=(s == 0),
                         stop=(s == PASSES - 1),
                     )
-                dst = h_bf[:, place, :].rearrange("p (u m d) -> p u m d", u=2, d=2)
+            for b in range(2):
+                h_t = banks[b]
+                dst = h_bf[:, b, :].rearrange("p (u m d) -> p u m d", u=2, d=2)
                 src = h_t[:].rearrange("p (m u d) -> p u m d", u=2, d=2)
-                if (e, b) == (E - 1, 0):
+                if (e, b) == (E - 1, 1):
                     nc.vector.tensor_copy(out=dst, in_=src)
                 else:
                     nc.scalar.activation(out=dst, in_=src, func=COPY)
+            return h_bf
+
+        def turn(e, h_bf):
+            turned = psum.tile([P, 2, 2, P], F32, name="turned")
             pairs = h_bf[:].bitcast(F32)
-            for place in range(count):
+            for b in range(2):
                 for u in range(2):
-                    nc.tensor.transpose(turned[:, place, u, :], pairs[:, place, u * P : (u + 1) * P], ident[:])
-            h_in = ring.tile([P, 4 * count * P], BF16, name="h_in", bufs=E + 1, align_bytes=64)
+                    nc.tensor.transpose(turned[:, b, u, :], pairs[:, b, u * P : (u + 1) * P], ident[:])
+            h_in = keep.tile([P, 4 * C], BF16, name="h_in%d" % e, align_bytes=64)
             nc.scalar.copy(
-                out=h_in[:].bitcast(F32).rearrange("p (b j u) -> p b j u", b=count, u=2),
+                out=h_in[:].bitcast(F32).rearrange("p (b j u) -> p b j u", b=2, u=2),
                 in_=turned[:].rearrange("p b u j -> p b j u"),
             )
             return h_in
 
-        def second_product(e, blocks, h_in, wbw):
-            slot, width = e * C + blocks[0] * P, len(blocks) * P
-            h_w = ring.tile([P, width], U32, name="h_w", bufs=H_READY, align_bytes=64)
-            h_s = ring.tile([P, width], U8, name="h_s", bufs=H_READY, align_bytes=64)
-            nc.vector.quantize_mx(out=h_w[:].bitcast(FP8X4), scales=h_s[:], in_=h_in[:])
-            y_e = psum.tile([P, BANK], F32, name="y_e")
-            nc.tensor.matmul_mx(
-                out=y_e[:, 0:width],
-                lhsT=wbw[:, e, :].bitcast(FP4X4),
-                lhsT_scale=wbs[:, e * N : (e + 1) * N],
-                rhs=h_w[:].bitcast(FP8X4),
-                rhs_scale=h_s[:],
-                start=True,
-                stop=True,
-            )
-            copy_out(e not in (E - 3, E - 2), y[:, slot : slot + width], y_e[:, 0:width])
+        rounded, hidden = [], []
+        for e in range(E):
+            rounded.append(first_product(e))
+            if e in (0, 2, 4):
+                shift_scales(2 + e // 2, gather_scales(2 + e // 2), nc.sync)
+            if e == 0:
+                load_wa(4, nc.sync)
+                wbw = keep.tile([P, E, 2 * N], U8, name="wbw", align_bytes=64)
+                nc.sync.dma_start(out=wbw[:].bitcast(I32), in_=wb_words.rearrange("e o p n -> p (e o) n").bitcast(I32))
+                load_scale_rows(wbs, wb_scales.rearrange("e o b n -> (e o) b n"), [nc.sync])
+            if e == 2:
+                load_scale_rows(ws, w_scales, [nc.sync])
+                ww = keep.tile([P, PASSES, 2 * N], U8, name="ww", align_bytes=64)
+                nc.sync.dma_start(out=ww[:].bitcast(I32), in_=w_words.rearrange("s p n -> p s n").bitcast(I32))
+                shift_second_pass(xs1[:], xs[:], nc.sync)
+                nc.sync.dma_start(
+                    out=gate_rows[0 : TURNED * BLOCKS, :], in_=gate[0:TURNED, 0, :].rearrange("r (b t) -> r b t", t=P)
+                )
+                gate_last = keep.tile([P, T], F32, name="gate_last")
+                nc.sync.dma_start(out=gate_last[:], in_=gate[TOP - 1])
+                for pos in (pos1, pos2, pos3):
+                    load_list(pos)
+            if e + 3 < E:
+                gather_words(e + 3)
+            if e > 0:
+                hidden.append(turn(e - 1, rounded[e - 1]))
+        hidden.append(turn(E - 1, rounded[E - 1]))
 
-        slot_planes = [gather_scales(*CHUNKS[0], nc.scalar)]
-        waws = [load_wa(*CHUNKS[0])]
-        load_scale_rows(was_early, wa_rows[0 : EARLY * PASSES], [nc.scalar])
-        waws.append(load_wa(*CHUNKS[1]))
-        slot_planes.append(gather_scales(*CHUNKS[1], nc.scalar))
-        slot_planes.append(gather_scales(*CHUNKS[2], nc.sync))
-        load_scale_rows(was_late, wa_rows[EARLY * PASSES :], [nc.sync, nc.scalar])
-        waws.append(load_wa(*CHUNKS[2]))
-
-        hidden = []
-        for c, (first, last) in enumerate(CHUNKS):
+        h_w = keep.tile([P, SLOTS], U32, name="waw3", align_bytes=64)
+        h_s = keep.tile([P, SLOTS], U8, name="h_s", align_bytes=64)
+        for e in range(E):
+            cols = slice(e * C, (e + 1) * C)
+            nc.vector.quantize_mx(out=h_w[:, cols].bitcast(FP8X4), scales=h_s[:, cols], in_=hidden[e][:])
+        for pair, first in enumerate(range(0, E, 2)):
+            last = min(first + 2, E)
+            y_bank = product_bank()
             for e in range(first, last):
-                if e == last - 1 and AHEAD <= c + 2 < len(CHUNKS):
-                    slot_planes.append(gather_scales(*CHUNKS[c + 2], nc.sync))
-                if e == EARLY - 1:
-                    load_scale_rows(wbs, wb_scales.rearrange("e o b n -> (e o) b n"), [nc.sync])
-                if e == WEAVE_FROM:
-                    wbw = weight_tile(E, 2 * N)
-                    nc.sync.dma_start(
-                        out=wbw[:].bitcast(I32), in_=wb_words.rearrange("e o p n -> p (e o) n").bitcast(I32)
-                    )
-                if e >= WEAVE_FROM:
-                    for done in range(2 * (e - WEAVE_FROM), 2 * (e - WEAVE_FROM + 1)):
-                        second_product(*hidden[done], wbw)
-                words = gather_words(e)
-                for blocks in [(0, 1)] if e < E - 1 else [(0,), (1,)]:
-                    hidden.append((e, blocks, first_product(e, blocks, first, waws[c], slot_planes[c], words)))
-            if c + AHEAD < len(CHUNKS):
-                waws.append(load_wa(*CHUNKS[c + AHEAD]))
-        for left in hidden[2 * (E - WEAVE_FROM) :]:
-            second_product(*left, wbw)
+                cols = slice(e * C, (e + 1) * C)
+                nc.tensor.matmul_mx(
+                    out=y_bank[:, (e - first) * C : (e - first + 1) * C],
+                    lhsT=wbw[:, e, :].bitcast(FP4X4),
+                    lhsT_scale=wbs[:, e * N : (e + 1) * N],
+                    rhs=h_w[:, cols].bitcast(FP8X4),
+                    rhs_scale=h_s[:, cols],
+                    start=True,
+                    stop=True,
+                )
+            copy_out(pair != 3, y[:, first * C : last * C], y_bank[:, 0 : (last - first) * C])
 
         per_half = HALF // P
-        ww = weight_tile(PASSES, 2 * N)
-        nc.sync.dma_start(out=ww[:].bitcast(I32), in_=w_words.rearrange("s p n -> p s n").bitcast(I32))
-        load_scale_rows(ws, w_scales, [nc.sync])
-        shift_second_pass(xs1[:], xs[:], nc.sync)
         base_t = keep.tile([P, BLOCKS, N], F32, name="base_t")
         for half in range(2):
-            acc = psum.tile([P, BANK], F32, name="turned")
+            acc = product_bank()
             for j in range(per_half):
                 cols = slice(half * HALF + j * P, half * HALF + (j + 1) * P)
                 for s in range(PASSES):
                     nc.tensor.matmul_mx(
                         out=acc[:, j * N : (j + 1) * N],
-                        lhsT=xw[:, s, cols].bitcast(FP8X4),
+                        lhsT=xw[s][:, cols].bitcast(FP8X4),
                         lhsT_scale=(xs, xs1)[s][:, cols],
                         rhs=ww[:, s, :].bitcast(FP4X4),
                         rhs_scale=ws[:, s * N : (s + 1) * N],
@@ -229,33 +254,20 @@ def tile_moe_adp_none_kernel(
                 in_=acc[:, 0 : per_half * N].rearrange("p (j n) -> p j n", j=per_half),
             )
 
-        gate_rows = keep.tile([P, P], F32, name="gate_rows")
-        nc.gpsimd.memset(gate_rows[:], 0.0)
-        nc.sync.dma_start(
-            out=gate_rows[0 : TURNED * BLOCKS, :], in_=gate[0:TURNED, 0, :].rearrange("r (b t) -> r b t", t=P)
-        )
-        gate_ps = psum.tile([P, 2, 2, P], F32, name="turned")
+        gate_ps = psum.tile([P, 2, 2, P], F32, name="total", bufs=3)
         nc.tensor.transpose(gate_ps[:, 0, 0, :], gate_rows[:], ident[:])
         gate_t = keep.tile([P, TURNED * BLOCKS], F32, name="gate_t")
         nc.scalar.copy(out=gate_t[:], in_=gate_ps[:, 0, 0, 0 : TURNED * BLOCKS])
-        gate_last = keep.tile([P, T], F32, name="gate_last")
-        nc.sync.dma_start(out=gate_last[:], in_=gate[TOP - 1])
-
-        lists = []
-        for r, pos in enumerate((pos1, pos2, pos3)):
-            pos_sb = keep.tile([P, T // PER_COLUMN], U16, name="pos%d_sb" % (r + 1))
-            nc.sync.dma_start(pos_sb[:], pos)
-            lists.append(pos_sb)
 
         def add_turned(total, tile_t, start, stop):
             nc.tensor.matmul(total[:, 0:P], lhsT=tile_t, rhs=ident[:], is_transpose=True, start=start, stop=stop)
 
         sums = []
         for block in range(BLOCKS):
-            if block < H_BANKS:
-                sums.append(psum.tile([P, BANK], F32, name="h_t", bufs=H_BANKS))
+            if block < 3:
+                sums.append(psum.tile([P, BANK], F32, name="total", bufs=3))
             else:
-                sums.append(psum.tile([P, BANK], F32, name="y_e"))
+                sums.append(product_bank())
             add_turned(sums[block], base_t[:, block, :], True, False)
         for half in range(2):
             for r in range(TURNED):

@@ -28,8 +28,8 @@ HALF = T // 2
 TURNED = TOP - 1
 
 CHUNKS = [(0, 1)] + [(e, e + 2) for e in range(1, E, 2)]
-EARLY = CHUNKS[1][1]
-H_BANKS = 3
+GROUP = 3
+H_BANKS = 4
 
 
 def tile_moe_adp_none_kernel(
@@ -77,9 +77,8 @@ def tile_moe_adp_none_kernel(
         xw = [xw_all[:, s, :] for s in range(PASSES)]
 
         wa_rows = wa_scales.rearrange("e s b n -> (e s) b n")
-        was_early = plane_tile(EARLY * PASSES * H, "was_early")
+        was = [plane_tile(GROUP * PASSES * H, "was%d" % g) for g in range(E // GROUP)]
         slot_s1 = plane_tile(SLOTS, "slot_s1")
-        was_late = plane_tile((E - EARLY) * PASSES * H, "was_late")
         wbs = plane_tile(E * N, "wbs")
         ws = plane_tile(PASSES * N, "ws")
         xs1 = plane_tile(T, "xs1")
@@ -90,7 +89,7 @@ def tile_moe_adp_none_kernel(
 
         def load_wa(c, queue):
             first, last = CHUNKS[c]
-            tile = keep.tile([P, (last - first) * PASSES, 2 * H], U8, name="waw%d" % c, align_bytes=64)
+            tile = keep.tile([P, (last - first) * PASSES, 2 * H], U8, name="waw%d" % (c if c != 2 else 0), align_bytes=64)
             queue.dma_start(
                 out=tile[:].bitcast(I32), in_=wa_words[first:last].rearrange("e s p n -> p (e s) n").bitcast(I32)
             )
@@ -124,40 +123,40 @@ def tile_moe_adp_none_kernel(
             nc.sync.dma_start(pos_sb[:], pos)
             lists.append(pos_sb)
 
-        load_scale_rows(was_early, wa_rows[0 : EARLY * PASSES], [nc.scalar, nc.sync, nc.sync, nc.sync])
-        load_wa(0, nc.scalar)
-        load_scale_rows(was_late, wa_rows[EARLY * PASSES :], [nc.scalar])
+        def load_was(g, queues):
+            load_scale_rows(was[g], wa_rows[g * GROUP * PASSES : (g + 1) * GROUP * PASSES], queues)
+
+        load_wa(0, nc.sync)
+        load_was(0, [nc.sync])
+        load_wa(1, nc.sync)
         ident = keep.tile([P, P], F32, name="ident")
         make_identity(nc, ident[:])
         gate_rows = keep.tile([P, P], F32, name="gate_rows")
         nc.gpsimd.memset(gate_rows[:], 0.0)
-        shift_scales(0, gather_scales(0), nc.sync)
-        load_wa(1, nc.sync)
-        shift_scales(1, gather_scales(1), nc.sync)
+        shift_scales(0, gather_scales(0), nc.scalar)
+        shift_scales(1, gather_scales(1), nc.scalar)
+        load_was(1, [nc.sync])
         gather_words(0)
         gather_words(1)
-        load_wa(2, nc.sync)
         gather_words(2)
-        load_wa(3, nc.sync)
 
         def product_bank():
             return psum.tile([P, BANK], F32, name="product", bufs=H_BANKS)
 
         def first_product(e):
-            was, was_first = (was_early, 0) if e < EARLY else (was_late, EARLY)
             h_bf = keep.tile([P, 2, H], BF16, name="h_bf%d" % e)
             banks = [product_bank() for b in range(2)]
             for s in range(PASSES):
                 for b in range(2):
                     slot = e * C + b * P
                     planes = (slot_s0[e][:, b * P : (b + 1) * P], slot_s1[:, slot : slot + P])
-                    g = (e - was_first) * PASSES + s
+                    g = e % GROUP * PASSES + s
                     nc.tensor.matmul_mx(
                         out=banks[b][:],
                         lhsT=words[e, s][:, b * P : (b + 1) * P].bitcast(FP8X4),
                         lhsT_scale=planes[s],
                         rhs=waw[e][:, s, :].bitcast(FP4X4),
-                        rhs_scale=was[:, g * H : (g + 1) * H],
+                        rhs_scale=was[e // GROUP][:, g * H : (g + 1) * H],
                         start=(s == 0),
                         stop=(s == PASSES - 1),
                     )
@@ -165,10 +164,7 @@ def tile_moe_adp_none_kernel(
                 h_t = banks[b]
                 dst = h_bf[:, b, :].rearrange("p (u m d) -> p u m d", u=2, d=2)
                 src = h_t[:].rearrange("p (m u d) -> p u m d", u=2, d=2)
-                if (e, b) == (E - 1, 1):
-                    nc.vector.tensor_copy(out=dst, in_=src)
-                else:
-                    nc.scalar.activation(out=dst, in_=src, func=COPY)
+                nc.scalar.activation(out=dst, in_=src, func=COPY)
             return h_bf
 
         def turn(e, h_bf):
@@ -190,11 +186,16 @@ def tile_moe_adp_none_kernel(
             if e in (0, 2, 4):
                 shift_scales(2 + e // 2, gather_scales(2 + e // 2), nc.sync)
             if e == 0:
+                load_wa(2, nc.scalar)
+                load_wa(3, nc.sync)
+            if e == 2:
+                load_was(2, [nc.sync])
                 load_wa(4, nc.sync)
+            if e == 4:
                 wbw = keep.tile([P, E, 2 * N], U8, name="wbw", align_bytes=64)
                 nc.sync.dma_start(out=wbw[:].bitcast(I32), in_=wb_words.rearrange("e o p n -> p (e o) n").bitcast(I32))
                 load_scale_rows(wbs, wb_scales.rearrange("e o b n -> (e o) b n"), [nc.sync])
-            if e == 2:
+            if e == 4:
                 load_scale_rows(ws, w_scales, [nc.sync])
                 ww = keep.tile([P, PASSES, 2 * N], U8, name="ww", align_bytes=64)
                 nc.sync.dma_start(out=ww[:].bitcast(I32), in_=w_words.rearrange("s p n -> p s n").bitcast(I32))
@@ -231,7 +232,7 @@ def tile_moe_adp_none_kernel(
                     start=True,
                     stop=True,
                 )
-            copy_out(pair != 3, y[:, first * C : last * C], y_bank[:, 0 : (last - first) * C])
+            copy_out(pair not in (2, 3), y[:, first * C : last * C], y_bank[:, 0 : (last - first) * C])
 
         per_half = HALF // P
         base_t = keep.tile([P, BLOCKS, N], F32, name="base_t")
@@ -254,7 +255,7 @@ def tile_moe_adp_none_kernel(
                 in_=acc[:, 0 : per_half * N].rearrange("p (j n) -> p j n", j=per_half),
             )
 
-        gate_ps = psum.tile([P, 2, 2, P], F32, name="total", bufs=3)
+        gate_ps = psum.tile([P, 2, 2, P], F32, name="total")
         nc.tensor.transpose(gate_ps[:, 0, 0, :], gate_rows[:], ident[:])
         gate_t = keep.tile([P, TURNED * BLOCKS], F32, name="gate_t")
         nc.scalar.copy(out=gate_t[:], in_=gate_ps[:, 0, 0, 0 : TURNED * BLOCKS])
@@ -264,8 +265,8 @@ def tile_moe_adp_none_kernel(
 
         sums = []
         for block in range(BLOCKS):
-            if block < 3:
-                sums.append(psum.tile([P, BANK], F32, name="total", bufs=3))
+            if block < 2:
+                sums.append(psum.tile([P, BANK], F32, name="total"))
             else:
                 sums.append(product_bank())
             add_turned(sums[block], base_t[:, block, :], True, False)

@@ -110,7 +110,7 @@ def tile_moe_adp_none_kernel(
 
         def gather_words(e):
             for s in range(PASSES):
-                tile = ring.tile([P, C], I32, name="slot_w", bufs=3 * PASSES, align_bytes=64)
+                tile = ring.tile([P, C], I32, name="slot_w", bufs=2 * PASSES, align_bytes=64)
                 nc.vector.tensor_copy(
                     tile[:].bitcast(U32), xw[s].bitcast(U32).indirect(entries(offs_sb, e * C, (e + 1) * C))
                 )
@@ -134,11 +134,10 @@ def tile_moe_adp_none_kernel(
         gate_rows = keep.tile([P, P], F32, name="gate_rows")
         nc.gpsimd.memset(gate_rows[:], 0.0)
         shift_scales(0, gather_scales(0), nc.scalar)
-        shift_scales(1, gather_scales(1), nc.scalar)
+        shift_scales(1, gather_scales(1), nc.sync)
         load_was(1, [nc.sync])
         gather_words(0)
         gather_words(1)
-        gather_words(2)
 
         def product_bank():
             return psum.tile([P, BANK], F32, name="product", bufs=H_BANKS)
@@ -146,8 +145,9 @@ def tile_moe_adp_none_kernel(
         def first_product(e):
             h_bf = keep.tile([P, 2, H], BF16, name="h_bf%d" % e)
             banks = [product_bank() for b in range(2)]
-            for s in range(PASSES):
-                for b in range(2):
+            order = [(s, b) for s in range(PASSES) for b in range(2)]
+            for s, b in order if e == 0 else sorted(order, key=lambda sb: sb[1]):
+                if True:
                     slot = e * C + b * P
                     planes = (slot_s0[e][:, b * P : (b + 1) * P], slot_s1[:, slot : slot + P])
                     g = e % GROUP * PASSES + s
@@ -164,7 +164,10 @@ def tile_moe_adp_none_kernel(
                 h_t = banks[b]
                 dst = h_bf[:, b, :].rearrange("p (u m d) -> p u m d", u=2, d=2)
                 src = h_t[:].rearrange("p (m u d) -> p u m d", u=2, d=2)
-                nc.scalar.activation(out=dst, in_=src, func=COPY)
+                if (e, b) == (E - 1, 1):
+                    nc.vector.tensor_copy(out=dst, in_=src)
+                else:
+                    nc.scalar.activation(out=dst, in_=src, func=COPY)
             return h_bf
 
         def turn(e, h_bf):
@@ -207,10 +210,11 @@ def tile_moe_adp_none_kernel(
                 nc.sync.dma_start(out=gate_last[:], in_=gate[TOP - 1])
                 for pos in (pos1, pos2, pos3):
                     load_list(pos)
-            if e + 3 < E:
-                gather_words(e + 3)
-            if e > 0:
-                hidden.append(turn(e - 1, rounded[e - 1]))
+            if e + 2 < E:
+                gather_words(e + 2)
+            if e % 2 == 1 or e == E - 1:
+                for done in range(len(hidden), e - e % 2):
+                    hidden.append(turn(done, rounded[done]))
         hidden.append(turn(E - 1, rounded[E - 1]))
 
         h_w = keep.tile([P, SLOTS], U32, name="waw3", align_bytes=64)

@@ -164,7 +164,7 @@ def tile_moe_adp_none_kernel(
                 h_t = banks[b]
                 dst = h_bf[:, b, :].rearrange("p (u m d) -> p u m d", u=2, d=2)
                 src = h_t[:].rearrange("p (m u d) -> p u m d", u=2, d=2)
-                if (e, b) == (E - 1, 1):
+                if e >= E - 2 and b == 1:
                     nc.vector.tensor_copy(out=dst, in_=src)
                 else:
                     nc.scalar.activation(out=dst, in_=src, func=COPY)
@@ -177,9 +177,10 @@ def tile_moe_adp_none_kernel(
                 for u in range(2):
                     nc.tensor.transpose(turned[:, b, u, :], pairs[:, b, u * P : (u + 1) * P], ident[:])
             h_in = keep.tile([P, 4 * C], BF16, name="h_in%d" % e, align_bytes=64)
-            nc.scalar.copy(
-                out=h_in[:].bitcast(F32).rearrange("p (b j u) -> p b j u", b=2, u=2),
-                in_=turned[:].rearrange("p b u j -> p b j u"),
+            copy_out(
+                e in (E - 4, E - 2),
+                h_in[:].bitcast(F32).rearrange("p (b j u) -> p b j u", b=2, u=2),
+                turned[:].rearrange("p b u j -> p b j u"),
             )
             return h_in
 
@@ -236,7 +237,7 @@ def tile_moe_adp_none_kernel(
                     start=True,
                     stop=True,
                 )
-            copy_out(pair not in (2, 3), y[:, first * C : last * C], y_bank[:, 0 : (last - first) * C])
+            copy_out(pair in (0, 4), y[:, first * C : last * C], y_bank[:, 0 : (last - first) * C])
 
         per_half = HALF // P
         base_t = keep.tile([P, BLOCKS, N], F32, name="base_t")

@@ -28,8 +28,10 @@ HALF = T // 2
 TURNED = TOP - 1
 
 CHUNKS = [(0, 1)] + [(e, e + 2) for e in range(1, E, 2)]
-GROUP = 3
-H_BANKS = 4
+VECTOR_ROUNDS = [(8, 1)]
+VECTOR_TURNED = [6, 8]
+VECTOR_Y = [6]
+SCALE_GROUPS = [(0, 2), (2, 4), (4, 6), (6, 9)]
 
 
 def tile_moe_adp_none_kernel(
@@ -39,15 +41,15 @@ def tile_moe_adp_none_kernel(
     with ExitStack() as ctx:
         keep = ctx.enter_context(tc.tile_pool(name="keep", bufs=1))
         ring = ctx.enter_context(tc.tile_pool(name="ring", bufs=2))
-        psum = ctx.enter_context(tc.psum_pool(name="psum", bufs=2))
+        psum = ctx.enter_context(tc.psum_pool(name="psum", bufs=1))
 
         def plane_tile(cols, name):
             return keep.tile([P, cols], U8, name=name, align_bytes=64)
 
-        def load_scale_rows(plane, rows, queues):
+        def load_scale_rows(plane, rows, quarters=range(4)):
             passes = rows.shape[0]
-            for q in range(4):
-                queues[q % len(queues)].dma_start(
+            for q in quarters:
+                nc.sync.dma_start(
                     out=plane[32 * q : 32 * q + 4, :].rearrange("b (g n) -> b g n", g=passes).bitcast(I32),
                     in_=rows[:, 4 * q : 4 * q + 4, :].rearrange("g b n -> b g n").bitcast(I32),
                 )
@@ -64,57 +66,31 @@ def tile_moe_adp_none_kernel(
             else:
                 nc.scalar.copy(out=dst, in_=src)
 
-        offs_sb = keep.tile([P, SLOTS // PER_COLUMN], U16, name="offs_sb")
-        nc.sync.dma_start(offs_sb[:], offs)
-        xs = plane_tile(T, "xs")
-        nc.gpsimd.memset(xs[:].bitcast(I32), 0)
-        for q in range(4):
-            (nc.sync, nc.scalar)[q // 2].dma_start(
-                out=xs[32 * q : 32 * q + 8, :].bitcast(I32), in_=x_scales[:, 4 * q : 4 * q + 4, :].bitcast(I32)
-            )
+        def bank(letter):
+            return psum.tile([P, BANK], F32, name="bank" + letter)
+
         xw_all = keep.tile([P, PASSES, T], I32, name="xw", align_bytes=64)
-        nc.sync.dma_start(out=xw_all[:], in_=x_words.rearrange("s p t d -> p s (t d)").bitcast(I32))
         xw = [xw_all[:, s, :] for s in range(PASSES)]
 
         wa_rows = wa_scales.rearrange("e s b n -> (e s) b n")
-        was = [plane_tile(GROUP * PASSES * H, "was%d" % g) for g in range(E // GROUP)]
-        slot_s1 = plane_tile(SLOTS, "slot_s1")
-        wbs = plane_tile(E * N, "wbs")
-        ws = plane_tile(PASSES * N, "ws")
-        xs1 = plane_tile(T, "xs1")
+        was, waw = {}, {}
 
-        y = keep.tile([P, SLOTS], F32, name="y")
-
-        waw, slot_s0, words = {}, {}, {}
-
-        def load_wa(c, queue):
-            first, last = CHUNKS[c]
-            tile = keep.tile([P, (last - first) * PASSES, 2 * H], U8, name="waw%d" % (c if c != 2 else 0), align_bytes=64)
-            queue.dma_start(
+        def load_wa(first, last):
+            tile = keep.tile([P, (last - first) * PASSES, 2 * H], U8, name="waw%d" % first, align_bytes=64)
+            nc.sync.dma_start(
                 out=tile[:].bitcast(I32), in_=wa_words[first:last].rearrange("e s p n -> p (e s) n").bitcast(I32)
             )
             for e in range(first, last):
                 waw[e] = tile[:, (e - first) * PASSES : (e - first + 1) * PASSES, :]
 
-        def gather_scales(c):
-            first, last = CHUNKS[c]
-            tile = ring.tile([P, (last - first) * C], U8, name="slot_s0", bufs=2, align_bytes=64)
-            nc.vector.tensor_copy(tile[:], xs[:].indirect(entries(offs_sb, first * C, last * C)))
+        for first, last in SCALE_GROUPS:
+            planes = plane_tile((last - first) * PASSES * H, "was%d" % first)
             for e in range(first, last):
-                slot_s0[e] = tile[:, (e - first) * C : (e - first + 1) * C]
-            return tile
+                was[e] = planes[:, (e - first) * PASSES * H :]
 
-        def shift_scales(c, tile, queue):
-            first, last = CHUNKS[c]
-            shift_second_pass(slot_s1[:, first * C : last * C], tile[:], queue)
-
-        def gather_words(e):
-            for s in range(PASSES):
-                tile = ring.tile([P, C], I32, name="slot_w", bufs=2 * PASSES, align_bytes=64)
-                nc.vector.tensor_copy(
-                    tile[:].bitcast(U32), xw[s].bitcast(U32).indirect(entries(offs_sb, e * C, (e + 1) * C))
-                )
-                words[e, s] = tile
+        def load_was(g, quarters=range(4)):
+            first, last = SCALE_GROUPS[g]
+            load_scale_rows(was[first], wa_rows[first * PASSES : last * PASSES], quarters)
 
         lists = []
 
@@ -123,109 +99,131 @@ def tile_moe_adp_none_kernel(
             nc.sync.dma_start(pos_sb[:], pos)
             lists.append(pos_sb)
 
-        def load_was(g, queues):
-            load_scale_rows(was[g], wa_rows[g * GROUP * PASSES : (g + 1) * GROUP * PASSES], queues)
+        load_was(0, [0])
+        xs = plane_tile(T, "xs")
+        nc.gpsimd.memset(xs[:].bitcast(I32), 0)
+        nc.gpsimd.dma_start(out=xw_all[:], in_=x_words.rearrange("s p t d -> p s (t d)").bitcast(I32))
+        for q in range(4):
+            nc.sync.dma_start(
+                out=xs[32 * q : 32 * q + 8, :].bitcast(I32), in_=x_scales[:, 4 * q : 4 * q + 4, :].bitcast(I32)
+            )
+        offs_sb = keep.tile([P, SLOTS // PER_COLUMN], U16, name="offs_sb")
+        nc.sync.dma_start(offs_sb[:], offs)
+        load_was(0, [1, 2, 3])
+        load_wa(0, 1)
+        load_wa(2, 4)
+        load_wa(1, 2)
 
-        load_wa(0, nc.sync)
-        load_was(0, [nc.sync])
-        load_wa(1, nc.sync)
+        slot_s1 = plane_tile(SLOTS, "slot_s1")
+        wbs = plane_tile(E * N, "wbs")
+        ws = plane_tile(PASSES * N, "ws")
+        xs1 = plane_tile(T, "xs1")
+        y = keep.tile([P, SLOTS], F32, name="y")
         ident = keep.tile([P, P], F32, name="ident")
         make_identity(nc, ident[:])
         gate_rows = keep.tile([P, P], F32, name="gate_rows")
         nc.gpsimd.memset(gate_rows[:], 0.0)
-        shift_scales(0, gather_scales(0), nc.scalar)
-        shift_scales(1, gather_scales(1), nc.sync)
-        load_was(1, [nc.sync])
+
+        slot_s0, words = {}, {}
+
+        def gather_scales(c):
+            first, last = CHUNKS[c]
+            tile = plane_tile((last - first) * C, "slot_s0_%d" % c)
+            nc.vector.tensor_copy(tile[:], xs[:].indirect(entries(offs_sb, first * C, last * C)))
+            for e in range(first, last):
+                slot_s0[e] = tile[:, (e - first) * C : (e - first + 1) * C]
+            shift_second_pass(slot_s1[:, first * C : last * C], tile[:], nc.sync if c else nc.scalar)
+
+        def gather_words(e):
+            for s in range(PASSES):
+                tile = keep.tile([P, C], I32, name="slot_w%d_%d" % (e, s), align_bytes=64)
+                nc.vector.tensor_copy(
+                    tile[:].bitcast(U32), xw[s].bitcast(U32).indirect(entries(offs_sb, e * C, (e + 1) * C))
+                )
+                words[e, s] = tile
+
+        gather_scales(0)
+        gather_scales(1)
+        load_wa(4, 6)
+        load_was(1)
         gather_words(0)
         gather_words(1)
+        gather_scales(2)
+        load_wa(6, 8)
+        load_list(pos1)
+        load_list(pos2)
+        load_was(2)
+        gather_words(2)
+        gather_words(3)
+        gather_scales(3)
+        load_wa(8, 9)
+        load_list(pos3)
+        nc.sync.dma_start(
+            out=gate_rows[0 : TURNED * BLOCKS, :], in_=gate[0:TURNED, 0, :].rearrange("r (b t) -> r b t", t=P)
+        )
+        load_was(3)
+        gather_words(4)
+        gather_words(5)
+        gather_scales(4)
+        wbw = keep.tile([P, E, 2 * N], U8, name="wbw", align_bytes=64)
+        nc.sync.dma_start(out=wbw[:].bitcast(I32), in_=wb_words.rearrange("e o p n -> p (e o) n").bitcast(I32))
+        load_scale_rows(wbs, wb_scales.rearrange("e o b n -> (e o) b n"))
+        load_scale_rows(ws, w_scales)
+        ww = keep.tile([P, PASSES, 2 * N], U8, name="ww", align_bytes=64)
+        nc.sync.dma_start(out=ww[:].bitcast(I32), in_=w_words.rearrange("s p n -> p s n").bitcast(I32))
+        shift_second_pass(xs1[:], xs[:], nc.sync)
+        gate_last = keep.tile([P, T], F32, name="gate_last")
+        nc.sync.dma_start(out=gate_last[:], in_=gate[TOP - 1])
+        gather_words(6)
+        gather_words(7)
+        gather_words(8)
 
-        def product_bank():
-            return psum.tile([P, BANK], F32, name="product", bufs=H_BANKS)
+        rounded = {}
+        h_w = keep.tile([P, SLOTS], U32, name="h_w", align_bytes=64)
+        h_s = keep.tile([P, SLOTS], U8, name="h_s", align_bytes=64)
 
         def first_product(e):
             h_bf = keep.tile([P, 2, H], BF16, name="h_bf%d" % e)
-            banks = [product_bank() for b in range(2)]
-            order = [(s, b) for s in range(PASSES) for b in range(2)]
-            for s, b in order if e == 0 else sorted(order, key=lambda sb: sb[1]):
-                if True:
-                    slot = e * C + b * P
-                    planes = (slot_s0[e][:, b * P : (b + 1) * P], slot_s1[:, slot : slot + P])
-                    g = e % GROUP * PASSES + s
-                    nc.tensor.matmul_mx(
-                        out=banks[b][:],
-                        lhsT=words[e, s][:, b * P : (b + 1) * P].bitcast(FP8X4),
-                        lhsT_scale=planes[s],
-                        rhs=waw[e][:, s, :].bitcast(FP4X4),
-                        rhs_scale=was[e // GROUP][:, g * H : (g + 1) * H],
-                        start=(s == 0),
-                        stop=(s == PASSES - 1),
-                    )
+            banks = [bank(letter) for letter in ("AG", "CD", "AB", "CD", "CD", "AB", "AB", "CD", "EF")[e]]
+            for b, s in [(b, s) for b in range(2) for s in range(PASSES)]:
+                slot = e * C + b * P
+                planes = (slot_s0[e][:, b * P : (b + 1) * P], slot_s1[:, slot : slot + P])
+                nc.tensor.matmul_mx(
+                    out=banks[b][:],
+                    lhsT=words[e, s][:, b * P : (b + 1) * P].bitcast(FP8X4),
+                    lhsT_scale=planes[s],
+                    rhs=waw[e][:, s, :].bitcast(FP4X4),
+                    rhs_scale=was[e][:, s * H : (s + 1) * H],
+                    start=(s == 0),
+                    stop=(s == PASSES - 1),
+                )
             for b in range(2):
-                h_t = banks[b]
                 dst = h_bf[:, b, :].rearrange("p (u m d) -> p u m d", u=2, d=2)
-                src = h_t[:].rearrange("p (m u d) -> p u m d", u=2, d=2)
-                if e >= E - 2 and b == 1:
+                src = banks[b][:].rearrange("p (m u d) -> p u m d", u=2, d=2)
+                if (e, b) in VECTOR_ROUNDS:
                     nc.vector.tensor_copy(out=dst, in_=src)
                 else:
                     nc.scalar.activation(out=dst, in_=src, func=COPY)
-            return h_bf
+            rounded[e] = h_bf
 
-        def turn(e, h_bf):
-            turned = psum.tile([P, 2, 2, P], F32, name="turned")
-            pairs = h_bf[:].bitcast(F32)
+        def turn(e):
+            turned = bank("GABCDABCE"[e])[:].rearrange("p (b u j) -> p b u j", b=2, u=2)
+            pairs = rounded[e][:].bitcast(F32)
             for b in range(2):
                 for u in range(2):
                     nc.tensor.transpose(turned[:, b, u, :], pairs[:, b, u * P : (u + 1) * P], ident[:])
             h_in = keep.tile([P, 4 * C], BF16, name="h_in%d" % e, align_bytes=64)
             copy_out(
-                e in (E - 4, E - 2),
+                e in VECTOR_TURNED,
                 h_in[:].bitcast(F32).rearrange("p (b j u) -> p b j u", b=2, u=2),
-                turned[:].rearrange("p b u j -> p b j u"),
+                turned.rearrange("p b u j -> p b j u"),
             )
-            return h_in
-
-        rounded, hidden = [], []
-        for e in range(E):
-            rounded.append(first_product(e))
-            if e in (0, 2, 4):
-                shift_scales(2 + e // 2, gather_scales(2 + e // 2), nc.sync)
-            if e == 0:
-                load_wa(2, nc.scalar)
-                load_wa(3, nc.sync)
-            if e == 2:
-                load_was(2, [nc.sync])
-                load_wa(4, nc.sync)
-            if e == 4:
-                wbw = keep.tile([P, E, 2 * N], U8, name="wbw", align_bytes=64)
-                nc.sync.dma_start(out=wbw[:].bitcast(I32), in_=wb_words.rearrange("e o p n -> p (e o) n").bitcast(I32))
-                load_scale_rows(wbs, wb_scales.rearrange("e o b n -> (e o) b n"), [nc.sync])
-            if e == 4:
-                load_scale_rows(ws, w_scales, [nc.sync])
-                ww = keep.tile([P, PASSES, 2 * N], U8, name="ww", align_bytes=64)
-                nc.sync.dma_start(out=ww[:].bitcast(I32), in_=w_words.rearrange("s p n -> p s n").bitcast(I32))
-                shift_second_pass(xs1[:], xs[:], nc.sync)
-                nc.sync.dma_start(
-                    out=gate_rows[0 : TURNED * BLOCKS, :], in_=gate[0:TURNED, 0, :].rearrange("r (b t) -> r b t", t=P)
-                )
-                gate_last = keep.tile([P, T], F32, name="gate_last")
-                nc.sync.dma_start(out=gate_last[:], in_=gate[TOP - 1])
-                for pos in (pos1, pos2, pos3):
-                    load_list(pos)
-            if e + 2 < E:
-                gather_words(e + 2)
-            if e % 2 == 1 or e == E - 1:
-                for done in range(len(hidden), e - e % 2):
-                    hidden.append(turn(done, rounded[done]))
-        hidden.append(turn(E - 1, rounded[E - 1]))
-
-        h_w = keep.tile([P, SLOTS], U32, name="waw3", align_bytes=64)
-        h_s = keep.tile([P, SLOTS], U8, name="h_s", align_bytes=64)
-        for e in range(E):
             cols = slice(e * C, (e + 1) * C)
-            nc.vector.quantize_mx(out=h_w[:, cols].bitcast(FP8X4), scales=h_s[:, cols], in_=hidden[e][:])
-        for pair, first in enumerate(range(0, E, 2)):
+            nc.vector.quantize_mx(out=h_w[:, cols].bitcast(FP8X4), scales=h_s[:, cols], in_=h_in[:])
+
+        def second_product(first, letter):
             last = min(first + 2, E)
-            y_bank = product_bank()
+            y_bank = bank(letter)
             for e in range(first, last):
                 cols = slice(e * C, (e + 1) * C)
                 nc.tensor.matmul_mx(
@@ -237,12 +235,13 @@ def tile_moe_adp_none_kernel(
                     start=True,
                     stop=True,
                 )
-            copy_out(pair in (0, 4), y[:, first * C : last * C], y_bank[:, 0 : (last - first) * C])
+            copy_out(first in VECTOR_Y, y[:, first * C : last * C], y_bank[:, 0 : (last - first) * C])
 
         per_half = HALF // P
         base_t = keep.tile([P, BLOCKS, N], F32, name="base_t")
-        for half in range(2):
-            acc = product_bank()
+
+        def frozen_layer(half, letter):
+            acc = bank(letter)
             for j in range(per_half):
                 cols = slice(half * HALF + j * P, half * HALF + (j + 1) * P)
                 for s in range(PASSES):
@@ -260,27 +259,39 @@ def tile_moe_adp_none_kernel(
                 in_=acc[:, 0 : per_half * N].rearrange("p (j n) -> p j n", j=per_half),
             )
 
-        gate_ps = psum.tile([P, 2, 2, P], F32, name="total")
-        nc.tensor.transpose(gate_ps[:, 0, 0, :], gate_rows[:], ident[:])
+        first_product(0)
+        first_product(1)
+        turn(0)
+        for e in range(2, E - 3, 2):
+            first_product(e)
+            first_product(e + 1)
+            turn(e - 1)
+            turn(e)
+        for e in range(E - 3, E):
+            first_product(e)
+        gate_ps = bank("D")
+        nc.tensor.transpose(gate_ps[:, 0:P], gate_rows[:], ident[:])
         gate_t = keep.tile([P, TURNED * BLOCKS], F32, name="gate_t")
-        nc.scalar.copy(out=gate_t[:], in_=gate_ps[:, 0, 0, 0 : TURNED * BLOCKS])
+        nc.scalar.copy(out=gate_t[:], in_=gate_ps[:, 0 : TURNED * BLOCKS])
+        for e in range(E - 4, E):
+            turn(e)
+        for first, letter in zip(range(0, E, 2), "ABFCE"):
+            second_product(first, letter)
+        frozen_layer(0, "A")
+        frozen_layer(1, "B")
 
         def add_turned(total, tile_t, start, stop):
             nc.tensor.matmul(total[:, 0:P], lhsT=tile_t, rhs=ident[:], is_transpose=True, start=start, stop=stop)
 
         sums = []
         for block in range(BLOCKS):
-            if block < 2:
-                sums.append(psum.tile([P, BANK], F32, name="total"))
-            else:
-                sums.append(product_bank())
+            sums.append(bank("GHDFAB"[block]))
             add_turned(sums[block], base_t[:, block, :], True, False)
         for half in range(2):
             for r in range(TURNED):
                 picked = ring.tile([P, HALF], F32, name="picked", bufs=2 * TURNED)
                 nc.vector.tensor_copy(picked[:], y[:].indirect(entries(lists[r], half * HALF, (half + 1) * HALF)))
-                picked_t = psum.tile([P, 2, 2, P], F32, name="turned")
-                flat_t = picked_t[:].rearrange("p b u j -> p (b u j)")
+                flat_t = bank("CE"[r])
                 for j in range(per_half):
                     nc.tensor.transpose(flat_t[:, j * P : (j + 1) * P], picked[:, j * P : (j + 1) * P], ident[:])
                 for j in range(per_half):

@@ -29,9 +29,9 @@ TURNED = TOP - 1
 
 CHUNKS = [(0, 1)] + [(e, e + 2) for e in range(1, E, 2)]
 VECTOR_ROUNDS = [(8, 1)]
-VECTOR_TURNED = [6, 8]
-VECTOR_Y = [6]
-SCALE_GROUPS = [(0, 2), (2, 4), (4, 6), (6, 9)]
+VECTOR_TURNED = [7]
+VECTOR_Y = [4, 8]
+SCALE_GROUPS = [(0, 7), (7, 14), (14, 18)]
 
 
 def tile_moe_adp_none_kernel(
@@ -46,10 +46,10 @@ def tile_moe_adp_none_kernel(
         def plane_tile(cols, name):
             return keep.tile([P, cols], U8, name=name, align_bytes=64)
 
-        def load_scale_rows(plane, rows, quarters=range(4)):
+        def load_scale_rows(plane, rows, quarters=range(4), queue=nc.sync):
             passes = rows.shape[0]
             for q in quarters:
-                nc.sync.dma_start(
+                queue.dma_start(
                     out=plane[32 * q : 32 * q + 4, :].rearrange("b (g n) -> b g n", g=passes).bitcast(I32),
                     in_=rows[:, 4 * q : 4 * q + 4, :].rearrange("g b n -> b g n").bitcast(I32),
                 )
@@ -75,22 +75,24 @@ def tile_moe_adp_none_kernel(
         wa_rows = wa_scales.rearrange("e s b n -> (e s) b n")
         was, waw = {}, {}
 
-        def load_wa(first, last):
-            tile = keep.tile([P, (last - first) * PASSES, 2 * H], U8, name="waw%d" % first, align_bytes=64)
-            nc.sync.dma_start(
-                out=tile[:].bitcast(I32), in_=wa_words[first:last].rearrange("e s p n -> p (e s) n").bitcast(I32)
-            )
+        def load_wa(first, last, passes=range(PASSES)):
+            count = len(passes)
+            name = "waw%d_%d" % (first, passes[0])
+            tile = keep.tile([P, (last - first) * count, 2 * H], U8, name=name, align_bytes=64)
+            rows = wa_words[first:last, passes[0] : passes[0] + count]
+            nc.sync.dma_start(out=tile[:].bitcast(I32), in_=rows.rearrange("e s p n -> p (e s) n").bitcast(I32))
             for e in range(first, last):
-                waw[e] = tile[:, (e - first) * PASSES : (e - first + 1) * PASSES, :]
+                for s in passes:
+                    waw[e, s] = tile[:, (e - first) * count + s - passes[0], :]
 
         for first, last in SCALE_GROUPS:
-            planes = plane_tile((last - first) * PASSES * H, "was%d" % first)
-            for e in range(first, last):
-                was[e] = planes[:, (e - first) * PASSES * H :]
+            planes = plane_tile((last - first) * H, "was%d" % first)
+            for g in range(first, last):
+                was[g] = planes[:, (g - first) * H :]
 
-        def load_was(g, quarters=range(4)):
-            first, last = SCALE_GROUPS[g]
-            load_scale_rows(was[first], wa_rows[first * PASSES : last * PASSES], quarters)
+        def load_was(group, quarters=range(4), queue=nc.sync):
+            first, last = SCALE_GROUPS[group]
+            load_scale_rows(was[first], wa_rows[first:last], quarters, queue)
 
         lists = []
 
@@ -99,20 +101,19 @@ def tile_moe_adp_none_kernel(
             nc.sync.dma_start(pos_sb[:], pos)
             lists.append(pos_sb)
 
-        load_was(0, [0])
-        xs = plane_tile(T, "xs")
-        nc.gpsimd.memset(xs[:].bitcast(I32), 0)
-        nc.gpsimd.dma_start(out=xw_all[:], in_=x_words.rearrange("s p t d -> p s (t d)").bitcast(I32))
-        for q in range(4):
-            nc.sync.dma_start(
-                out=xs[32 * q : 32 * q + 8, :].bitcast(I32), in_=x_scales[:, 4 * q : 4 * q + 4, :].bitcast(I32)
-            )
         offs_sb = keep.tile([P, SLOTS // PER_COLUMN], U16, name="offs_sb")
         nc.sync.dma_start(offs_sb[:], offs)
-        load_was(0, [1, 2, 3])
+        load_was(0, [0, 2], nc.scalar)
+        xs = plane_tile(T, "xs")
+        nc.gpsimd.memset(xs[:].bitcast(I32), 0)
+        for q in range(4):
+            (nc.sync, nc.scalar)[q // 2].dma_start(
+                out=xs[32 * q : 32 * q + 8, :].bitcast(I32), in_=x_scales[:, 4 * q : 4 * q + 4, :].bitcast(I32)
+            )
+        nc.sync.dma_start(out=xw_all[:], in_=x_words.rearrange("s p t d -> p s (t d)").bitcast(I32))
+        load_was(0, [1, 3])
         load_wa(0, 1)
-        load_wa(2, 4)
-        load_wa(1, 2)
+        load_wa(1, 3, [1])
 
         slot_s1 = plane_tile(SLOTS, "slot_s1")
         wbs = plane_tile(E * N, "wbs")
@@ -144,36 +145,39 @@ def tile_moe_adp_none_kernel(
 
         gather_scales(0)
         gather_scales(1)
-        load_wa(4, 6)
+        load_wa(1, 3, [0])
         load_was(1)
+        load_wa(3, 5, [1])
+        load_wa(5, 7, [1])
         gather_words(0)
-        gather_words(1)
         gather_scales(2)
-        load_wa(6, 8)
-        load_list(pos1)
-        load_list(pos2)
+        load_wa(3, 5, [0])
+        load_wa(7, 9, [1])
         load_was(2)
-        gather_words(2)
-        gather_words(3)
-        gather_scales(3)
-        load_wa(8, 9)
-        load_list(pos3)
-        nc.sync.dma_start(
-            out=gate_rows[0 : TURNED * BLOCKS, :], in_=gate[0:TURNED, 0, :].rearrange("r (b t) -> r b t", t=P)
-        )
-        load_was(3)
-        gather_words(4)
-        gather_words(5)
-        gather_scales(4)
-        wbw = keep.tile([P, E, 2 * N], U8, name="wbw", align_bytes=64)
-        nc.sync.dma_start(out=wbw[:].bitcast(I32), in_=wb_words.rearrange("e o p n -> p (e o) n").bitcast(I32))
-        load_scale_rows(wbs, wb_scales.rearrange("e o b n -> (e o) b n"))
-        load_scale_rows(ws, w_scales)
         ww = keep.tile([P, PASSES, 2 * N], U8, name="ww", align_bytes=64)
         nc.sync.dma_start(out=ww[:].bitcast(I32), in_=w_words.rearrange("s p n -> p s n").bitcast(I32))
         shift_second_pass(xs1[:], xs[:], nc.sync)
+        gather_words(1)
+        gather_words(2)
+        gather_scales(3)
+        load_wa(5, 7, [0])
+        load_scale_rows(ws, w_scales)
+        nc.sync.dma_start(
+            out=gate_rows[0 : TURNED * BLOCKS, :], in_=gate[0:TURNED, 0, :].rearrange("r (b t) -> r b t", t=P)
+        )
+        load_list(pos1)
+        load_list(pos2)
+        gather_words(3)
+        gather_words(4)
+        gather_scales(4)
+        load_wa(7, 9, [0])
+        wbw = keep.tile([P, E, 2 * N], U8, name="wbw", align_bytes=64)
+        nc.sync.dma_start(out=wbw[:].bitcast(I32), in_=wb_words.rearrange("e o p n -> p (e o) n").bitcast(I32))
+        load_scale_rows(wbs, wb_scales.rearrange("e o b n -> (e o) b n"))
+        load_list(pos3)
         gate_last = keep.tile([P, T], F32, name="gate_last")
         nc.sync.dma_start(out=gate_last[:], in_=gate[TOP - 1])
+        gather_words(5)
         gather_words(6)
         gather_words(7)
         gather_words(8)
@@ -184,7 +188,7 @@ def tile_moe_adp_none_kernel(
 
         def first_product(e):
             h_bf = keep.tile([P, 2, H], BF16, name="h_bf%d" % e)
-            banks = [bank(letter) for letter in ("AG", "CD", "AB", "CD", "CD", "AB", "AB", "CD", "EF")[e]]
+            banks = [bank(letter) for letter in ("GH", "AB", "CD", "CD", "AB", "AB", "CD", "CD", "AB")[e]]
             for b, s in [(b, s) for b in range(2) for s in range(PASSES)]:
                 slot = e * C + b * P
                 planes = (slot_s0[e][:, b * P : (b + 1) * P], slot_s1[:, slot : slot + P])
@@ -192,8 +196,8 @@ def tile_moe_adp_none_kernel(
                     out=banks[b][:],
                     lhsT=words[e, s][:, b * P : (b + 1) * P].bitcast(FP8X4),
                     lhsT_scale=planes[s],
-                    rhs=waw[e][:, s, :].bitcast(FP4X4),
-                    rhs_scale=was[e][:, s * H : (s + 1) * H],
+                    rhs=waw[e, s].bitcast(FP4X4),
+                    rhs_scale=was[e * PASSES + s][:, 0:H],
                     start=(s == 0),
                     stop=(s == PASSES - 1),
                 )
@@ -207,7 +211,7 @@ def tile_moe_adp_none_kernel(
             rounded[e] = h_bf
 
         def turn(e):
-            turned = bank("GABCDABCE"[e])[:].rearrange("p (b u j) -> p b u j", b=2, u=2)
+            turned = bank("ABCDABCDA"[e])[:].rearrange("p (b u j) -> p b u j", b=2, u=2)
             pairs = rounded[e][:].bitcast(F32)
             for b in range(2):
                 for u in range(2):
@@ -260,38 +264,33 @@ def tile_moe_adp_none_kernel(
             )
 
         first_product(0)
-        first_product(1)
-        turn(0)
-        for e in range(2, E - 3, 2):
+        for e in range(1, E, 2):
             first_product(e)
             first_product(e + 1)
             turn(e - 1)
             turn(e)
-        for e in range(E - 3, E):
-            first_product(e)
-        gate_ps = bank("D")
+        turn(E - 1)
+        for first, letter in zip(range(0, E, 2), "BCDAE"):
+            second_product(first, letter)
+        frozen_layer(0, "B")
+        frozen_layer(1, "C")
+        gate_ps = bank("B")
         nc.tensor.transpose(gate_ps[:, 0:P], gate_rows[:], ident[:])
         gate_t = keep.tile([P, TURNED * BLOCKS], F32, name="gate_t")
         nc.scalar.copy(out=gate_t[:], in_=gate_ps[:, 0 : TURNED * BLOCKS])
-        for e in range(E - 4, E):
-            turn(e)
-        for first, letter in zip(range(0, E, 2), "ABFCE"):
-            second_product(first, letter)
-        frozen_layer(0, "A")
-        frozen_layer(1, "B")
 
         def add_turned(total, tile_t, start, stop):
             nc.tensor.matmul(total[:, 0:P], lhsT=tile_t, rhs=ident[:], is_transpose=True, start=start, stop=stop)
 
         sums = []
         for block in range(BLOCKS):
-            sums.append(bank("GHDFAB"[block]))
+            sums.append(bank("FGHDBC"[block]))
             add_turned(sums[block], base_t[:, block, :], True, False)
         for half in range(2):
             for r in range(TURNED):
                 picked = ring.tile([P, HALF], F32, name="picked", bufs=2 * TURNED)
                 nc.vector.tensor_copy(picked[:], y[:].indirect(entries(lists[r], half * HALF, (half + 1) * HALF)))
-                flat_t = bank("CE"[r])
+                flat_t = bank("AE"[r])
                 for j in range(per_half):
                     nc.tensor.transpose(flat_t[:, j * P : (j + 1) * P], picked[:, j * P : (j + 1) * P], ident[:])
                 for j in range(per_half):

@@ -50,8 +50,8 @@ def tile_moe_adp_none_kernel(
             passes = rows.shape[0]
             for q in quarters:
                 queue.dma_start(
-                    out=plane[32 * q : 32 * q + 4, :].rearrange("b (g n) -> b g n", g=passes).bitcast(I32),
-                    in_=rows[:, 4 * q : 4 * q + 4, :].rearrange("g b n -> b g n").bitcast(I32),
+                    out=plane[q:P:32, :].rearrange("b (g n) -> b g n", g=passes).bitcast(I32),
+                    in_=rows[:, q:16:4, :].rearrange("g b n -> b g n").bitcast(I32),
                 )
 
         def shift_second_pass(dst, src, queue):
@@ -186,10 +186,11 @@ def tile_moe_adp_none_kernel(
         h_w = keep.tile([P, SLOTS], U32, name="h_w", align_bytes=64)
         h_s = keep.tile([P, SLOTS], U8, name="h_s", align_bytes=64)
 
-        def first_product(e):
+        def first_product(e, letters, passes_first=False):
             h_bf = keep.tile([P, 2, H], BF16, name="h_bf%d" % e)
-            banks = [bank(letter) for letter in ("GH", "AB", "CD", "CD", "AB", "AB", "CD", "CD", "AB")[e]]
-            for b, s in [(b, s) for b in range(2) for s in range(PASSES)]:
+            banks = [bank(letter) for letter in letters]
+            order = [(b, s) for b in range(2) for s in range(PASSES)]
+            for b, s in sorted(order, key=lambda bs: bs[1]) if passes_first else order:
                 slot = e * C + b * P
                 planes = (slot_s0[e][:, b * P : (b + 1) * P], slot_s1[:, slot : slot + P])
                 nc.tensor.matmul_mx(
@@ -210,8 +211,8 @@ def tile_moe_adp_none_kernel(
                     nc.scalar.activation(out=dst, in_=src, func=COPY)
             rounded[e] = h_bf
 
-        def turn(e):
-            turned = bank("ABCDABCDA"[e])[:].rearrange("p (b u j) -> p b u j", b=2, u=2)
+        def turn(e, letter):
+            turned = bank(letter)[:].rearrange("p (b u j) -> p b u j", b=2, u=2)
             pairs = rounded[e][:].bitcast(F32)
             for b in range(2):
                 for u in range(2):
@@ -225,8 +226,7 @@ def tile_moe_adp_none_kernel(
             cols = slice(e * C, (e + 1) * C)
             nc.vector.quantize_mx(out=h_w[:, cols].bitcast(FP8X4), scales=h_s[:, cols], in_=h_in[:])
 
-        def second_product(first, letter):
-            last = min(first + 2, E)
+        def second_product(first, last, letter):
             y_bank = bank(letter)
             for e in range(first, last):
                 cols = slice(e * C, (e + 1) * C)
@@ -263,15 +263,29 @@ def tile_moe_adp_none_kernel(
                 in_=acc[:, 0 : per_half * N].rearrange("p (j n) -> p j n", j=per_half),
             )
 
-        first_product(0)
-        for e in range(1, E, 2):
-            first_product(e)
-            first_product(e + 1)
-            turn(e - 1)
-            turn(e)
-        turn(E - 1)
-        for first, letter in zip(range(0, E, 2), "BCDAE"):
-            second_product(first, letter)
+        first_product(0, "GH")
+        first_product(1, "AB")
+        first_product(2, "CD")
+        turn(0, "A")
+        turn(1, "B")
+        first_product(3, "CD")
+        first_product(4, "AB")
+        turn(2, "C")
+        turn(3, "D")
+        first_product(5, "AB")
+        first_product(6, "CD")
+        turn(4, "A")
+        turn(5, "B")
+        first_product(7, "CD")
+        first_product(8, "AB")
+        turn(6, "C")
+        turn(7, "D")
+        turn(8, "A")
+        second_product(0, 2, "B")
+        second_product(2, 4, "C")
+        second_product(4, 6, "D")
+        second_product(6, 8, "A")
+        second_product(8, 9, "E")
         frozen_layer(0, "B")
         frozen_layer(1, "C")
         gate_ps = bank("B")
@@ -295,22 +309,39 @@ def tile_moe_adp_none_kernel(
                     nc.tensor.transpose(flat_t[:, j * P : (j + 1) * P], picked[:, j * P : (j + 1) * P], ident[:])
                 for j in range(per_half):
                     block = half * per_half + j
-                    scaled = ring.tile([P, N], F32, name="scaled", bufs=2 * per_half)
+                    if (half, r, j) == (0, TURNED - 1, per_half - 1):
+                        scaled = keep.tile([P, N], F32, name="closing")
+                    else:
+                        scaled = ring.tile([P, N], F32, name="scaled", bufs=2 * per_half)
                     col = r * BLOCKS + block
                     nc.scalar.activation(
                         out=scaled[:], in_=flat_t[:, j * P : (j + 1) * P], func=COPY, scale=gate_t[:, col : col + 1]
                     )
                     add_turned(sums[block], scaled[:], False, r == TURNED - 1)
-        for half in range(2):
-            cols = slice(half * HALF, (half + 1) * HALF)
-            third = ring.tile([P, HALF], F32, name="third")
+        runs = [(0, per_half), (per_half, BLOCKS - 1), (BLOCKS - 1, BLOCKS)]
+        thirds = []
+
+        def gather_third(first, last):
+            name = "closing" if last == BLOCKS else "third%d" % first
+            third = keep.tile([P, (last - first) * P], F32, name=name)
             nc.vector.tensor_tensor(
-                third[:], y[:].indirect(entries(lists[TOP - 1], cols.start, cols.stop)), gate_last[:, cols], MULT
+                third[:],
+                y[:].indirect(entries(lists[TOP - 1], first * P, last * P)),
+                gate_last[:, first * P : last * P],
+                MULT,
             )
-            result = ring.tile([P, HALF], F32, name="result")
-            for j in range(per_half):
-                block_cols = slice(j * P, (j + 1) * P)
-                nc.vector.tensor_tensor(
-                    result[:, block_cols], sums[half * per_half + j][:, 0:P], third[:, block_cols], ADD
-                )
-            nc.sync.dma_start(out=out[:, cols], in_=result[:])
+            thirds.append(third)
+
+        def add_and_store(first, last, third):
+            result = keep.tile([P, (last - first) * P], F32, name="result%d" % first)
+            for block in range(first, last):
+                cols = slice((block - first) * P, (block - first + 1) * P)
+                nc.vector.tensor_tensor(result[:, cols], sums[block][:, 0:P], third[:, cols], ADD)
+            queue = nc.scalar if last == BLOCKS else nc.sync
+            queue.dma_start(out=out[:, first * P : last * P], in_=result[:])
+
+        gather_third(*runs[0])
+        for k in range(len(runs)):
+            if k + 1 < len(runs):
+                gather_third(*runs[k + 1])
+            add_and_store(*runs[k], thirds[k])

@@ -31,7 +31,7 @@ CHUNKS = [(0, 1)] + [(e, e + 2) for e in range(1, E, 2)]
 VECTOR_ROUNDS = [(8, 1)]
 VECTOR_TURNED = [7]
 VECTOR_Y = [4, 8]
-SCALE_GROUPS = [(0, 7), (7, 14), (14, 18)]
+SCALE_GROUPS = [(0, 7), (7, 18)]
 
 
 def tile_moe_adp_none_kernel(
@@ -97,7 +97,7 @@ def tile_moe_adp_none_kernel(
         lists = []
 
         def load_list(pos):
-            pos_sb = keep.tile([P, T // PER_COLUMN], U16, name="pos%d_sb" % (len(lists) + 1))
+            pos_sb = keep.tile([P, T // PER_COLUMN], U16, name="pos_sb%d" % len(lists))
             nc.sync.dma_start(pos_sb[:], pos)
             lists.append(pos_sb)
 
@@ -113,7 +113,7 @@ def tile_moe_adp_none_kernel(
         nc.sync.dma_start(out=xw_all[:], in_=x_words.rearrange("s p t d -> p s (t d)").bitcast(I32))
         load_was(0, [1, 3])
         load_wa(0, 1)
-        load_wa(1, 3, [1])
+        load_wa(1, 2)
 
         slot_s1 = plane_tile(SLOTS, "slot_s1")
         wbs = plane_tile(E * N, "wbs")
@@ -144,37 +144,33 @@ def tile_moe_adp_none_kernel(
                 words[e, s] = tile
 
         gather_scales(0)
-        gather_scales(1)
-        load_wa(1, 3, [0])
         load_was(1)
+        gather_scales(1)
+        load_wa(2, 3)
         load_wa(3, 5, [1])
-        load_wa(5, 7, [1])
         gather_words(0)
         gather_scales(2)
         load_wa(3, 5, [0])
-        load_wa(7, 9, [1])
-        load_was(2)
+        load_wa(5, 7)
         ww = keep.tile([P, PASSES, 2 * N], U8, name="ww", align_bytes=64)
         nc.sync.dma_start(out=ww[:].bitcast(I32), in_=w_words.rearrange("s p n -> p s n").bitcast(I32))
         shift_second_pass(xs1[:], xs[:], nc.sync)
         gather_words(1)
         gather_words(2)
         gather_scales(3)
-        load_wa(5, 7, [0])
-        load_scale_rows(ws, w_scales)
-        nc.sync.dma_start(
-            out=gate_rows[0 : TURNED * BLOCKS, :], in_=gate[0:TURNED, 0, :].rearrange("r (b t) -> r b t", t=P)
-        )
-        load_list(pos1)
-        load_list(pos2)
+        load_wa(7, 9)
         gather_words(3)
         gather_words(4)
         gather_scales(4)
-        load_wa(7, 9, [0])
+        load_scale_rows(ws, w_scales)
         wbw = keep.tile([P, E, 2 * N], U8, name="wbw", align_bytes=64)
         nc.sync.dma_start(out=wbw[:].bitcast(I32), in_=wb_words.rearrange("e o p n -> p (e o) n").bitcast(I32))
         load_scale_rows(wbs, wb_scales.rearrange("e o b n -> (e o) b n"))
-        load_list(pos3)
+        for pos in (pos1, pos2, pos3):
+            load_list(pos)
+        nc.sync.dma_start(
+            out=gate_rows[0 : TURNED * BLOCKS, :], in_=gate[0:TURNED, 0, :].rearrange("r (b t) -> r b t", t=P)
+        )
         gate_last = keep.tile([P, T], F32, name="gate_last")
         nc.sync.dma_start(out=gate_last[:], in_=gate[TOP - 1])
         gather_words(5)
@@ -226,6 +222,21 @@ def tile_moe_adp_none_kernel(
             cols = slice(e * C, (e + 1) * C)
             nc.vector.quantize_mx(out=h_w[:, cols].bitcast(FP8X4), scales=h_s[:, cols], in_=h_in[:])
 
+        def turn_blocks(e, letters):
+            pairs = rounded[e][:].bitcast(F32)
+            for b in range(2):
+                turned = bank(letters[b])[:, 0 : 2 * P].rearrange("p (u j) -> p u j", u=2)
+                for u in range(2):
+                    nc.tensor.transpose(turned[:, u, :], pairs[:, b, u * P : (u + 1) * P], ident[:])
+                h_in = keep.tile([P, 4 * P], BF16, name="h_in%d_%d" % (e, b), align_bytes=64)
+                copy_out(
+                    b == 1,
+                    h_in[:].bitcast(F32).rearrange("p (j u) -> p j u", u=2),
+                    turned.rearrange("p u j -> p j u"),
+                )
+                cols = slice(e * C + b * P, e * C + (b + 1) * P)
+                nc.vector.quantize_mx(out=h_w[:, cols].bitcast(FP8X4), scales=h_s[:, cols], in_=h_in[:])
+
         def second_product(first, last, letter):
             y_bank = bank(letter)
             for e in range(first, last):
@@ -263,7 +274,7 @@ def tile_moe_adp_none_kernel(
                 in_=acc[:, 0 : per_half * N].rearrange("p (j n) -> p j n", j=per_half),
             )
 
-        first_product(0, "GH")
+        first_product(0, "GH", True)
         first_product(1, "AB")
         first_product(2, "CD")
         turn(0, "A")
@@ -288,7 +299,7 @@ def tile_moe_adp_none_kernel(
         second_product(8, 9, "E")
         frozen_layer(0, "B")
         frozen_layer(1, "C")
-        gate_ps = bank("B")
+        gate_ps = bank("H")
         nc.tensor.transpose(gate_ps[:, 0:P], gate_rows[:], ident[:])
         gate_t = keep.tile([P, TURNED * BLOCKS], F32, name="gate_t")
         nc.scalar.copy(out=gate_t[:], in_=gate_ps[:, 0 : TURNED * BLOCKS])
@@ -300,24 +311,35 @@ def tile_moe_adp_none_kernel(
         for block in range(BLOCKS):
             sums.append(bank("FGHDBC"[block]))
             add_turned(sums[block], base_t[:, block, :], True, False)
-        for half in range(2):
-            for r in range(TURNED):
-                picked = ring.tile([P, HALF], F32, name="picked", bufs=2 * TURNED)
-                nc.vector.tensor_copy(picked[:], y[:].indirect(entries(lists[r], half * HALF, (half + 1) * HALF)))
-                flat_t = bank("AE"[r])
-                for j in range(per_half):
-                    nc.tensor.transpose(flat_t[:, j * P : (j + 1) * P], picked[:, j * P : (j + 1) * P], ident[:])
-                for j in range(per_half):
-                    block = half * per_half + j
-                    if (half, r, j) == (0, TURNED - 1, per_half - 1):
-                        scaled = keep.tile([P, N], F32, name="closing")
-                    else:
-                        scaled = ring.tile([P, N], F32, name="scaled", bufs=2 * per_half)
-                    col = r * BLOCKS + block
-                    nc.scalar.activation(
-                        out=scaled[:], in_=flat_t[:, j * P : (j + 1) * P], func=COPY, scale=gate_t[:, col : col + 1]
-                    )
-                    add_turned(sums[block], scaled[:], False, r == TURNED - 1)
+        steps = [(half, r) for half in range(2) for r in range(TURNED)]
+        scaled = {}
+
+        def turn_picked(half, r):
+            picked = ring.tile([P, HALF], F32, name="picked", bufs=2 * TURNED)
+            nc.vector.tensor_copy(picked[:], y[:].indirect(entries(lists[r], half * HALF, (half + 1) * HALF)))
+            flat_t = bank("AE"[r])
+            for j in range(per_half):
+                nc.tensor.transpose(flat_t[:, j * P : (j + 1) * P], picked[:, j * P : (j + 1) * P], ident[:])
+            for j in range(per_half):
+                block = half * per_half + j
+                closing = (half, r, j) == (0, TURNED - 1, per_half - 1)
+                tile = keep.tile([P, N], F32, name="closing" if closing else "scaled%d_%d" % (block, r))
+                col = r * BLOCKS + block
+                nc.scalar.activation(
+                    out=tile[:], in_=flat_t[:, j * P : (j + 1) * P], func=COPY, scale=gate_t[:, col : col + 1]
+                )
+                scaled[block, r] = tile
+
+        def add_scaled(half, r):
+            for block in range(half * per_half, (half + 1) * per_half):
+                add_turned(sums[block], scaled[block, r][:], False, r == TURNED - 1)
+
+        turn_picked(*steps[0])
+        for k in range(len(steps)):
+            if k + 1 < len(steps):
+                turn_picked(*steps[k + 1])
+            add_scaled(*steps[k])
+
         runs = [(0, per_half), (per_half, BLOCKS - 1), (BLOCKS - 1, BLOCKS)]
         thirds = []
 

@@ -27,7 +27,7 @@ BLOCKS = T // P
 HALF = T // 2
 TURNED = TOP - 1
 
-CHUNKS = [(0, 1)] + [(e, e + 2) for e in range(1, E, 2)]
+CHUNKS = [(0, 1), (1, 3), (3, 5), (5, 7), (7, 8), (8, 9)]
 VECTOR_ROUNDS = [(8, 1)]
 VECTOR_TURNED = [7]
 VECTOR_Y = [4, 8]
@@ -55,7 +55,7 @@ def tile_moe_adp_none_kernel(
                 )
 
         def shift_second_pass(dst, src, queue):
-            queue.dma_start(out=dst[0:112, :].bitcast(I32), in_=src[4:116, :].bitcast(I32))
+            queue.dma_start(out=dst[0:112, :].bitcast(I32), in_=src[16:128, :].bitcast(I32))
 
         def entries(offsets, lo, hi):
             return offsets[:, lo // PER_COLUMN : hi // PER_COLUMN]
@@ -108,7 +108,8 @@ def tile_moe_adp_none_kernel(
         nc.gpsimd.memset(xs[:].bitcast(I32), 0)
         for q in range(4):
             (nc.sync, nc.scalar)[q // 2].dma_start(
-                out=xs[32 * q : 32 * q + 8, :].bitcast(I32), in_=x_scales[:, 4 * q : 4 * q + 4, :].bitcast(I32)
+                out=xs[q:P:16, :].bitcast(I32),
+                in_=x_scales[:, q:16:4, :].rearrange("s g t -> g s t").bitcast(I32),
             )
         nc.sync.dma_start(out=xw_all[:], in_=x_words.rearrange("s p t d -> p s (t d)").bitcast(I32))
         load_was(0, [1, 3])
@@ -163,6 +164,9 @@ def tile_moe_adp_none_kernel(
         gather_words(4)
         gather_scales(4)
         load_scale_rows(ws, w_scales)
+        gather_words(5)
+        gather_words(6)
+        gather_scales(5)
         wbw = keep.tile([P, E, 2 * N], U8, name="wbw", align_bytes=64)
         nc.sync.dma_start(out=wbw[:].bitcast(I32), in_=wb_words.rearrange("e o p n -> p (e o) n").bitcast(I32))
         load_scale_rows(wbs, wb_scales.rearrange("e o b n -> (e o) b n"))
@@ -173,8 +177,6 @@ def tile_moe_adp_none_kernel(
         )
         gate_last = keep.tile([P, T], F32, name="gate_last")
         nc.sync.dma_start(out=gate_last[:], in_=gate[TOP - 1])
-        gather_words(5)
-        gather_words(6)
         gather_words(7)
         gather_words(8)
 

@@ -28,10 +28,11 @@ HALF = T // 2
 TURNED = TOP - 1
 
 CHUNKS = [(0, 1), (1, 3), (3, 5), (5, 7), (7, 8), (8, 9)]
-VECTOR_ROUNDS = [(8, 1)]
-VECTOR_TURNED = [7]
-VECTOR_Y = [4, 8]
-SCALE_GROUPS = [(0, 7), (7, 18)]
+VECTOR_ROUNDS = []
+DIRECT = 6
+VECTOR_Y = [0, 2]
+EARLY_Q = 9
+SCALE_GROUPS = [(0, 2), (2, 9), (9, 18)]
 
 
 def tile_moe_adp_none_kernel(
@@ -67,7 +68,11 @@ def tile_moe_adp_none_kernel(
                 nc.scalar.copy(out=dst, in_=src)
 
         def bank(letter):
-            return psum.tile([P, BANK], F32, name="bank" + letter)
+            return psum.tile([P, BANK], F32, name="bank" + letter)[:]
+
+        def pair(letter):
+            tile = psum.tile([P, 2, BANK], F32, name="pair" + letter)
+            return [tile[:, 0, :], tile[:, 1, :]]
 
         xw_all = keep.tile([P, PASSES, T], I32, name="xw", align_bytes=64)
         xw = [xw_all[:, s, :] for s in range(PASSES)]
@@ -79,8 +84,8 @@ def tile_moe_adp_none_kernel(
             count = len(passes)
             name = "waw%d_%d" % (first, passes[0])
             tile = keep.tile([P, (last - first) * count, 2 * H], U8, name=name, align_bytes=64)
-            rows = wa_words[first:last, passes[0] : passes[0] + count]
-            nc.sync.dma_start(out=tile[:].bitcast(I32), in_=rows.rearrange("e s p n -> p (e s) n").bitcast(I32))
+            rows = wa_words.bitcast(I32)[first:last, passes[0] : passes[0] + count]
+            nc.sync.dma_start(out=tile[:].bitcast(I32), in_=rows.rearrange("e s p n -> p (e s) n"))
             for e in range(first, last):
                 for s in passes:
                     waw[e, s] = tile[:, (e - first) * count + s - passes[0], :]
@@ -94,6 +99,9 @@ def tile_moe_adp_none_kernel(
             first, last = SCALE_GROUPS[group]
             load_scale_rows(was[first], wa_rows[first:last], quarters, queue)
 
+        def pass_order(e):
+            return (0, 1) if e < 2 else (1, 0)
+
         lists = []
 
         def load_list(pos):
@@ -103,7 +111,7 @@ def tile_moe_adp_none_kernel(
 
         offs_sb = keep.tile([P, SLOTS // PER_COLUMN], U16, name="offs_sb")
         nc.sync.dma_start(offs_sb[:], offs)
-        load_was(0, [0, 2], nc.scalar)
+        load_was(1, [0, 2], nc.scalar)
         xs = plane_tile(T, "xs")
         nc.gpsimd.memset(xs[:].bitcast(I32), 0)
         for q in range(4):
@@ -112,9 +120,11 @@ def tile_moe_adp_none_kernel(
                 in_=x_scales[:, q:16:4, :].rearrange("s g t -> g s t").bitcast(I32),
             )
         nc.sync.dma_start(out=xw_all[:], in_=x_words.rearrange("s p t d -> p s (t d)").bitcast(I32))
-        load_was(0, [1, 3])
+        load_was(0, [0, 1], nc.scalar)
         load_wa(0, 1)
+        load_was(0, [2, 3])
         load_wa(1, 2)
+        load_was(1, [1, 3])
 
         slot_s1 = plane_tile(SLOTS, "slot_s1")
         wbs = plane_tile(E * N, "wbs")
@@ -126,139 +136,178 @@ def tile_moe_adp_none_kernel(
         gate_rows = keep.tile([P, P], F32, name="gate_rows")
         nc.gpsimd.memset(gate_rows[:], 0.0)
 
+        nc.gpsimd.memset(was[PASSES * DIRECT].bitcast(I32), 0)
         slot_s0, words = {}, {}
 
-        def gather_scales(c):
-            first, last = CHUNKS[c]
-            tile = plane_tile((last - first) * C, "slot_s0_%d" % c)
-            nc.vector.tensor_copy(tile[:], xs[:].indirect(entries(offs_sb, first * C, last * C)))
+        scale_tiles = {}
+
+        def gather_scales(first, last):
+            c = [k for k, (lo, hi) in enumerate(CHUNKS) if lo <= first < hi][0]
+            lo, hi = CHUNKS[c]
+            if c not in scale_tiles:
+                scale_tiles[c] = plane_tile((hi - lo) * C, "slot_s0_%d" % c)
+            tile = scale_tiles[c]
+            nc.vector.tensor_copy(
+                tile[:, (first - lo) * C : (last - lo) * C], xs[:].indirect(entries(offs_sb, first * C, last * C))
+            )
             for e in range(first, last):
-                slot_s0[e] = tile[:, (e - first) * C : (e - first + 1) * C]
-            shift_second_pass(slot_s1[:, first * C : last * C], tile[:], nc.sync if c else nc.scalar)
+                slot_s0[e] = tile[:, (e - lo) * C : (e - lo + 1) * C]
+            if last == hi:
+                shift_second_pass(slot_s1[:, lo * C : hi * C], tile[:], nc.sync if c else nc.scalar)
 
         def gather_words(e):
-            for s in range(PASSES):
+            for s in pass_order(e):
                 tile = keep.tile([P, C], I32, name="slot_w%d_%d" % (e, s), align_bytes=64)
                 nc.vector.tensor_copy(
                     tile[:].bitcast(U32), xw[s].bitcast(U32).indirect(entries(offs_sb, e * C, (e + 1) * C))
                 )
                 words[e, s] = tile
 
-        gather_scales(0)
-        load_was(1)
-        gather_scales(1)
+        gather_scales(0, 1)
+        gather_scales(1, 3)
         load_wa(2, 3)
-        load_wa(3, 5, [1])
+        load_was(2)
+        load_wa(3, 5)
         gather_words(0)
-        gather_scales(2)
-        load_wa(3, 5, [0])
-        load_wa(5, 7)
-        ww = keep.tile([P, PASSES, 2 * N], U8, name="ww", align_bytes=64)
-        nc.sync.dma_start(out=ww[:].bitcast(I32), in_=w_words.rearrange("s p n -> p s n").bitcast(I32))
-        shift_second_pass(xs1[:], xs[:], nc.sync)
+        gather_scales(3, 5)
+        load_wa(DIRECT, E)
+        load_wa(5, 6)
         gather_words(1)
         gather_words(2)
-        gather_scales(3)
-        load_wa(7, 9)
-        gather_words(3)
-        gather_words(4)
-        gather_scales(4)
-        load_scale_rows(ws, w_scales)
-        gather_words(5)
-        gather_words(6)
-        gather_scales(5)
-        wbw = keep.tile([P, E, 2 * N], U8, name="wbw", align_bytes=64)
-        nc.sync.dma_start(out=wbw[:].bitcast(I32), in_=wb_words.rearrange("e o p n -> p (e o) n").bitcast(I32))
-        load_scale_rows(wbs, wb_scales.rearrange("e o b n -> (e o) b n"))
+        gather_scales(5, 7)
         for pos in (pos1, pos2, pos3):
             load_list(pos)
         nc.sync.dma_start(
             out=gate_rows[0 : TURNED * BLOCKS, :], in_=gate[0:TURNED, 0, :].rearrange("r (b t) -> r b t", t=P)
         )
+        ww = keep.tile([P, PASSES, 2 * N], U8, name="ww", align_bytes=64)
+        nc.sync.dma_start(out=ww[:].bitcast(I32), in_=w_words.rearrange("s p n -> p s n").bitcast(I32))
+        gather_words(3)
+        gather_words(4)
+        gather_scales(7, 8)
+        shift_second_pass(xs1[:], xs[:], nc.sync)
+        wbw = keep.tile([P, E, 2 * N], U8, name="wbw", align_bytes=64)
+        nc.sync.dma_start(out=wbw[:].bitcast(I32), in_=wb_words.rearrange("e o p n -> p (e o) n").bitcast(I32))
+        wb_rows = wb_scales.rearrange("e o b n -> (e o) b n")
+        load_scale_rows(ws, w_scales, [0, 1, 2])
+        load_scale_rows(wbs, wb_rows, [0, 1])
+        gather_words(5)
+        gather_words(6)
+        gather_scales(8, 9)
+        load_scale_rows(wbs, wb_rows, [2, 3])
         gate_last = keep.tile([P, T], F32, name="gate_last")
         nc.sync.dma_start(out=gate_last[:], in_=gate[TOP - 1])
+        load_scale_rows(ws, w_scales, [3])
         gather_words(7)
         gather_words(8)
 
-        rounded = {}
-        h_w = keep.tile([P, SLOTS], U32, name="h_w", align_bytes=64)
+        rounded, turned_in, codes, spread = {}, {}, {}, {}
         h_s = keep.tile([P, SLOTS], U8, name="h_s", align_bytes=64)
 
-        def first_product(e, letters, passes_first=False):
+        def first_product(e, banks):
             h_bf = keep.tile([P, 2, H], BF16, name="h_bf%d" % e)
-            banks = [bank(letter) for letter in letters]
-            order = [(b, s) for b in range(2) for s in range(PASSES)]
-            for b, s in sorted(order, key=lambda bs: bs[1]) if passes_first else order:
-                slot = e * C + b * P
-                planes = (slot_s0[e][:, b * P : (b + 1) * P], slot_s1[:, slot : slot + P])
-                nc.tensor.matmul_mx(
-                    out=banks[b][:],
-                    lhsT=words[e, s][:, b * P : (b + 1) * P].bitcast(FP8X4),
-                    lhsT_scale=planes[s],
-                    rhs=waw[e, s].bitcast(FP4X4),
-                    rhs_scale=was[e * PASSES + s][:, 0:H],
-                    start=(s == 0),
-                    stop=(s == PASSES - 1),
-                )
+            for k, s in enumerate(pass_order(e)):
+                for b in range(2):
+                    slot = e * C + b * P
+                    planes = (slot_s0[e][:, b * P : (b + 1) * P], slot_s1[:, slot : slot + P])
+                    nc.tensor.matmul_mx(
+                        out=banks[b],
+                        lhsT=words[e, s][:, b * P : (b + 1) * P].bitcast(FP8X4),
+                        lhsT_scale=planes[s],
+                        rhs=waw[e, s].bitcast(FP4X4),
+                        rhs_scale=was[e * PASSES + s][:, 0:H],
+                        start=(k == 0),
+                        stop=(k == PASSES - 1),
+                    )
             for b in range(2):
                 dst = h_bf[:, b, :].rearrange("p (u m d) -> p u m d", u=2, d=2)
-                src = banks[b][:].rearrange("p (m u d) -> p u m d", u=2, d=2)
+                src = banks[b].rearrange("p (m u d) -> p u m d", u=2, d=2)
                 if (e, b) in VECTOR_ROUNDS:
                     nc.vector.tensor_copy(out=dst, in_=src)
                 else:
                     nc.scalar.activation(out=dst, in_=src, func=COPY)
             rounded[e] = h_bf
 
-        def turn(e, letter):
-            turned = bank(letter)[:].rearrange("p (b u j) -> p b u j", b=2, u=2)
+        def spread_columns(e):
+            for s in pass_order(e):
+                tile = keep.tile([P, 4, P], U16, name="wa_by_d%d_%d" % (e, s), align_bytes=64)
+                nc.gpsimd.tensor_copy(out=tile[:], in_=waw[e, s].bitcast(U16).rearrange("p (m d) -> p d m", d=4))
+                plane = keep.tile([P, 4, P], U8, name="was_by_d%d_%d" % (e, s), align_bytes=64)
+                nc.gpsimd.tensor_copy(
+                    out=plane[:], in_=was[e * PASSES + s][:, 0:H].rearrange("p (m d) -> p d m", d=4)
+                )
+                spread[e, s] = (tile, plane)
+
+        def direct_product(e, banks):
+            h_in = keep.tile([P, 4 * C], BF16, name="h_in%d" % e, align_bytes=64)
+            for k, s in enumerate(pass_order(e)):
+                tile, plane = spread[e, s]
+                for b in range(2):
+                    slot = e * C + b * P
+                    planes = (slot_s0[e][:, b * P : (b + 1) * P], slot_s1[:, slot : slot + P])
+                    for d in range(4):
+                        nc.tensor.matmul_mx(
+                            out=banks[b][:, d * P : (d + 1) * P],
+                            lhsT=tile[:, d, :].bitcast(U8).bitcast(FP4X4),
+                            lhsT_scale=plane[:, d, :],
+                            rhs=words[e, s][:, b * P : (b + 1) * P].bitcast(FP8X4),
+                            rhs_scale=planes[s],
+                            start=(k == 0 and d == 0),
+                            stop=(k == PASSES - 1 and d == 3),
+                        )
+            for b in range(2):
+                dst = h_in[:, b * 4 * P : (b + 1) * 4 * P].rearrange("p (j d) -> p j d", d=4)
+                src = banks[b].rearrange("p (d j) -> p j d", d=4)
+                if (e, b) in VECTOR_ROUNDS:
+                    nc.vector.tensor_copy(out=dst, in_=src)
+                else:
+                    nc.scalar.activation(out=dst, in_=src, func=COPY)
+            turned_in[e] = h_in
+
+        def turn(e, target):
+            turned = target.rearrange("p (b u j) -> p b u j", b=2, u=2)
             pairs = rounded[e][:].bitcast(F32)
             for b in range(2):
                 for u in range(2):
                     nc.tensor.transpose(turned[:, b, u, :], pairs[:, b, u * P : (u + 1) * P], ident[:])
             h_in = keep.tile([P, 4 * C], BF16, name="h_in%d" % e, align_bytes=64)
-            copy_out(
-                e in VECTOR_TURNED,
-                h_in[:].bitcast(F32).rearrange("p (b j u) -> p b j u", b=2, u=2),
-                turned.rearrange("p b u j -> p b j u"),
+            nc.scalar.copy(
+                out=h_in[:].bitcast(F32).rearrange("p (b j u) -> p b j u", b=2, u=2),
+                in_=turned.rearrange("p b u j -> p b j u"),
             )
-            cols = slice(e * C, (e + 1) * C)
-            nc.vector.quantize_mx(out=h_w[:, cols].bitcast(FP8X4), scales=h_s[:, cols], in_=h_in[:])
+            turned_in[e] = h_in
 
-        def turn_blocks(e, letters):
-            pairs = rounded[e][:].bitcast(F32)
-            for b in range(2):
-                turned = bank(letters[b])[:, 0 : 2 * P].rearrange("p (u j) -> p u j", u=2)
-                for u in range(2):
-                    nc.tensor.transpose(turned[:, u, :], pairs[:, b, u * P : (u + 1) * P], ident[:])
-                h_in = keep.tile([P, 4 * P], BF16, name="h_in%d_%d" % (e, b), align_bytes=64)
-                copy_out(
-                    b == 1,
-                    h_in[:].bitcast(F32).rearrange("p (j u) -> p j u", u=2),
-                    turned.rearrange("p u j -> p j u"),
-                )
-                cols = slice(e * C + b * P, e * C + (b + 1) * P)
-                nc.vector.quantize_mx(out=h_w[:, cols].bitcast(FP8X4), scales=h_s[:, cols], in_=h_in[:])
-
-        def second_product(first, last, letter):
-            y_bank = bank(letter)
+        def quantize(first, last, name):
+            tile = keep.tile([P, (last - first) * C], I32, name=name, align_bytes=64)
             for e in range(first, last):
-                cols = slice(e * C, (e + 1) * C)
+                codes[e] = tile[:, (e - first) * C : (e - first + 1) * C]
+
+        def quantize_slots(first, last):
+            e = first // C
+            cols = slice(first - e * C, last - e * C)
+            nc.vector.quantize_mx(
+                out=codes[e][:, cols].bitcast(FP8X4),
+                scales=h_s[:, first:last],
+                in_=turned_in[e][:, 4 * cols.start : 4 * cols.stop],
+            )
+
+        def second_product(first, last, y_bank, on_vector):
+            for lo in range(first, last, C):
+                e, hi = lo // C, min(lo + C, last)
                 nc.tensor.matmul_mx(
-                    out=y_bank[:, (e - first) * C : (e - first + 1) * C],
+                    out=y_bank[:, lo - first : hi - first],
                     lhsT=wbw[:, e, :].bitcast(FP4X4),
                     lhsT_scale=wbs[:, e * N : (e + 1) * N],
-                    rhs=h_w[:, cols].bitcast(FP8X4),
-                    rhs_scale=h_s[:, cols],
+                    rhs=codes[e][:, lo - e * C : hi - e * C].bitcast(FP8X4),
+                    rhs_scale=h_s[:, lo:hi],
                     start=True,
                     stop=True,
                 )
-            copy_out(first in VECTOR_Y, y[:, first * C : last * C], y_bank[:, 0 : (last - first) * C])
+            copy_out(on_vector, y[:, first:last], y_bank[:, 0 : last - first])
 
         per_half = HALF // P
-        base_t = keep.tile([P, BLOCKS, N], F32, name="base_t")
 
-        def frozen_layer(half, letter):
-            acc = bank(letter)
+        def frozen_layer(half, acc):
             for j in range(per_half):
                 cols = slice(half * HALF + j * P, half * HALF + (j + 1) * P)
                 for s in range(PASSES):
@@ -271,37 +320,45 @@ def tile_moe_adp_none_kernel(
                         start=(s == 0),
                         stop=(s == PASSES - 1),
                     )
+            return acc
+
+        for e in range(DIRECT, E):
+            spread_columns(e)
+        first_product(0, pair("A"))
+        first_product(1, [bank("C"), bank("D")])
+        first_product(2, pair("B"))
+        turn(0, bank("C"))
+        turn(1, bank("D"))
+        first_product(3, [bank("E"), bank("F")])
+        first_product(4, pair("A"))
+        turn(2, bank("E"))
+        turn(3, bank("F"))
+        first_product(5, [bank("C"), bank("D")])
+        direct_product(6, pair("B"))
+        turn(4, bank("C"))
+        turn(5, bank("D"))
+        direct_product(7, pair("A"))
+        direct_product(8, [bank("E"), bank("F")])
+        quantize(0, EARLY_Q, "h_w")
+        last = (E - 1) * C
+        for e in range(E - 1):
+            quantize_slots(e * C, (e + 1) * C)
+        for b in range(2):
+            quantize_slots(last + b * P, last + (b + 1) * P)
+        scalar_banks = pair("B")
+        y_banks = [bank("C"), scalar_banks[0], bank("D"), scalar_banks[1]]
+        for k in range(4):
+            second_product(2 * k * C, (2 * k + 2) * C, y_banks[k], k in VECTOR_Y)
+        for b, target in enumerate(pair("A")):
+            second_product(last + b * P, last + (b + 1) * P, target, True)
+        base_sums = [frozen_layer(half, bank("EF"[half])) for half in range(2)]
+        base_t = keep.tile([P, BLOCKS, N], F32, name="base_t")
+        for half in range(2):
             nc.scalar.copy(
                 out=base_t[:, half * per_half : (half + 1) * per_half, :],
-                in_=acc[:, 0 : per_half * N].rearrange("p (j n) -> p j n", j=per_half),
+                in_=base_sums[half][:, 0 : per_half * N].rearrange("p (j n) -> p j n", j=per_half),
             )
-
-        first_product(0, "GH", True)
-        first_product(1, "AB")
-        first_product(2, "CD")
-        turn(0, "A")
-        turn(1, "B")
-        first_product(3, "CD")
-        first_product(4, "AB")
-        turn(2, "C")
-        turn(3, "D")
-        first_product(5, "AB")
-        first_product(6, "CD")
-        turn(4, "A")
-        turn(5, "B")
-        first_product(7, "CD")
-        first_product(8, "AB")
-        turn(6, "C")
-        turn(7, "D")
-        turn(8, "A")
-        second_product(0, 2, "B")
-        second_product(2, 4, "C")
-        second_product(4, 6, "D")
-        second_product(6, 8, "A")
-        second_product(8, 9, "E")
-        frozen_layer(0, "B")
-        frozen_layer(1, "C")
-        gate_ps = bank("H")
+        gate_ps = bank("D")
         nc.tensor.transpose(gate_ps[:, 0:P], gate_rows[:], ident[:])
         gate_t = keep.tile([P, TURNED * BLOCKS], F32, name="gate_t")
         nc.scalar.copy(out=gate_t[:], in_=gate_ps[:, 0 : TURNED * BLOCKS])
@@ -309,9 +366,8 @@ def tile_moe_adp_none_kernel(
         def add_turned(total, tile_t, start, stop):
             nc.tensor.matmul(total[:, 0:P], lhsT=tile_t, rhs=ident[:], is_transpose=True, start=start, stop=stop)
 
-        sums = []
+        sums = pair("B") + [bank("E")] + pair("A") + [bank("F")]
         for block in range(BLOCKS):
-            sums.append(bank("FGHDBC"[block]))
             add_turned(sums[block], base_t[:, block, :], True, False)
         steps = [(half, r) for half in range(2) for r in range(TURNED)]
         scaled = {}
@@ -319,7 +375,7 @@ def tile_moe_adp_none_kernel(
         def turn_picked(half, r):
             picked = ring.tile([P, HALF], F32, name="picked", bufs=2 * TURNED)
             nc.vector.tensor_copy(picked[:], y[:].indirect(entries(lists[r], half * HALF, (half + 1) * HALF)))
-            flat_t = bank("AE"[r])
+            flat_t = bank("CD"[r])
             for j in range(per_half):
                 nc.tensor.transpose(flat_t[:, j * P : (j + 1) * P], picked[:, j * P : (j + 1) * P], ident[:])
             for j in range(per_half):

@@ -29,10 +29,10 @@ TURNED = TOP - 1
 
 CHUNKS = [(0, 1), (1, 3), (3, 5), (5, 7), (7, 8), (8, 9)]
 VECTOR_ROUNDS = []
-DIRECT = 6
+DIRECT = 5
 VECTOR_Y = [0, 2]
 EARLY_Q = 9
-SCALE_GROUPS = [(0, 2), (2, 9), (9, 18)]
+SCALE_GROUPS = [(0, 3), (3, 10)]
 
 
 def tile_moe_adp_none_kernel(
@@ -71,8 +71,7 @@ def tile_moe_adp_none_kernel(
             return psum.tile([P, BANK], F32, name="bank" + letter)[:]
 
         def pair(letter):
-            tile = psum.tile([P, 2, BANK], F32, name="pair" + letter)
-            return [tile[:, 0, :], tile[:, 1, :]]
+            return [bank(letter + "0"), bank(letter + "1")]
 
         xw_all = keep.tile([P, PASSES, T], I32, name="xw", align_bytes=64)
         xw = [xw_all[:, s, :] for s in range(PASSES)]
@@ -100,7 +99,7 @@ def tile_moe_adp_none_kernel(
             load_scale_rows(was[first], wa_rows[first:last], quarters, queue)
 
         def pass_order(e):
-            return (0, 1) if e < 2 else (1, 0)
+            return (0, 1) if e in (0, 1, E - 1) else (1, 0)
 
         lists = []
 
@@ -123,7 +122,7 @@ def tile_moe_adp_none_kernel(
         load_was(0, [0, 1], nc.scalar)
         load_wa(0, 1)
         load_was(0, [2, 3])
-        load_wa(1, 2)
+        load_wa(1, 3)
         load_was(1, [1, 3])
 
         slot_s1 = plane_tile(SLOTS, "slot_s1")
@@ -133,10 +132,7 @@ def tile_moe_adp_none_kernel(
         y = keep.tile([P, SLOTS], F32, name="y")
         ident = keep.tile([P, P], F32, name="ident")
         make_identity(nc, ident[:])
-        gate_rows = keep.tile([P, P], F32, name="gate_rows")
-        nc.gpsimd.memset(gate_rows[:], 0.0)
 
-        nc.gpsimd.memset(was[PASSES * DIRECT].bitcast(I32), 0)
         slot_s0, words = {}, {}
 
         scale_tiles = {}
@@ -165,26 +161,38 @@ def tile_moe_adp_none_kernel(
 
         gather_scales(0, 1)
         gather_scales(1, 3)
-        load_wa(2, 3)
-        load_was(2)
         load_wa(3, 5)
+        stacked = plane_tile(H, "stacked")
+        direct_rows = wa_rows[PASSES * DIRECT : PASSES * E]
+        for g in range(4):
+            nc.sync.dma_start(
+                out=stacked[32 * g : 32 * (g + 1), :].bitcast(I32),
+                in_=direct_rows[:, 4 * g : 4 * (g + 1), :].bitcast(I32),
+            )
         gather_words(0)
         gather_scales(3, 5)
-        load_wa(DIRECT, E)
-        load_wa(5, 6)
+        load_wa(DIRECT, DIRECT + 2)
+        load_wa(DIRECT + 2, E)
+        load_list(pos1)
+        stacked_by_d = plane_tile(H, "stacked_by_d")
+        nc.gpsimd.tensor_copy(
+            out=stacked_by_d[:].rearrange("p (d m) -> p d m", d=4), in_=stacked[:].rearrange("p (m d) -> p d m", d=4)
+        )
+        direct_planes = keep.tile([P, PASSES * (E - DIRECT), H], U8, name="direct_planes", align_bytes=64)
+        for q in range(4):
+            nc.sync.dma_start(
+                out=direct_planes[q:P:32, :, :].bitcast(I32), in_=stacked_by_d[q:P:4, :].bitcast(I32)
+            )
         gather_words(1)
         gather_words(2)
         gather_scales(5, 7)
-        for pos in (pos1, pos2, pos3):
+        for pos in (pos2, pos3):
             load_list(pos)
-        nc.sync.dma_start(
-            out=gate_rows[0 : TURNED * BLOCKS, :], in_=gate[0:TURNED, 0, :].rearrange("r (b t) -> r b t", t=P)
-        )
-        ww = keep.tile([P, PASSES, 2 * N], U8, name="ww", align_bytes=64)
-        nc.sync.dma_start(out=ww[:].bitcast(I32), in_=w_words.rearrange("s p n -> p s n").bitcast(I32))
         gather_words(3)
         gather_words(4)
         gather_scales(7, 8)
+        ww = keep.tile([P, PASSES, 2 * N], U8, name="ww", align_bytes=64)
+        nc.sync.dma_start(out=ww[:].bitcast(I32), in_=w_words.rearrange("s p n -> p s n").bitcast(I32))
         shift_second_pass(xs1[:], xs[:], nc.sync)
         wbw = keep.tile([P, E, 2 * N], U8, name="wbw", align_bytes=64)
         nc.sync.dma_start(out=wbw[:].bitcast(I32), in_=wb_words.rearrange("e o p n -> p (e o) n").bitcast(I32))
@@ -195,14 +203,13 @@ def tile_moe_adp_none_kernel(
         gather_words(6)
         gather_scales(8, 9)
         load_scale_rows(wbs, wb_rows, [2, 3])
-        gate_last = keep.tile([P, T], F32, name="gate_last")
-        nc.sync.dma_start(out=gate_last[:], in_=gate[TOP - 1])
         load_scale_rows(ws, w_scales, [3])
+        gates = keep.tile([P, TOP, T], F32, name="gates")
+        nc.sync.dma_start(out=gates[:], in_=gate.rearrange("r p t -> p r t"))
         gather_words(7)
         gather_words(8)
 
         rounded, turned_in, codes, spread = {}, {}, {}, {}
-        h_s = keep.tile([P, SLOTS], U8, name="h_s", align_bytes=64)
 
         def first_product(e, banks):
             h_bf = keep.tile([P, 2, H], BF16, name="h_bf%d" % e)
@@ -232,11 +239,7 @@ def tile_moe_adp_none_kernel(
             for s in pass_order(e):
                 tile = keep.tile([P, 4, P], U16, name="wa_by_d%d_%d" % (e, s), align_bytes=64)
                 nc.gpsimd.tensor_copy(out=tile[:], in_=waw[e, s].bitcast(U16).rearrange("p (m d) -> p d m", d=4))
-                plane = keep.tile([P, 4, P], U8, name="was_by_d%d_%d" % (e, s), align_bytes=64)
-                nc.gpsimd.tensor_copy(
-                    out=plane[:], in_=was[e * PASSES + s][:, 0:H].rearrange("p (m d) -> p d m", d=4)
-                )
-                spread[e, s] = (tile, plane)
+                spread[e, s] = (tile, direct_planes[:, (e - DIRECT) * PASSES + s, :])
 
         def direct_product(e, banks):
             h_in = keep.tile([P, 4 * C], BF16, name="h_in%d" % e, align_bytes=64)
@@ -249,7 +252,7 @@ def tile_moe_adp_none_kernel(
                         nc.tensor.matmul_mx(
                             out=banks[b][:, d * P : (d + 1) * P],
                             lhsT=tile[:, d, :].bitcast(U8).bitcast(FP4X4),
-                            lhsT_scale=plane[:, d, :],
+                            lhsT_scale=plane[:, d * P : (d + 1) * P],
                             rhs=words[e, s][:, b * P : (b + 1) * P].bitcast(FP8X4),
                             rhs_scale=planes[s],
                             start=(k == 0 and d == 0),
@@ -277,29 +280,27 @@ def tile_moe_adp_none_kernel(
             )
             turned_in[e] = h_in
 
-        def quantize(first, last, name):
-            tile = keep.tile([P, (last - first) * C], I32, name=name, align_bytes=64)
-            for e in range(first, last):
-                codes[e] = tile[:, (e - first) * C : (e - first + 1) * C]
-
         def quantize_slots(first, last):
             e = first // C
-            cols = slice(first - e * C, last - e * C)
+            h_w = keep.tile([P, last - first], I32, name="h_w%d" % first, align_bytes=64)
+            h_s = plane_tile(last - first, "h_s%d" % first)
             nc.vector.quantize_mx(
-                out=codes[e][:, cols].bitcast(FP8X4),
-                scales=h_s[:, first:last],
-                in_=turned_in[e][:, 4 * cols.start : 4 * cols.stop],
+                out=h_w[:].bitcast(FP8X4),
+                scales=h_s[:],
+                in_=turned_in[e][:, 4 * (first - e * C) : 4 * (last - e * C)],
             )
+            codes[first] = (h_w, h_s)
 
         def second_product(first, last, y_bank, on_vector):
             for lo in range(first, last, C):
                 e, hi = lo // C, min(lo + C, last)
+                h_w, h_s = codes[lo]
                 nc.tensor.matmul_mx(
                     out=y_bank[:, lo - first : hi - first],
                     lhsT=wbw[:, e, :].bitcast(FP4X4),
                     lhsT_scale=wbs[:, e * N : (e + 1) * N],
-                    rhs=codes[e][:, lo - e * C : hi - e * C].bitcast(FP8X4),
-                    rhs_scale=h_s[:, lo:hi],
+                    rhs=h_w[:].bitcast(FP8X4),
+                    rhs_scale=h_s[:],
                     start=True,
                     stop=True,
                 )
@@ -307,20 +308,23 @@ def tile_moe_adp_none_kernel(
 
         per_half = HALF // P
 
-        def frozen_layer(half, acc):
-            for j in range(per_half):
-                cols = slice(half * HALF + j * P, half * HALF + (j + 1) * P)
+        base = keep.tile([P, T], F32, name="base")
+
+        def frozen_layer(first, last, acc):
+            width = BANK if last - first == BANK else P
+            for lo in range(first, last, width):
+                cols = slice(lo, lo + width)
                 for s in range(PASSES):
                     nc.tensor.matmul_mx(
-                        out=acc[:, j * N : (j + 1) * N],
-                        lhsT=xw[s][:, cols].bitcast(FP8X4),
-                        lhsT_scale=(xs, xs1)[s][:, cols],
-                        rhs=ww[:, s, :].bitcast(FP4X4),
-                        rhs_scale=ws[:, s * N : (s + 1) * N],
+                        out=acc[:, lo - first : lo - first + width],
+                        lhsT=ww[:, s, :].bitcast(FP4X4),
+                        lhsT_scale=ws[:, s * N : (s + 1) * N],
+                        rhs=xw[s][:, cols].bitcast(FP8X4),
+                        rhs_scale=(xs, xs1)[s][:, cols],
                         start=(s == 0),
                         stop=(s == PASSES - 1),
                     )
-            return acc
+            nc.scalar.copy(out=base[:, first:last], in_=acc[:, 0 : last - first])
 
         for e in range(DIRECT, E):
             spread_columns(e)
@@ -333,13 +337,11 @@ def tile_moe_adp_none_kernel(
         first_product(4, pair("A"))
         turn(2, bank("E"))
         turn(3, bank("F"))
-        first_product(5, [bank("C"), bank("D")])
-        direct_product(6, pair("B"))
+        direct_product(5, [bank("C"), bank("D")])
+        direct_product(6, [bank("E"), bank("F")])
         turn(4, bank("C"))
-        turn(5, bank("D"))
         direct_product(7, pair("A"))
-        direct_product(8, [bank("E"), bank("F")])
-        quantize(0, EARLY_Q, "h_w")
+        direct_product(8, [bank("D"), bank("E")])
         last = (E - 1) * C
         for e in range(E - 1):
             quantize_slots(e * C, (e + 1) * C)
@@ -351,74 +353,44 @@ def tile_moe_adp_none_kernel(
             second_product(2 * k * C, (2 * k + 2) * C, y_banks[k], k in VECTOR_Y)
         for b, target in enumerate(pair("A")):
             second_product(last + b * P, last + (b + 1) * P, target, True)
-        base_sums = [frozen_layer(half, bank("EF"[half])) for half in range(2)]
-        base_t = keep.tile([P, BLOCKS, N], F32, name="base_t")
-        for half in range(2):
-            nc.scalar.copy(
-                out=base_t[:, half * per_half : (half + 1) * per_half, :],
-                in_=base_sums[half][:, 0 : per_half * N].rearrange("p (j n) -> p j n", j=per_half),
-            )
-        gate_ps = bank("D")
-        nc.tensor.transpose(gate_ps[:, 0:P], gate_rows[:], ident[:])
-        gate_t = keep.tile([P, TURNED * BLOCKS], F32, name="gate_t")
-        nc.scalar.copy(out=gate_t[:], in_=gate_ps[:, 0 : TURNED * BLOCKS])
+        frozen_layer(0, BANK, bank("F"))
+        frozen_layer(BANK, T, bank("E"))
 
-        def add_turned(total, tile_t, start, stop):
-            nc.tensor.matmul(total[:, 0:P], lhsT=tile_t, rhs=ident[:], is_transpose=True, start=start, stop=stop)
+        def add_turned(total, tile, start, stop):
+            nc.tensor.matmul(total, lhsT=tile, rhs=ident[:], is_transpose=True, start=start, stop=stop)
 
-        sums = pair("B") + [bank("E")] + pair("A") + [bank("F")]
+        def weighted(r, first, last, name):
+            tile = keep.tile([P, last - first], F32, name=name)
+            nc.vector.tensor_tensor(tile[:], y[:].indirect(entries(lists[r], first, last)), gates[:, r, first:last], MULT)
+            return tile
+
+        sums_t = [bank(name)[:, 0:N] for name in ("C", "B0", "D", "B1", "A0", "A1")]
         for block in range(BLOCKS):
-            add_turned(sums[block], base_t[:, block, :], True, False)
-        steps = [(half, r) for half in range(2) for r in range(TURNED)]
-        scaled = {}
+            add_turned(sums_t[block], base[:, block * P : (block + 1) * P], True, False)
+        for half in range(2):
+            for r in range(TURNED):
+                picked = weighted(r, half * HALF, (half + 1) * HALF, "picked%d_%d" % (half, r))
+                for j in range(per_half):
+                    add_turned(sums_t[half * per_half + j], picked[:, j * P : (j + 1) * P], False, r == TURNED - 1)
+        sums = [bank("F"), bank("E")]
+        for block in range(BLOCKS):
+            half, j = divmod(block, per_half)
+            tile = keep.tile([P, N], F32, name="closing" if block == per_half - 1 else "sum_t%d" % block)
+            nc.scalar.copy(out=tile[:], in_=sums_t[block])
+            nc.tensor.transpose(sums[half][:, j * P : (j + 1) * P], tile[:], ident[:])
 
-        def turn_picked(half, r):
-            picked = ring.tile([P, HALF], F32, name="picked", bufs=2 * TURNED)
-            nc.vector.tensor_copy(picked[:], y[:].indirect(entries(lists[r], half * HALF, (half + 1) * HALF)))
-            flat_t = bank("CD"[r])
-            for j in range(per_half):
-                nc.tensor.transpose(flat_t[:, j * P : (j + 1) * P], picked[:, j * P : (j + 1) * P], ident[:])
-            for j in range(per_half):
-                block = half * per_half + j
-                closing = (half, r, j) == (0, TURNED - 1, per_half - 1)
-                tile = keep.tile([P, N], F32, name="closing" if closing else "scaled%d_%d" % (block, r))
-                col = r * BLOCKS + block
-                nc.scalar.activation(
-                    out=tile[:], in_=flat_t[:, j * P : (j + 1) * P], func=COPY, scale=gate_t[:, col : col + 1]
-                )
-                scaled[block, r] = tile
-
-        def add_scaled(half, r):
-            for block in range(half * per_half, (half + 1) * per_half):
-                add_turned(sums[block], scaled[block, r][:], False, r == TURNED - 1)
-
-        turn_picked(*steps[0])
-        for k in range(len(steps)):
-            if k + 1 < len(steps):
-                turn_picked(*steps[k + 1])
-            add_scaled(*steps[k])
-
-        runs = [(0, per_half), (per_half, BLOCKS - 1), (BLOCKS - 1, BLOCKS)]
+        runs = [(0, HALF), (HALF, T - P), (T - P, T)]
         thirds = []
 
         def gather_third(first, last):
-            name = "closing" if last == BLOCKS else "third%d" % first
-            third = keep.tile([P, (last - first) * P], F32, name=name)
-            nc.vector.tensor_tensor(
-                third[:],
-                y[:].indirect(entries(lists[TOP - 1], first * P, last * P)),
-                gate_last[:, first * P : last * P],
-                MULT,
-            )
-            thirds.append(third)
+            thirds.append(weighted(TOP - 1, first, last, "closing" if last == T else "third%d" % first))
 
         def add_and_store(first, last, third):
-            result = keep.tile([P, (last - first) * P], F32, name="result%d" % first)
-            for block in range(first, last):
-                cols = slice((block - first) * P, (block - first + 1) * P)
-                nc.vector.tensor_tensor(result[:, cols], sums[block][:, 0:P], third[:, cols], ADD)
-            queue = nc.scalar if last == BLOCKS else nc.sync
-            queue.dma_start(out=out[:, first * P : last * P], in_=result[:])
+            result = keep.tile([P, last - first], F32, name="result%d" % first)
+            half = first // HALF
+            nc.vector.tensor_tensor(result[:], sums[half][:, first - half * HALF : last - half * HALF], third[:], ADD)
+            queue = nc.scalar if last == T else nc.sync
+            queue.dma_start(out=out[:, first:last], in_=result[:])
 
         gather_third(*runs[0])
         for k in range(len(runs)):

@@ -32,7 +32,7 @@ VECTOR_ROUNDS = []
 DIRECT = 5
 VECTOR_Y = [0, 2]
 EARLY_Q = 9
-SCALE_GROUPS = [(0, 3), (3, 10)]
+SCALE_GROUPS = [(0, 10)]
 
 
 def tile_moe_adp_none_kernel(
@@ -110,7 +110,17 @@ def tile_moe_adp_none_kernel(
 
         offs_sb = keep.tile([P, SLOTS // PER_COLUMN], U16, name="offs_sb")
         nc.sync.dma_start(offs_sb[:], offs)
-        load_was(1, [0, 2], nc.scalar)
+        stacked = plane_tile(H, "stacked")
+        direct_rows = wa_rows[PASSES * DIRECT : PASSES * E]
+
+        def load_stacked(g, queue=nc.sync):
+            queue.dma_start(
+                out=stacked[32 * g : 32 * (g + 1), :].bitcast(I32),
+                in_=direct_rows[:, 4 * g : 4 * (g + 1), :].bitcast(I32),
+            )
+
+        load_was(0, [0], nc.scalar)
+        load_stacked(0, nc.scalar)
         xs = plane_tile(T, "xs")
         nc.gpsimd.memset(xs[:].bitcast(I32), 0)
         for q in range(4):
@@ -119,11 +129,13 @@ def tile_moe_adp_none_kernel(
                 in_=x_scales[:, q:16:4, :].rearrange("s g t -> g s t").bitcast(I32),
             )
         nc.sync.dma_start(out=xw_all[:], in_=x_words.rearrange("s p t d -> p s (t d)").bitcast(I32))
-        load_was(0, [0, 1], nc.scalar)
+        load_was(0, [1, 2], nc.scalar)
         load_wa(0, 1)
-        load_was(0, [2, 3])
+        load_was(0, [3])
+        load_stacked(1)
         load_wa(1, 3)
-        load_was(1, [1, 3])
+        load_stacked(2)
+        load_stacked(3)
 
         slot_s1 = plane_tile(SLOTS, "slot_s1")
         wbs = plane_tile(E * N, "wbs")
@@ -162,18 +174,9 @@ def tile_moe_adp_none_kernel(
         gather_scales(0, 1)
         gather_scales(1, 3)
         load_wa(3, 5)
-        stacked = plane_tile(H, "stacked")
-        direct_rows = wa_rows[PASSES * DIRECT : PASSES * E]
-        for g in range(4):
-            nc.sync.dma_start(
-                out=stacked[32 * g : 32 * (g + 1), :].bitcast(I32),
-                in_=direct_rows[:, 4 * g : 4 * (g + 1), :].bitcast(I32),
-            )
+        load_wa(DIRECT, DIRECT + 2)
         gather_words(0)
         gather_scales(3, 5)
-        load_wa(DIRECT, DIRECT + 2)
-        load_wa(DIRECT + 2, E)
-        load_list(pos1)
         stacked_by_d = plane_tile(H, "stacked_by_d")
         nc.gpsimd.tensor_copy(
             out=stacked_by_d[:].rearrange("p (d m) -> p d m", d=4), in_=stacked[:].rearrange("p (m d) -> p d m", d=4)
@@ -183,10 +186,11 @@ def tile_moe_adp_none_kernel(
             nc.sync.dma_start(
                 out=direct_planes[q:P:32, :, :].bitcast(I32), in_=stacked_by_d[q:P:4, :].bitcast(I32)
             )
+        load_wa(DIRECT + 2, E)
         gather_words(1)
         gather_words(2)
         gather_scales(5, 7)
-        for pos in (pos2, pos3):
+        for pos in (pos1, pos2, pos3):
             load_list(pos)
         gather_words(3)
         gather_words(4)

@@ -208,8 +208,11 @@ def tile_moe_adp_none_kernel(
         gather_scales(8, 9)
         load_scale_rows(wbs, wb_rows, [2, 3])
         load_scale_rows(ws, w_scales, [3])
-        gates = keep.tile([P, TOP, T], F32, name="gates")
-        nc.sync.dma_start(out=gates[:], in_=gate.rearrange("r p t -> p r t"))
+        gates = keep.tile([P, TOP - 1, T], F32, name="gates")
+        nc.sync.dma_start(out=gates[:], in_=gate[1:TOP].rearrange("r p t -> p r t"))
+        gate_t = keep.tile([P, BLOCKS], F32, name="gate_t")
+        with nc.allow_non_contiguous_dma(reason="one gate value a token and partition"):
+            nc.sync.dma_start(out=gate_t[:], in_=gate[0, 0, :].rearrange("(b p) -> p b", p=P))
         gather_words(7)
         gather_words(8)
 
@@ -365,29 +368,41 @@ def tile_moe_adp_none_kernel(
 
         def weighted(r, first, last, name):
             tile = keep.tile([P, last - first], F32, name=name)
-            nc.vector.tensor_tensor(tile[:], y[:].indirect(entries(lists[r], first, last)), gates[:, r, first:last], MULT)
+            nc.vector.tensor_tensor(tile[:], y[:].indirect(entries(lists[r], first, last)), gates[:, r - 1, first:last], MULT)
             return tile
 
-        sums_t = [bank(name)[:, 0:N] for name in ("C", "B0", "D", "B1", "A0", "A1")]
-        for block in range(BLOCKS):
-            add_turned(sums_t[block], base[:, block * P : (block + 1) * P], True, False)
-        for half in range(2):
-            for r in range(TURNED):
-                picked = weighted(r, half * HALF, (half + 1) * HALF, "picked%d_%d" % (half, r))
-                for j in range(per_half):
-                    add_turned(sums_t[half * per_half + j], picked[:, j * P : (j + 1) * P], False, r == TURNED - 1)
-        sums = [bank("F"), bank("E")]
+        sums_t = pair("B")
+        raw_t = pair("A")
         for block in range(BLOCKS):
             half, j = divmod(block, per_half)
-            tile = keep.tile([P, N], F32, name="closing" if block == per_half - 1 else "sum_t%d" % block)
-            nc.scalar.copy(out=tile[:], in_=sums_t[block])
-            nc.tensor.transpose(sums[half][:, j * P : (j + 1) * P], tile[:], ident[:])
+            add_turned(sums_t[half][:, j * N : (j + 1) * N], base[:, block * P : (block + 1) * P], j == 0, False)
+        for half in range(2):
+            raw = keep.tile([P, HALF], F32, name="raw%d" % half)
+            nc.scalar.activation(raw[:], y[:].indirect(entries(lists[0], half * HALF, (half + 1) * HALF)), COPY)
+            for j in range(per_half):
+                nc.tensor.transpose(raw_t[half][:, j * N : (j + 1) * N], raw[:, j * P : (j + 1) * P], ident[:])
+            picked = weighted(1, half * HALF, (half + 1) * HALF, "picked%d" % half)
+            for j in range(per_half):
+                add_turned(sums_t[half][:, j * N : (j + 1) * N], picked[:, j * P : (j + 1) * P], False, j == per_half - 1)
+        sums = [bank("C"), bank("D")]
+        for half in range(2):
+            for j in range(per_half):
+                block = half * per_half + j
+                scaled = keep.tile([P, N], F32, name="scaled%d" % block)
+                nc.scalar.activation(
+                    out=scaled[:], in_=raw_t[half][:, j * N : (j + 1) * N], func=COPY, scale=gate_t[:, block : block + 1]
+                )
+                add_turned(sums[half][:, j * P : (j + 1) * P], scaled[:], j == 0, False)
+            tile = keep.tile([P, HALF], F32, name="sum_t%d" % half)
+            nc.scalar.copy(out=tile[:], in_=sums_t[half][:, 0:HALF])
+            for j in range(per_half):
+                add_turned(sums[half][:, j * P : (j + 1) * P], tile[:, j * N : (j + 1) * N], False, j == per_half - 1)
 
         runs = [(0, HALF), (HALF, T - P), (T - P, T)]
         thirds = []
 
         def gather_third(first, last):
-            thirds.append(weighted(TOP - 1, first, last, "closing" if last == T else "third%d" % first))
+            thirds.append(weighted(TOP - 1, first, last, "third%d" % first))
 
         def add_and_store(first, last, third):
             result = keep.tile([P, last - first], F32, name="result%d" % first)

@@ -208,11 +208,16 @@ def tile_moe_adp_none_kernel(
         gather_scales(8, 9)
         load_scale_rows(wbs, wb_rows, [2, 3])
         load_scale_rows(ws, w_scales, [3])
-        gates = keep.tile([P, TOP - 1, T], F32, name="gates")
-        nc.sync.dma_start(out=gates[:], in_=gate[1:TOP].rearrange("r p t -> p r t"))
-        gate_t = keep.tile([P, BLOCKS], F32, name="gate_t")
-        with nc.allow_non_contiguous_dma(reason="one gate value a token and partition"):
-            nc.sync.dma_start(out=gate_t[:], in_=gate[0, 0, :].rearrange("(b p) -> p b", p=P))
+        gate_mid = keep.tile([P, HALF], F32, name="gate_mid")
+        nc.sync.dma_start(out=gate_mid[:], in_=gate[1][:, HALF:T])
+        gate_last = keep.tile([P, T], F32, name="gate_last")
+        nc.sync.dma_start(out=gate_last[:], in_=gate[2])
+        gate_t = []
+        for r, blocks in enumerate((BLOCKS, BLOCKS // 2)):
+            tile = keep.tile([P, blocks], F32, name="gate_t%d" % r)
+            with nc.allow_non_contiguous_dma(reason="one gate value a token and partition"):
+                nc.sync.dma_start(out=tile[:], in_=gate[r, 0, 0 : blocks * P].rearrange("(b p) -> p b", p=P))
+            gate_t.append(tile)
         gather_words(7)
         gather_words(8)
 
@@ -315,11 +320,8 @@ def tile_moe_adp_none_kernel(
 
         per_half = HALF // P
 
-        base = keep.tile([P, T], F32, name="base")
-
         def frozen_layer(first, last, acc):
-            width = BANK if last - first == BANK else P
-            for lo in range(first, last, width):
+            for lo, width in ((first, 2 * P), (first + 2 * P, P)):
                 cols = slice(lo, lo + width)
                 for s in range(PASSES):
                     nc.tensor.matmul_mx(
@@ -331,7 +333,7 @@ def tile_moe_adp_none_kernel(
                         start=(s == 0),
                         stop=(s == PASSES - 1),
                     )
-            nc.scalar.copy(out=base[:, first:last], in_=acc[:, 0 : last - first])
+            return acc[:, 0 : last - first]
 
         for e in range(DIRECT, E):
             spread_columns(e)
@@ -360,59 +362,56 @@ def tile_moe_adp_none_kernel(
             second_product(2 * k * C, (2 * k + 2) * C, y_banks[k], k in VECTOR_Y)
         for b, target in enumerate(pair("A")):
             second_product(last + b * P, last + (b + 1) * P, target, True)
-        frozen_layer(0, BANK, bank("F"))
-        frozen_layer(BANK, T, bank("E"))
+        base = [frozen_layer(0, HALF, bank("F")), frozen_layer(HALF, T, bank("E"))]
 
         def add_turned(total, tile, start, stop):
             nc.tensor.matmul(total, lhsT=tile, rhs=ident[:], is_transpose=True, start=start, stop=stop)
 
-        def weighted(r, first, last, name):
+        def weighted(r, first, last, gates, name):
             tile = keep.tile([P, last - first], F32, name=name)
-            nc.vector.tensor_tensor(tile[:], y[:].indirect(entries(lists[r], first, last)), gates[:, r - 1, first:last], MULT)
+            nc.vector.tensor_tensor(tile[:], y[:].indirect(entries(lists[r], first, last)), gates, MULT)
             return tile
 
-        sums_t = pair("B")
-        raw_t = pair("A")
-        for block in range(BLOCKS):
-            half, j = divmod(block, per_half)
-            add_turned(sums_t[half][:, j * N : (j + 1) * N], base[:, block * P : (block + 1) * P], j == 0, False)
-        for half in range(2):
-            raw = keep.tile([P, HALF], F32, name="raw%d" % half)
-            nc.scalar.activation(raw[:], y[:].indirect(entries(lists[0], half * HALF, (half + 1) * HALF)), COPY)
+        jobs = [(0, 1, "B0"), (0, 0, "B1"), (1, 0, "A0")]
+        raw_t = []
+        for r, half, name in jobs:
+            raw = keep.tile([P, HALF], F32, name="raw%d_%d" % (r, half))
+            nc.scalar.activation(raw[:], y[:].indirect(entries(lists[r], half * HALF, (half + 1) * HALF)), COPY)
+            target = bank(name)
             for j in range(per_half):
-                nc.tensor.transpose(raw_t[half][:, j * N : (j + 1) * N], raw[:, j * P : (j + 1) * P], ident[:])
-            picked = weighted(1, half * HALF, (half + 1) * HALF, "picked%d" % half)
-            for j in range(per_half):
-                add_turned(sums_t[half][:, j * N : (j + 1) * N], picked[:, j * P : (j + 1) * P], False, j == per_half - 1)
-        sums = [bank("C"), bank("D")]
-        for half in range(2):
-            for j in range(per_half):
-                block = half * per_half + j
-                scaled = keep.tile([P, N], F32, name="scaled%d" % block)
-                nc.scalar.activation(
-                    out=scaled[:], in_=raw_t[half][:, j * N : (j + 1) * N], func=COPY, scale=gate_t[:, block : block + 1]
-                )
-                add_turned(sums[half][:, j * P : (j + 1) * P], scaled[:], j == 0, False)
-            tile = keep.tile([P, HALF], F32, name="sum_t%d" % half)
-            nc.scalar.copy(out=tile[:], in_=sums_t[half][:, 0:HALF])
-            for j in range(per_half):
-                add_turned(sums[half][:, j * P : (j + 1) * P], tile[:, j * N : (j + 1) * N], False, j == per_half - 1)
+                nc.tensor.transpose(target[:, j * N : (j + 1) * N], raw[:, j * P : (j + 1) * P], ident[:])
+            raw_t.append(target)
 
-        runs = [(0, HALF), (HALF, T - P), (T - P, T)]
-        thirds = []
+        def added(a, b, name):
+            tile = keep.tile([P, HALF], F32, name=name)
+            nc.vector.tensor_tensor(tile[:], a, b, ADD)
+            return tile[:]
 
-        def gather_third(first, last):
-            thirds.append(weighted(TOP - 1, first, last, "third%d" % first))
+        mid = weighted(1, HALF, T, gate_mid[:], "mid")
+        end = weighted(2, HALF, T, gate_last[:, HALF:T], "end")
+        low = weighted(2, 0, HALF, gate_last[:, 0:HALF], "low")
+        rest = [None, added(base[1], mid[:], "part")]
+        rest[0] = added(base[0], low[:], "rest0")
+        rest[1] = added(rest[1], end[:], "rest1")
 
-        def add_and_store(first, last, third):
-            result = keep.tile([P, last - first], F32, name="result%d" % first)
+        turned_raw = {(r, half): target for (r, half, name), target in zip(jobs, raw_t)}
+        runs = ((HALF, T, "C", nc.sync), (0, 2 * P, "D", nc.sync), (2 * P, HALF, "A1", nc.scalar))
+        for first, last, name, queue in runs:
             half = first // HALF
-            nc.vector.tensor_tensor(result[:], sums[half][:, first - half * HALF : last - half * HALF], third[:], ADD)
-            queue = nc.scalar if last == T else nc.sync
+            total = bank(name)
+            steps = [(block, r) for block in range(first // P, last // P) for r in range(2 - half)]
+            for block, r in steps:
+                j = block - half * per_half
+                scaled = keep.tile([P, N], F32, name="scaled%d_%d" % (r, block))
+                nc.scalar.activation(
+                    out=scaled[:],
+                    in_=turned_raw[r, half][:, j * N : (j + 1) * N],
+                    func=COPY,
+                    scale=gate_t[r][:, block : block + 1],
+                )
+                cols = slice(block * P - first, (block + 1) * P - first)
+                add_turned(total[:, cols], scaled[:], (block, r) == steps[0], (block, r) == steps[-1])
+            result = keep.tile([P, last - first], F32, name="result%d" % first)
+            cols = slice(first - half * HALF, last - half * HALF)
+            nc.vector.tensor_tensor(result[:], total[:, 0 : last - first], rest[half][:, cols], ADD)
             queue.dma_start(out=out[:, first:last], in_=result[:])
-
-        gather_third(*runs[0])
-        for k in range(len(runs)):
-            if k + 1 < len(runs):
-                gather_third(*runs[k + 1])
-            add_and_store(*runs[k], thirds[k])

@@ -30,7 +30,7 @@ TURNED = TOP - 1
 CHUNKS = [(0, 1), (1, 3), (3, 5), (5, 7), (7, 8), (8, 9)]
 VECTOR_ROUNDS = []
 DIRECT = 5
-VECTOR_Y = [0, 2]
+VECTOR_Y = [2]
 EARLY_Q = 9
 SCALE_GROUPS = [(0, 10)]
 
@@ -113,14 +113,8 @@ def tile_moe_adp_none_kernel(
         stacked = plane_tile(H, "stacked")
         direct_rows = wa_rows[PASSES * DIRECT : PASSES * E]
 
-        def load_stacked(g, queue=nc.sync):
-            queue.dma_start(
-                out=stacked[32 * g : 32 * (g + 1), :].bitcast(I32),
-                in_=direct_rows[:, 4 * g : 4 * (g + 1), :].bitcast(I32),
-            )
-
         load_was(0, [0], nc.scalar)
-        load_stacked(0, nc.scalar)
+        nc.scalar.dma_start(out=stacked[:].bitcast(I32), in_=direct_rows.rearrange("g b n -> b g n").bitcast(I32))
         xs = plane_tile(T, "xs")
         nc.gpsimd.memset(xs[:].bitcast(I32), 0)
         for q in range(4):
@@ -129,13 +123,10 @@ def tile_moe_adp_none_kernel(
                 in_=x_scales[:, q:16:4, :].rearrange("s g t -> g s t").bitcast(I32),
             )
         nc.sync.dma_start(out=xw_all[:], in_=x_words.rearrange("s p t d -> p s (t d)").bitcast(I32))
-        load_was(0, [1, 2], nc.scalar)
+        load_was(0, [1], nc.scalar)
         load_wa(0, 1)
-        load_was(0, [3])
-        load_stacked(1)
+        load_was(0, [2, 3])
         load_wa(1, 3)
-        load_stacked(2)
-        load_stacked(3)
 
         slot_s1 = plane_tile(SLOTS, "slot_s1")
         wbs = plane_tile(E * N, "wbs")
@@ -184,7 +175,8 @@ def tile_moe_adp_none_kernel(
         direct_planes = keep.tile([P, PASSES * (E - DIRECT), H], U8, name="direct_planes", align_bytes=64)
         for q in range(4):
             nc.sync.dma_start(
-                out=direct_planes[q:P:32, :, :].bitcast(I32), in_=stacked_by_d[q:P:4, :].bitcast(I32)
+                out=direct_planes[32 * q : 32 * q + 4, :, :].bitcast(I32),
+                in_=stacked_by_d[32 * q : 32 * (q + 1), :].bitcast(I32),
             )
         load_wa(DIRECT + 2, E)
         gather_words(1)
@@ -223,10 +215,18 @@ def tile_moe_adp_none_kernel(
 
         rounded, turned_in, codes, spread = {}, {}, {}, {}
 
+        def h_tile(e):
+            first = e - e % 2
+            if first not in turned_in:
+                width = (min(first + 2, E) - first) * 4 * C
+                turned_in[first] = keep.tile([P, width], BF16, name="h_in%d" % first, align_bytes=64)
+            return turned_in[first][:, (e - first) * 4 * C : (e - first + 1) * 4 * C]
+
         def first_product(e, banks):
             h_bf = keep.tile([P, 2, H], BF16, name="h_bf%d" % e)
-            for k, s in enumerate(pass_order(e)):
-                for b in range(2):
+            steps = [(k, s, b) for k, s in enumerate(pass_order(e)) for b in range(2)]
+            for k, s, b in sorted(steps, key=lambda step: step[2]) if e == 0 else steps:
+                if True:
                     slot = e * C + b * P
                     planes = (slot_s0[e][:, b * P : (b + 1) * P], slot_s1[:, slot : slot + P])
                     nc.tensor.matmul_mx(
@@ -254,7 +254,7 @@ def tile_moe_adp_none_kernel(
                 spread[e, s] = (tile, direct_planes[:, (e - DIRECT) * PASSES + s, :])
 
         def direct_product(e, banks):
-            h_in = keep.tile([P, 4 * C], BF16, name="h_in%d" % e, align_bytes=64)
+            h_in = h_tile(e)
             for k, s in enumerate(pass_order(e)):
                 tile, plane = spread[e, s]
                 for b in range(2):
@@ -277,7 +277,6 @@ def tile_moe_adp_none_kernel(
                     nc.vector.tensor_copy(out=dst, in_=src)
                 else:
                     nc.scalar.activation(out=dst, in_=src, func=COPY)
-            turned_in[e] = h_in
 
         def turn(e, target):
             turned = target.rearrange("p (b u j) -> p b u j", b=2, u=2)
@@ -285,12 +284,11 @@ def tile_moe_adp_none_kernel(
             for b in range(2):
                 for u in range(2):
                     nc.tensor.transpose(turned[:, b, u, :], pairs[:, b, u * P : (u + 1) * P], ident[:])
-            h_in = keep.tile([P, 4 * C], BF16, name="h_in%d" % e, align_bytes=64)
+            h_in = h_tile(e)
             nc.scalar.copy(
-                out=h_in[:].bitcast(F32).rearrange("p (b j u) -> p b j u", b=2, u=2),
+                out=h_in.bitcast(F32).rearrange("p (b j u) -> p b j u", b=2, u=2),
                 in_=turned.rearrange("p b u j -> p b j u"),
             )
-            turned_in[e] = h_in
 
         def quantize_slots(first, last):
             e = first // C
@@ -301,7 +299,9 @@ def tile_moe_adp_none_kernel(
                 scales=h_s[:],
                 in_=turned_in[e][:, 4 * (first - e * C) : 4 * (last - e * C)],
             )
-            codes[first] = (h_w, h_s)
+            for lo in range(first, last, C):
+                cols = slice(lo - first, min(lo + C, last) - first)
+                codes[lo] = (h_w[:, cols], h_s[:, cols])
 
         def second_product(first, last, y_bank, on_vector):
             for lo in range(first, last, C):
@@ -311,8 +311,8 @@ def tile_moe_adp_none_kernel(
                     out=y_bank[:, lo - first : hi - first],
                     lhsT=wbw[:, e, :].bitcast(FP4X4),
                     lhsT_scale=wbs[:, e * N : (e + 1) * N],
-                    rhs=h_w[:].bitcast(FP8X4),
-                    rhs_scale=h_s[:],
+                    rhs=h_w.bitcast(FP8X4),
+                    rhs_scale=h_s,
                     start=True,
                     stop=True,
                 )
@@ -344,23 +344,23 @@ def tile_moe_adp_none_kernel(
         turn(1, bank("D"))
         first_product(3, [bank("E"), bank("F")])
         first_product(4, pair("A"))
-        turn(2, bank("E"))
-        turn(3, bank("F"))
         direct_product(5, [bank("C"), bank("D")])
-        direct_product(6, [bank("E"), bank("F")])
-        turn(4, bank("C"))
-        direct_product(7, pair("A"))
-        direct_product(8, [bank("D"), bank("E")])
+        turn(2, bank("B0"))
+        turn(3, bank("E"))
+        turn(4, bank("F"))
+        direct_product(6, pair("A"))
+        direct_product(7, [bank("C"), bank("D")])
+        direct_product(8, [bank("E"), bank("F")])
         last = (E - 1) * C
-        for e in range(E - 1):
-            quantize_slots(e * C, (e + 1) * C)
+        for e in range(0, E - 1, 2):
+            quantize_slots(e * C, (e + 2) * C)
         for b in range(2):
             quantize_slots(last + b * P, last + (b + 1) * P)
         scalar_banks = pair("B")
-        y_banks = [bank("C"), scalar_banks[0], bank("D"), scalar_banks[1]]
+        y_banks = [bank("A0"), scalar_banks[0], bank("A1"), scalar_banks[1]]
         for k in range(4):
             second_product(2 * k * C, (2 * k + 2) * C, y_banks[k], k in VECTOR_Y)
-        for b, target in enumerate(pair("A")):
+        for b, target in enumerate([bank("C"), bank("D")]):
             second_product(last + b * P, last + (b + 1) * P, target, True)
         base = [frozen_layer(0, HALF, bank("F")), frozen_layer(HALF, T, bank("E"))]
 

@@ -23,16 +23,10 @@ PASSES = K // 512
 SLOTS = E * C
 BANK = 512
 PER_COLUMN = 16
-BLOCKS = T // P
 HALF = T // 2
-TURNED = TOP - 1
-
-CHUNKS = [(0, 1), (1, 3), (3, 5), (5, 7), (7, 8), (8, 9)]
-VECTOR_ROUNDS = []
-DIRECT = 5
-VECTOR_Y = [2]
-EARLY_Q = 9
-SCALE_GROUPS = [(0, 10)]
+PER_HALF = HALF // P
+LIFT = 16
+SORTED_FROM = 5
 
 
 def tile_moe_adp_none_kernel(
@@ -41,242 +35,177 @@ def tile_moe_adp_none_kernel(
     nc = tc.nc
     with ExitStack() as ctx:
         keep = ctx.enter_context(tc.tile_pool(name="keep", bufs=1))
-        ring = ctx.enter_context(tc.tile_pool(name="ring", bufs=2))
         psum = ctx.enter_context(tc.psum_pool(name="psum", bufs=1))
 
-        def plane_tile(cols, name):
-            return keep.tile([P, cols], U8, name=name, align_bytes=64)
+        def sbuf(shape, dtype, name):
+            return keep.tile(shape, dtype, name=name, align_bytes=64)
 
-        def load_scale_rows(plane, rows, quarters=range(4), queue=nc.sync):
-            passes = rows.shape[0]
+        def bank(number):
+            return psum.tile([P, BANK], F32, name="bank%d" % number)[:]
+
+        def load_scale_rows(planes, rows, quarters, queue):
             for q in quarters:
                 queue.dma_start(
-                    out=plane[q:P:32, :].rearrange("b (g n) -> b g n", g=passes).bitcast(I32),
-                    in_=rows[:, q:16:4, :].rearrange("g b n -> b g n").bitcast(I32),
+                    out=planes[q:P:32, :].rearrange("g (c n) -> g c n", c=rows.shape[0]).bitcast(I32),
+                    in_=rows[:, q:16:4, :].rearrange("c g n -> g c n").bitcast(I32),
                 )
 
-        def shift_second_pass(dst, src, queue):
-            queue.dma_start(out=dst[0:112, :].bitcast(I32), in_=src[16:128, :].bitcast(I32))
+        def lift(dst, src, queue):
+            queue.dma_start(out=dst[0 : P - LIFT, :].bitcast(I32), in_=src[LIFT:P, :].bitcast(I32))
 
-        def entries(offsets, lo, hi):
-            return offsets[:, lo // PER_COLUMN : hi // PER_COLUMN]
-
-        def copy_out(on_vector, dst, src):
-            if on_vector:
-                nc.vector.tensor_copy(out=dst, in_=src)
-            else:
-                nc.scalar.copy(out=dst, in_=src)
-
-        def bank(letter):
-            return psum.tile([P, BANK], F32, name="bank" + letter)[:]
-
-        def pair(letter):
-            return [bank(letter + "0"), bank(letter + "1")]
-
-        xw_all = keep.tile([P, PASSES, T], I32, name="xw", align_bytes=64)
-        xw = [xw_all[:, s, :] for s in range(PASSES)]
+        def entries(offsets, first, last):
+            return offsets[:, first // PER_COLUMN : last // PER_COLUMN]
 
         wa_rows = wa_scales.rearrange("e s b n -> (e s) b n")
-        was, waw = {}, {}
+        wa_sb = {}
 
-        def load_wa(first, last, passes=range(PASSES)):
-            count = len(passes)
-            name = "waw%d_%d" % (first, passes[0])
-            tile = keep.tile([P, (last - first) * count, 2 * H], U8, name=name, align_bytes=64)
-            rows = wa_words.bitcast(I32)[first:last, passes[0] : passes[0] + count]
+        def load_wa(first, last):
+            tile = sbuf([P, (last - first) * PASSES, 2 * H], U8, "wa%d" % first)
+            rows = wa_words.bitcast(I32)[first:last]
             nc.sync.dma_start(out=tile[:].bitcast(I32), in_=rows.rearrange("e s p n -> p (e s) n"))
             for e in range(first, last):
-                for s in passes:
-                    waw[e, s] = tile[:, (e - first) * count + s - passes[0], :]
-
-        for first, last in SCALE_GROUPS:
-            planes = plane_tile((last - first) * H, "was%d" % first)
-            for g in range(first, last):
-                was[g] = planes[:, (g - first) * H :]
-
-        def load_was(group, quarters=range(4), queue=nc.sync):
-            first, last = SCALE_GROUPS[group]
-            load_scale_rows(was[first], wa_rows[first:last], quarters, queue)
-
-        def pass_order(e):
-            return (0, 1) if e in (0, 1, E - 1) else (1, 0)
-
-        lists = []
-
-        def load_list(pos):
-            pos_sb = keep.tile([P, T // PER_COLUMN], U16, name="pos_sb%d" % len(lists))
-            nc.sync.dma_start(pos_sb[:], pos)
-            lists.append(pos_sb)
+                for s in range(PASSES):
+                    wa_sb[e, s] = tile[:, (e - first) * PASSES + s, :]
 
         offs_sb = keep.tile([P, SLOTS // PER_COLUMN], U16, name="offs_sb")
         nc.sync.dma_start(offs_sb[:], offs)
-        stacked = plane_tile(H, "stacked")
-        direct_rows = wa_rows[PASSES * DIRECT : PASSES * E]
-
-        load_was(0, [0], nc.scalar)
-        nc.scalar.dma_start(out=stacked[:].bitcast(I32), in_=direct_rows.rearrange("g b n -> b g n").bitcast(I32))
-        xs = plane_tile(T, "xs")
+        wa_planes = sbuf([P, PASSES * SORTED_FROM * H], U8, "wa_planes")
+        turned_rows = wa_rows[0 : PASSES * SORTED_FROM]
+        load_scale_rows(wa_planes, turned_rows, [0], nc.scalar)
+        stacked = sbuf([P, H], U8, "stacked")
+        nc.scalar.dma_start(
+            out=stacked[:].bitcast(I32),
+            in_=wa_rows[PASSES * SORTED_FROM :].rearrange("c b n -> b c n").bitcast(I32),
+        )
+        xs = sbuf([P, T], U8, "xs")
         nc.gpsimd.memset(xs[:].bitcast(I32), 0)
         for q in range(4):
             (nc.sync, nc.scalar)[q // 2].dma_start(
-                out=xs[q:P:16, :].bitcast(I32),
+                out=xs[q:P:LIFT, :].bitcast(I32),
                 in_=x_scales[:, q:16:4, :].rearrange("s g t -> g s t").bitcast(I32),
             )
-        nc.sync.dma_start(out=xw_all[:], in_=x_words.rearrange("s p t d -> p s (t d)").bitcast(I32))
-        load_was(0, [1], nc.scalar)
+        xw = sbuf([P, PASSES, T], I32, "xw")
+        nc.sync.dma_start(out=xw[:], in_=x_words.rearrange("s p t d -> p s (t d)").bitcast(I32))
+        load_scale_rows(wa_planes, turned_rows, [1], nc.scalar)
         load_wa(0, 1)
-        load_was(0, [2, 3])
+        load_scale_rows(wa_planes, turned_rows, [2, 3], nc.sync)
         load_wa(1, 3)
 
-        slot_s1 = plane_tile(SLOTS, "slot_s1")
-        wbs = plane_tile(E * N, "wbs")
-        ws = plane_tile(PASSES * N, "ws")
-        xs1 = plane_tile(T, "xs1")
         y = keep.tile([P, SLOTS], F32, name="y")
         ident = keep.tile([P, P], F32, name="ident")
         make_identity(nc, ident[:])
 
-        slot_s0, words = {}, {}
+        slot_planes, slot_words = {}, {}
+        lifted = sbuf([P, SLOTS], U8, "lifted")
 
-        scale_tiles = {}
-
-        def gather_scales(first, last):
-            c = [k for k, (lo, hi) in enumerate(CHUNKS) if lo <= first < hi][0]
-            lo, hi = CHUNKS[c]
-            if c not in scale_tiles:
-                scale_tiles[c] = plane_tile((hi - lo) * C, "slot_s0_%d" % c)
-            tile = scale_tiles[c]
-            nc.vector.tensor_copy(
-                tile[:, (first - lo) * C : (last - lo) * C], xs[:].indirect(entries(offs_sb, first * C, last * C))
-            )
+        def gather_scales(first, last, queue):
+            tile = sbuf([P, (last - first) * C], U8, "slot_scales%d" % first)
+            nc.vector.tensor_copy(tile[:], xs[:].indirect(entries(offs_sb, first * C, last * C)))
+            lift(lifted[:, first * C : last * C], tile[:], queue)
             for e in range(first, last):
-                slot_s0[e] = tile[:, (e - lo) * C : (e - lo + 1) * C]
-            if last == hi:
-                shift_second_pass(slot_s1[:, lo * C : hi * C], tile[:], nc.sync if c else nc.scalar)
+                slot_planes[e] = (tile[:, (e - first) * C : (e - first + 1) * C], lifted[:, e * C : (e + 1) * C])
+
+        def pass_order(e):
+            return (0, 1) if e in (0, 1, E - 1) else (1, 0)
 
         def gather_words(e):
             for s in pass_order(e):
-                tile = keep.tile([P, C], I32, name="slot_w%d_%d" % (e, s), align_bytes=64)
+                tile = sbuf([P, C], I32, "slot_words%d_%d" % (e, s))
                 nc.vector.tensor_copy(
-                    tile[:].bitcast(U32), xw[s].bitcast(U32).indirect(entries(offs_sb, e * C, (e + 1) * C))
+                    tile[:].bitcast(U32), xw[:, s, :].bitcast(U32).indirect(entries(offs_sb, e * C, (e + 1) * C))
                 )
-                words[e, s] = tile
+                slot_words[e, s] = tile
 
-        gather_scales(0, 1)
-        gather_scales(1, 3)
-        load_wa(3, 5)
-        load_wa(DIRECT, DIRECT + 2)
+        def load_list(pos, name):
+            tile = keep.tile([P, T // PER_COLUMN], U16, name=name)
+            nc.sync.dma_start(tile[:], pos)
+            return tile
+
+        def load_gate_column(r, blocks):
+            tile = keep.tile([P, blocks], F32, name="gate_column%d" % r)
+            with nc.allow_non_contiguous_dma(reason="one gate value a token and partition"):
+                nc.sync.dma_start(out=tile[:], in_=gate[r, 0, 0 : blocks * P].rearrange("(b p) -> p b", p=P))
+            return tile
+
+        gather_scales(0, 1, nc.scalar)
+        gather_scales(1, 3, nc.sync)
+        load_wa(3, SORTED_FROM)
+        load_wa(SORTED_FROM, SORTED_FROM + 2)
         gather_words(0)
-        gather_scales(3, 5)
-        stacked_by_d = plane_tile(H, "stacked_by_d")
+        gather_scales(3, 5, nc.sync)
+        stacked_by_d = sbuf([P, H], U8, "stacked_by_d")
         nc.gpsimd.tensor_copy(
             out=stacked_by_d[:].rearrange("p (d m) -> p d m", d=4), in_=stacked[:].rearrange("p (m d) -> p d m", d=4)
         )
-        direct_planes = keep.tile([P, PASSES * (E - DIRECT), H], U8, name="direct_planes", align_bytes=64)
-        for q in range(4):
+        sorted_planes = sbuf([P, PASSES * (E - SORTED_FROM), H], U8, "sorted_planes")
+        for g in range(4):
             nc.sync.dma_start(
-                out=direct_planes[32 * q : 32 * q + 4, :, :].bitcast(I32),
-                in_=stacked_by_d[32 * q : 32 * (q + 1), :].bitcast(I32),
+                out=sorted_planes[32 * g : 32 * g + 4, :, :].bitcast(I32),
+                in_=stacked_by_d[32 * g : 32 * (g + 1), :].bitcast(I32),
             )
-        load_wa(DIRECT + 2, E)
+        load_wa(SORTED_FROM + 2, E)
         gather_words(1)
         gather_words(2)
-        gather_scales(5, 7)
-        for pos in (pos1, pos2, pos3):
-            load_list(pos)
+        gather_scales(5, 7, nc.sync)
+        lists = [load_list(pos, "pos_sb%d" % r) for r, pos in enumerate((pos1, pos2, pos3))]
         gather_words(3)
         gather_words(4)
-        gather_scales(7, 8)
-        ww = keep.tile([P, PASSES, 2 * N], U8, name="ww", align_bytes=64)
-        nc.sync.dma_start(out=ww[:].bitcast(I32), in_=w_words.rearrange("s p n -> p s n").bitcast(I32))
-        shift_second_pass(xs1[:], xs[:], nc.sync)
-        wbw = keep.tile([P, E, 2 * N], U8, name="wbw", align_bytes=64)
-        nc.sync.dma_start(out=wbw[:].bitcast(I32), in_=wb_words.rearrange("e o p n -> p (e o) n").bitcast(I32))
-        wb_rows = wb_scales.rearrange("e o b n -> (e o) b n")
-        load_scale_rows(ws, w_scales, [0, 1, 2])
-        load_scale_rows(wbs, wb_rows, [0, 1])
+        gather_scales(7, 8, nc.sync)
+        w_sb = sbuf([P, PASSES, 2 * N], U8, "w_sb")
+        nc.sync.dma_start(out=w_sb[:].bitcast(I32), in_=w_words.rearrange("s p n -> p s n").bitcast(I32))
+        xs_lifted = sbuf([P, T], U8, "xs_lifted")
+        lift(xs_lifted[:], xs[:], nc.sync)
+        wb_sb = sbuf([P, E, 2 * N], U8, "wb_sb")
+        nc.sync.dma_start(out=wb_sb[:].bitcast(I32), in_=wb_words.rearrange("e o p n -> p (e o) n").bitcast(I32))
+        w_planes = sbuf([P, PASSES * N], U8, "w_planes")
+        load_scale_rows(w_planes, w_scales, range(4), nc.sync)
         gather_words(5)
         gather_words(6)
-        gather_scales(8, 9)
-        load_scale_rows(wbs, wb_rows, [2, 3])
-        load_scale_rows(ws, w_scales, [3])
-        gate_mid = keep.tile([P, HALF], F32, name="gate_mid")
-        nc.sync.dma_start(out=gate_mid[:], in_=gate[1][:, HALF:T])
-        gate_last = keep.tile([P, T], F32, name="gate_last")
-        nc.sync.dma_start(out=gate_last[:], in_=gate[2])
-        gate_t = []
-        for r, blocks in enumerate((BLOCKS, BLOCKS // 2)):
-            tile = keep.tile([P, blocks], F32, name="gate_t%d" % r)
-            with nc.allow_non_contiguous_dma(reason="one gate value a token and partition"):
-                nc.sync.dma_start(out=tile[:], in_=gate[r, 0, 0 : blocks * P].rearrange("(b p) -> p b", p=P))
-            gate_t.append(tile)
+        gather_scales(8, 9, nc.sync)
+        wb_planes = sbuf([P, E * N], U8, "wb_planes")
+        load_scale_rows(wb_planes, wb_scales.rearrange("e o b n -> (e o) b n"), range(4), nc.sync)
+        gate_second = keep.tile([P, HALF], F32, name="gate_second")
+        nc.sync.dma_start(out=gate_second[:], in_=gate[1][:, HALF:T])
+        gate_third = keep.tile([P, T], F32, name="gate_third")
+        nc.sync.dma_start(out=gate_third[:], in_=gate[2])
+        gate_columns = [load_gate_column(0, T // P), load_gate_column(1, PER_HALF)]
         gather_words(7)
         gather_words(8)
 
-        rounded, turned_in, codes, spread = {}, {}, {}, {}
+        rounded, h_pairs, codes, sorted_wa = {}, {}, {}, {}
 
-        def h_tile(e):
+        def h_of(e):
             first = e - e % 2
-            if first not in turned_in:
-                width = (min(first + 2, E) - first) * 4 * C
-                turned_in[first] = keep.tile([P, width], BF16, name="h_in%d" % first, align_bytes=64)
-            return turned_in[first][:, (e - first) * 4 * C : (e - first + 1) * 4 * C]
+            if first not in h_pairs:
+                h_pairs[first] = sbuf([P, (min(first + 2, E) - first) * 4 * C], BF16, "h%d" % first)
+            return h_pairs[first][:, (e - first) * 4 * C : (e - first + 1) * 4 * C]
 
-        def first_product(e, banks):
-            h_bf = keep.tile([P, 2, H], BF16, name="h_bf%d" % e)
-            steps = [(k, s, b) for k, s in enumerate(pass_order(e)) for b in range(2)]
-            for k, s, b in sorted(steps, key=lambda step: step[2]) if e == 0 else steps:
-                if True:
-                    slot = e * C + b * P
-                    planes = (slot_s0[e][:, b * P : (b + 1) * P], slot_s1[:, slot : slot + P])
-                    nc.tensor.matmul_mx(
-                        out=banks[b],
-                        lhsT=words[e, s][:, b * P : (b + 1) * P].bitcast(FP8X4),
-                        lhsT_scale=planes[s],
-                        rhs=waw[e, s].bitcast(FP4X4),
-                        rhs_scale=was[e * PASSES + s][:, 0:H],
-                        start=(k == 0),
-                        stop=(k == PASSES - 1),
-                    )
+        def tokens_stationary(e, banks, steps):
+            for s, b in steps:
+                cols = slice(b * P, (b + 1) * P)
+                plane = e * PASSES + s
+                nc.tensor.matmul_mx(
+                    out=banks[b],
+                    lhsT=slot_words[e, s][:, cols].bitcast(FP8X4),
+                    lhsT_scale=slot_planes[e][s][:, cols],
+                    rhs=wa_sb[e, s].bitcast(FP4X4),
+                    rhs_scale=wa_planes[:, plane * H : (plane + 1) * H],
+                    start=(s == pass_order(e)[0]),
+                    stop=(s == pass_order(e)[-1]),
+                )
+            rounded[e] = keep.tile([P, 2, H], BF16, name="rounded%d" % e)
             for b in range(2):
-                dst = h_bf[:, b, :].rearrange("p (u m d) -> p u m d", u=2, d=2)
-                src = banks[b].rearrange("p (m u d) -> p u m d", u=2, d=2)
-                if (e, b) in VECTOR_ROUNDS:
-                    nc.vector.tensor_copy(out=dst, in_=src)
-                else:
-                    nc.scalar.activation(out=dst, in_=src, func=COPY)
-            rounded[e] = h_bf
+                nc.scalar.activation(
+                    out=rounded[e][:, b, :].rearrange("p (u m d) -> p u m d", u=2, d=2),
+                    in_=banks[b].rearrange("p (m u d) -> p u m d", u=2, d=2),
+                    func=COPY,
+                )
 
-        def spread_columns(e):
-            for s in pass_order(e):
-                tile = keep.tile([P, 4, P], U16, name="wa_by_d%d_%d" % (e, s), align_bytes=64)
-                nc.gpsimd.tensor_copy(out=tile[:], in_=waw[e, s].bitcast(U16).rearrange("p (m d) -> p d m", d=4))
-                spread[e, s] = (tile, direct_planes[:, (e - DIRECT) * PASSES + s, :])
+        def by_pass(e):
+            return [(s, b) for s in pass_order(e) for b in range(2)]
 
-        def direct_product(e, banks):
-            h_in = h_tile(e)
-            for k, s in enumerate(pass_order(e)):
-                tile, plane = spread[e, s]
-                for b in range(2):
-                    slot = e * C + b * P
-                    planes = (slot_s0[e][:, b * P : (b + 1) * P], slot_s1[:, slot : slot + P])
-                    for d in range(4):
-                        nc.tensor.matmul_mx(
-                            out=banks[b][:, d * P : (d + 1) * P],
-                            lhsT=tile[:, d, :].bitcast(U8).bitcast(FP4X4),
-                            lhsT_scale=plane[:, d * P : (d + 1) * P],
-                            rhs=words[e, s][:, b * P : (b + 1) * P].bitcast(FP8X4),
-                            rhs_scale=planes[s],
-                            start=(k == 0 and d == 0),
-                            stop=(k == PASSES - 1 and d == 3),
-                        )
-            for b in range(2):
-                dst = h_in[:, b * 4 * P : (b + 1) * 4 * P].rearrange("p (j d) -> p j d", d=4)
-                src = banks[b].rearrange("p (d j) -> p j d", d=4)
-                if (e, b) in VECTOR_ROUNDS:
-                    nc.vector.tensor_copy(out=dst, in_=src)
-                else:
-                    nc.scalar.activation(out=dst, in_=src, func=COPY)
+        def by_block(e):
+            return [(s, b) for b in range(2) for s in pass_order(e)]
 
         def turn(e, target):
             turned = target.rearrange("p (b u j) -> p b u j", b=2, u=2)
@@ -284,134 +213,157 @@ def tile_moe_adp_none_kernel(
             for b in range(2):
                 for u in range(2):
                     nc.tensor.transpose(turned[:, b, u, :], pairs[:, b, u * P : (u + 1) * P], ident[:])
-            h_in = h_tile(e)
             nc.scalar.copy(
-                out=h_in.bitcast(F32).rearrange("p (b j u) -> p b j u", b=2, u=2),
+                out=h_of(e).bitcast(F32).rearrange("p (b j u) -> p b j u", b=2, u=2),
                 in_=turned.rearrange("p b u j -> p b j u"),
             )
 
-        def quantize_slots(first, last):
+        def sort_columns(e):
+            for s in pass_order(e):
+                tile = sbuf([P, 4, P], U16, "sorted_wa%d_%d" % (e, s))
+                nc.gpsimd.tensor_copy(out=tile[:], in_=wa_sb[e, s].bitcast(U16).rearrange("p (m d) -> p d m", d=4))
+                sorted_wa[e, s] = tile
+
+        def wa_stationary(e, banks):
+            for s, b in by_pass(e):
+                cols = slice(b * P, (b + 1) * P)
+                plane = sorted_planes[:, (e - SORTED_FROM) * PASSES + s, :]
+                for d in range(4):
+                    nc.tensor.matmul_mx(
+                        out=banks[b][:, d * P : (d + 1) * P],
+                        lhsT=sorted_wa[e, s][:, d, :].bitcast(U8).bitcast(FP4X4),
+                        lhsT_scale=plane[:, d * P : (d + 1) * P],
+                        rhs=slot_words[e, s][:, cols].bitcast(FP8X4),
+                        rhs_scale=slot_planes[e][s][:, cols],
+                        start=(s == pass_order(e)[0] and d == 0),
+                        stop=(s == pass_order(e)[-1] and d == 3),
+                    )
+            for b in range(2):
+                nc.scalar.activation(
+                    out=h_of(e)[:, b * 4 * P : (b + 1) * 4 * P].rearrange("p (j d) -> p j d", d=4),
+                    in_=banks[b].rearrange("p (d j) -> p j d", d=4),
+                    func=COPY,
+                )
+
+        def quantize(first, last):
             e = first // C
-            h_w = keep.tile([P, last - first], I32, name="h_w%d" % first, align_bytes=64)
-            h_s = plane_tile(last - first, "h_s%d" % first)
+            words = sbuf([P, last - first], I32, "h_words%d" % first)
+            plane = sbuf([P, last - first], U8, "h_plane%d" % first)
             nc.vector.quantize_mx(
-                out=h_w[:].bitcast(FP8X4),
-                scales=h_s[:],
-                in_=turned_in[e][:, 4 * (first - e * C) : 4 * (last - e * C)],
+                out=words[:].bitcast(FP8X4),
+                scales=plane[:],
+                in_=h_pairs[e][:, 4 * (first - e * C) : 4 * (last - e * C)],
             )
             for lo in range(first, last, C):
                 cols = slice(lo - first, min(lo + C, last) - first)
-                codes[lo] = (h_w[:, cols], h_s[:, cols])
+                codes[lo] = (words[:, cols], plane[:, cols])
 
-        def second_product(first, last, y_bank, on_vector):
+        def second_product(first, last, target, copy_out):
             for lo in range(first, last, C):
                 e, hi = lo // C, min(lo + C, last)
-                h_w, h_s = codes[lo]
                 nc.tensor.matmul_mx(
-                    out=y_bank[:, lo - first : hi - first],
-                    lhsT=wbw[:, e, :].bitcast(FP4X4),
-                    lhsT_scale=wbs[:, e * N : (e + 1) * N],
-                    rhs=h_w.bitcast(FP8X4),
-                    rhs_scale=h_s,
+                    out=target[:, lo - first : hi - first],
+                    lhsT=wb_sb[:, e, :].bitcast(FP4X4),
+                    lhsT_scale=wb_planes[:, e * N : (e + 1) * N],
+                    rhs=codes[lo][0].bitcast(FP8X4),
+                    rhs_scale=codes[lo][1],
                     start=True,
                     stop=True,
                 )
-            copy_out(on_vector, y[:, first:last], y_bank[:, 0 : last - first])
+            copy_out(out=y[:, first:last], in_=target[:, 0 : last - first])
 
-        per_half = HALF // P
-
-        def frozen_layer(first, last, acc):
-            for lo, width in ((first, 2 * P), (first + 2 * P, P)):
-                cols = slice(lo, lo + width)
+        def frozen_layer(half, target):
+            for lo, width in ((0, 2 * P), (2 * P, P)):
+                cols = slice(half * HALF + lo, half * HALF + lo + width)
                 for s in range(PASSES):
                     nc.tensor.matmul_mx(
-                        out=acc[:, lo - first : lo - first + width],
-                        lhsT=ww[:, s, :].bitcast(FP4X4),
-                        lhsT_scale=ws[:, s * N : (s + 1) * N],
-                        rhs=xw[s][:, cols].bitcast(FP8X4),
-                        rhs_scale=(xs, xs1)[s][:, cols],
+                        out=target[:, lo : lo + width],
+                        lhsT=w_sb[:, s, :].bitcast(FP4X4),
+                        lhsT_scale=w_planes[:, s * N : (s + 1) * N],
+                        rhs=xw[:, s, cols].bitcast(FP8X4),
+                        rhs_scale=(xs, xs_lifted)[s][:, cols],
                         start=(s == 0),
                         stop=(s == PASSES - 1),
                     )
-            return acc[:, 0 : last - first]
+            return target[:, 0:HALF]
 
-        for e in range(DIRECT, E):
-            spread_columns(e)
-        first_product(0, pair("A"))
-        first_product(1, [bank("C"), bank("D")])
-        first_product(2, pair("B"))
-        turn(0, bank("C"))
-        turn(1, bank("D"))
-        first_product(3, [bank("E"), bank("F")])
-        first_product(4, pair("A"))
-        direct_product(5, [bank("C"), bank("D")])
-        turn(2, bank("B0"))
-        turn(3, bank("E"))
-        turn(4, bank("F"))
-        direct_product(6, pair("A"))
-        direct_product(7, [bank("C"), bank("D")])
-        direct_product(8, [bank("E"), bank("F")])
+        for e in range(SORTED_FROM, E):
+            sort_columns(e)
+        tokens_stationary(0, [bank(0), bank(1)], by_block(0))
+        tokens_stationary(1, [bank(4), bank(5)], by_pass(1))
+        tokens_stationary(2, [bank(2), bank(3)], by_pass(2))
+        turn(0, bank(4))
+        turn(1, bank(5))
+        tokens_stationary(3, [bank(6), bank(7)], by_pass(3))
+        tokens_stationary(4, [bank(0), bank(1)], by_pass(4))
+        wa_stationary(5, [bank(4), bank(5)])
+        turn(2, bank(2))
+        turn(3, bank(6))
+        turn(4, bank(7))
+        wa_stationary(6, [bank(0), bank(1)])
+        wa_stationary(7, [bank(4), bank(5)])
+        wa_stationary(8, [bank(6), bank(7)])
+
         last = (E - 1) * C
-        for e in range(0, E - 1, 2):
-            quantize_slots(e * C, (e + 2) * C)
+        for first in range(0, last, 2 * C):
+            quantize(first, first + 2 * C)
         for b in range(2):
-            quantize_slots(last + b * P, last + (b + 1) * P)
-        scalar_banks = pair("B")
-        y_banks = [bank("A0"), scalar_banks[0], bank("A1"), scalar_banks[1]]
-        for k in range(4):
-            second_product(2 * k * C, (2 * k + 2) * C, y_banks[k], k in VECTOR_Y)
-        for b, target in enumerate([bank("C"), bank("D")]):
-            second_product(last + b * P, last + (b + 1) * P, target, True)
-        base = [frozen_layer(0, HALF, bank("F")), frozen_layer(HALF, T, bank("E"))]
+            quantize(last + b * P, last + (b + 1) * P)
+        for k, number in enumerate((0, 2, 1, 3)):
+            copy_out = nc.vector.tensor_copy if k == 2 else nc.scalar.copy
+            second_product(2 * k * C, (2 * k + 2) * C, bank(number), copy_out)
+        for b in range(2):
+            second_product(last + b * P, last + (b + 1) * P, bank(4 + b), nc.vector.tensor_copy)
+        base = {half: frozen_layer(half, bank(5 - half)) for half in (1, 0)}
 
-        def add_turned(total, tile, start, stop):
-            nc.tensor.matmul(total, lhsT=tile, rhs=ident[:], is_transpose=True, start=start, stop=stop)
+        turned_y = {}
+        for r, half, number in ((0, 1, 2), (0, 0, 3), (1, 0, 0)):
+            picked = keep.tile([P, HALF], F32, name="picked%d_%d" % (r, half))
+            nc.scalar.activation(picked[:], y[:].indirect(entries(lists[r], half * HALF, (half + 1) * HALF)), COPY)
+            turned_y[r, half] = bank(number)
+            for j in range(PER_HALF):
+                cols = slice(j * P, (j + 1) * P)
+                nc.tensor.transpose(turned_y[r, half][:, cols], picked[:, cols], ident[:])
 
-        def weighted(r, first, last, gates, name):
-            tile = keep.tile([P, last - first], F32, name=name)
-            nc.vector.tensor_tensor(tile[:], y[:].indirect(entries(lists[r], first, last)), gates, MULT)
-            return tile
-
-        jobs = [(0, 1, "B0"), (0, 0, "B1"), (1, 0, "A0")]
-        raw_t = []
-        for r, half, name in jobs:
-            raw = keep.tile([P, HALF], F32, name="raw%d_%d" % (r, half))
-            nc.scalar.activation(raw[:], y[:].indirect(entries(lists[r], half * HALF, (half + 1) * HALF)), COPY)
-            target = bank(name)
-            for j in range(per_half):
-                nc.tensor.transpose(target[:, j * N : (j + 1) * N], raw[:, j * P : (j + 1) * P], ident[:])
-            raw_t.append(target)
+        def weighted(r, half, gates):
+            tile = keep.tile([P, HALF], F32, name="weighted%d_%d" % (r, half))
+            nc.vector.tensor_tensor(tile[:], y[:].indirect(entries(lists[r], half * HALF, (half + 1) * HALF)), gates, MULT)
+            return tile[:]
 
         def added(a, b, name):
             tile = keep.tile([P, HALF], F32, name=name)
             nc.vector.tensor_tensor(tile[:], a, b, ADD)
             return tile[:]
 
-        mid = weighted(1, HALF, T, gate_mid[:], "mid")
-        end = weighted(2, HALF, T, gate_last[:, HALF:T], "end")
-        low = weighted(2, 0, HALF, gate_last[:, 0:HALF], "low")
-        rest = [None, added(base[1], mid[:], "part")]
-        rest[0] = added(base[0], low[:], "rest0")
-        rest[1] = added(rest[1], end[:], "rest1")
+        upper_second = weighted(1, 1, gate_second[:])
+        upper_third = weighted(2, 1, gate_third[:, HALF:T])
+        upper_part = added(base[1], upper_second, "upper_part")
+        lower_third = weighted(2, 0, gate_third[:, 0:HALF])
+        upper_sum = added(upper_part, upper_third, "upper_sum")
+        vector_sums = [added(base[0], lower_third, "lower_sum"), upper_sum]
 
-        turned_raw = {(r, half): target for (r, half, name), target in zip(jobs, raw_t)}
-        runs = ((HALF, T, "C", nc.sync), (0, 2 * P, "D", nc.sync), (2 * P, HALF, "A1", nc.scalar))
-        for first, last, name, queue in runs:
+        for first, last, number, queue in ((HALF, T, 6, nc.sync), (0, 2 * P, 7, nc.sync), (2 * P, HALF, 1, nc.scalar)):
             half = first // HALF
-            total = bank(name)
+            total = bank(number)
             steps = [(block, r) for block in range(first // P, last // P) for r in range(2 - half)]
             for block, r in steps:
-                j = block - half * per_half
+                j = block - half * PER_HALF
                 scaled = keep.tile([P, N], F32, name="scaled%d_%d" % (r, block))
                 nc.scalar.activation(
                     out=scaled[:],
-                    in_=turned_raw[r, half][:, j * N : (j + 1) * N],
+                    in_=turned_y[r, half][:, j * P : (j + 1) * P],
                     func=COPY,
-                    scale=gate_t[r][:, block : block + 1],
+                    scale=gate_columns[r][:, block : block + 1],
                 )
-                cols = slice(block * P - first, (block + 1) * P - first)
-                add_turned(total[:, cols], scaled[:], (block, r) == steps[0], (block, r) == steps[-1])
+                nc.tensor.matmul(
+                    total[:, block * P - first : (block + 1) * P - first],
+                    lhsT=scaled[:],
+                    rhs=ident[:],
+                    is_transpose=True,
+                    start=((block, r) == steps[0]),
+                    stop=((block, r) == steps[-1]),
+                )
             result = keep.tile([P, last - first], F32, name="result%d" % first)
             cols = slice(first - half * HALF, last - half * HALF)
-            nc.vector.tensor_tensor(result[:], total[:, 0 : last - first], rest[half][:, cols], ADD)
+            nc.vector.tensor_tensor(result[:], total[:, 0 : last - first], vector_sums[half][:, cols], ADD)
             queue.dma_start(out=out[:, first:last], in_=result[:])

@@ -224,8 +224,8 @@ def tile_moe_adp_none_kernel(
                 nc.gpsimd.tensor_copy(out=tile[:], in_=wa_sb[e, s].bitcast(U16).rearrange("p (m d) -> p d m", d=4))
                 sorted_wa[e, s] = tile
 
-        def wa_stationary(e, banks):
-            for s, b in by_pass(e):
+        def wa_stationary(e, banks, steps):
+            for s, b in steps:
                 cols = slice(b * P, (b + 1) * P)
                 plane = sorted_planes[:, (e - SORTED_FROM) * PASSES + s, :]
                 for d in range(4):
@@ -296,13 +296,13 @@ def tile_moe_adp_none_kernel(
         turn(1, bank(5))
         tokens_stationary(3, [bank(6), bank(7)], by_pass(3))
         tokens_stationary(4, [bank(0), bank(1)], by_pass(4))
-        wa_stationary(5, [bank(4), bank(5)])
+        wa_stationary(5, [bank(4), bank(5)], by_pass(5))
         turn(2, bank(2))
         turn(3, bank(6))
         turn(4, bank(7))
-        wa_stationary(6, [bank(0), bank(1)])
-        wa_stationary(7, [bank(4), bank(5)])
-        wa_stationary(8, [bank(6), bank(7)])
+        wa_stationary(6, [bank(0), bank(1)], by_block(6))
+        wa_stationary(7, [bank(4), bank(5)], by_block(7))
+        wa_stationary(8, [bank(6), bank(7)], by_block(8))
 
         last = (E - 1) * C
         for first in range(0, last, 2 * C):

from contextlib import ExitStack

import concourse.mybir as mybir
from concourse.masks import make_identity

K, T, E, C, H, N, TOP = 1024, 768, 9, 256, 512, 128, 3
FLOPS = 2 * K * N * T + 2 * E * C * (K * H + H * N)

F32 = mybir.dt.float32
BF16 = mybir.dt.bfloat16
I32 = mybir.dt.int32
U32 = mybir.dt.uint32
U16 = mybir.dt.uint16
U8 = mybir.dt.uint8
FP8X4 = mybir.dt.float8_e4m3fn_x4
FP4X4 = mybir.dt.float4_e2m1fn_x4
MULT = mybir.AluOpType.mult
ADD = mybir.AluOpType.add
COPY = mybir.ActivationFunctionType.Copy

P = 128
PASSES = K // 512
SLOTS = E * C
BANK = 512
PER_COLUMN = 16
HALF = T // 2
PER_HALF = HALF // P
LIFT = 16
SORTED_FROM = 5


def tile_moe_adp_none_kernel(
    tc, x_words, x_scales, w_words, w_scales, wa_words, wa_scales, wb_words, wb_scales, gate, offs, pos1, pos2, pos3, out
):
    nc = tc.nc
    with ExitStack() as ctx:
        keep = ctx.enter_context(tc.tile_pool(name="keep", bufs=1))
        psum = ctx.enter_context(tc.psum_pool(name="psum", bufs=1))

        def sbuf(shape, dtype, name):
            return keep.tile(shape, dtype, name=name, align_bytes=64)

        def bank(number):
            return psum.tile([P, BANK], F32, name="bank%d" % number)[:]

        def load_scale_rows(planes, rows, quarters, queue):
            for q in quarters:
                queue.dma_start(
                    out=planes[q:P:32, :].rearrange("g (c n) -> g c n", c=rows.shape[0]).bitcast(I32),
                    in_=rows[:, q:16:4, :].rearrange("c g n -> g c n").bitcast(I32),
                )

        def lift(dst, src, queue):
            queue.dma_start(out=dst[0 : P - LIFT, :].bitcast(I32), in_=src[LIFT:P, :].bitcast(I32))

        def entries(offsets, first, last):
            return offsets[:, first // PER_COLUMN : last // PER_COLUMN]

        wa_rows = wa_scales.rearrange("e s b n -> (e s) b n")
        wa_sb = {}

        def load_wa(first, last):
            tile = sbuf([P, (last - first) * PASSES, 2 * H], U8, "wa%d" % first)
            rows = wa_words.bitcast(I32)[first:last]
            nc.sync.dma_start(out=tile[:].bitcast(I32), in_=rows.rearrange("e s p n -> p (e s) n"))
            for e in range(first, last):
                for s in range(PASSES):
                    wa_sb[e, s] = tile[:, (e - first) * PASSES + s, :]

        offs_sb = keep.tile([P, SLOTS // PER_COLUMN], U16, name="offs_sb")
        nc.sync.dma_start(offs_sb[:], offs)
        wa_planes = sbuf([P, PASSES * SORTED_FROM * H], U8, "wa_planes")
        turned_rows = wa_rows[0 : PASSES * SORTED_FROM]
        load_scale_rows(wa_planes, turned_rows, [0], nc.scalar)
        stacked = sbuf([P, H], U8, "stacked")
        nc.scalar.dma_start(
            out=stacked[:].bitcast(I32),
            in_=wa_rows[PASSES * SORTED_FROM :].rearrange("c b n -> b c n").bitcast(I32),
        )
        xs = sbuf([P, T], U8, "xs")
        nc.gpsimd.memset(xs[:].bitcast(I32), 0)
        for q in range(4):
            (nc.sync, nc.scalar)[q // 2].dma_start(
                out=xs[q:P:LIFT, :].bitcast(I32),
                in_=x_scales[:, q:16:4, :].rearrange("s g t -> g s t").bitcast(I32),
            )
        xw = sbuf([P, PASSES, T], I32, "xw")
        nc.sync.dma_start(out=xw[:], in_=x_words.rearrange("s p t d -> p s (t d)").bitcast(I32))
        load_scale_rows(wa_planes, turned_rows, [1], nc.scalar)
        load_wa(0, 1)
        load_scale_rows(wa_planes, turned_rows, [2, 3], nc.sync)
        load_wa(1, 3)

        y = keep.tile([P, SLOTS], F32, name="y")
        ident = keep.tile([P, P], F32, name="ident")
        make_identity(nc, ident[:])

        slot_planes, slot_words = {}, {}
        lifted = sbuf([P, SLOTS], U8, "lifted")

        def gather_scales(first, last, queue):
            tile = sbuf([P, (last - first) * C], U8, "slot_scales%d" % first)
            nc.vector.tensor_copy(tile[:], xs[:].indirect(entries(offs_sb, first * C, last * C)))
            lift(lifted[:, first * C : last * C], tile[:], queue)
            for e in range(first, last):
                slot_planes[e] = (tile[:, (e - first) * C : (e - first + 1) * C], lifted[:, e * C : (e + 1) * C])

        def pass_order(e):
            return (0, 1) if e in (0, 1, E - 1) else (1, 0)

        def gather_words(e):
            for s in pass_order(e):
                tile = sbuf([P, C], I32, "slot_words%d_%d" % (e, s))
                nc.vector.tensor_copy(
                    tile[:].bitcast(U32), xw[:, s, :].bitcast(U32).indirect(entries(offs_sb, e * C, (e + 1) * C))
                )
                slot_words[e, s] = tile

        def load_list(pos, name):
            tile = keep.tile([P, T // PER_COLUMN], U16, name=name)
            nc.sync.dma_start(tile[:], pos)
            return tile

        def load_gate_column(r, blocks):
            tile = keep.tile([P, blocks], F32, name="gate_column%d" % r)
            with nc.allow_non_contiguous_dma(reason="one gate value a token and partition"):
                nc.sync.dma_start(out=tile[:], in_=gate[r, 0, 0 : blocks * P].rearrange("(b p) -> p b", p=P))
            return tile

        gather_scales(0, 1, nc.scalar)
        gather_scales(1, 3, nc.sync)
        load_wa(3, SORTED_FROM)
        load_wa(SORTED_FROM, SORTED_FROM + 2)
        gather_words(0)
        gather_scales(3, 5, nc.sync)
        stacked_by_d = sbuf([P, H], U8, "stacked_by_d")
        nc.gpsimd.tensor_copy(
            out=stacked_by_d[:].rearrange("p (d m) -> p d m", d=4), in_=stacked[:].rearrange("p (m d) -> p d m", d=4)
        )
        sorted_planes = sbuf([P, PASSES * (E - SORTED_FROM), H], U8, "sorted_planes")
        for g in range(4):
            nc.sync.dma_start(
                out=sorted_planes[32 * g : 32 * g + 4, :, :].bitcast(I32),
                in_=stacked_by_d[32 * g : 32 * (g + 1), :].bitcast(I32),
            )
        load_wa(SORTED_FROM + 2, E)
        gather_words(1)
        gather_words(2)
        gather_scales(5, 7, nc.sync)
        lists = [load_list(pos, "pos_sb%d" % r) for r, pos in enumerate((pos1, pos2, pos3))]
        gather_words(3)
        gather_words(4)
        gather_scales(7, 8, nc.sync)
        w_sb = sbuf([P, PASSES, 2 * N], U8, "w_sb")
        nc.sync.dma_start(out=w_sb[:].bitcast(I32), in_=w_words.rearrange("s p n -> p s n").bitcast(I32))
        xs_lifted = sbuf([P, T], U8, "xs_lifted")
        lift(xs_lifted[:], xs[:], nc.sync)
        wb_sb = sbuf([P, E, 2 * N], U8, "wb_sb")
        nc.sync.dma_start(out=wb_sb[:].bitcast(I32), in_=wb_words.rearrange("e o p n -> p (e o) n").bitcast(I32))
        w_planes = sbuf([P, PASSES * N], U8, "w_planes")
        load_scale_rows(w_planes, w_scales, range(4), nc.sync)
        gather_words(5)
        gather_words(6)
        gather_scales(8, 9, nc.sync)
        wb_planes = sbuf([P, E * N], U8, "wb_planes")
        load_scale_rows(wb_planes, wb_scales.rearrange("e o b n -> (e o) b n"), range(4), nc.sync)
        gate_second = keep.tile([P, HALF], F32, name="gate_second")
        nc.sync.dma_start(out=gate_second[:], in_=gate[1][:, HALF:T])
        gate_third = keep.tile([P, T], F32, name="gate_third")
        nc.sync.dma_start(out=gate_third[:], in_=gate[2])
        gate_columns = [load_gate_column(0, T // P), load_gate_column(1, PER_HALF)]
        gather_words(7)
        gather_words(8)

        rounded, h_pairs, codes, sorted_wa = {}, {}, {}, {}

        def h_of(e):
            first = e - e % 2
            if first not in h_pairs:
                h_pairs[first] = sbuf([P, (min(first + 2, E) - first) * 4 * C], BF16, "h%d" % first)
            return h_pairs[first][:, (e - first) * 4 * C : (e - first + 1) * 4 * C]

        def tokens_stationary(e, banks, steps):
            for s, b in steps:
                cols = slice(b * P, (b + 1) * P)
                plane = e * PASSES + s
                nc.tensor.matmul_mx(
                    out=banks[b],
                    lhsT=slot_words[e, s][:, cols].bitcast(FP8X4),
                    lhsT_scale=slot_planes[e][s][:, cols],
                    rhs=wa_sb[e, s].bitcast(FP4X4),
                    rhs_scale=wa_planes[:, plane * H : (plane + 1) * H],
                    start=(s == pass_order(e)[0]),
                    stop=(s == pass_order(e)[-1]),
                )
            rounded[e] = keep.tile([P, 2, H], BF16, name="rounded%d" % e)
            for b in range(2):
                nc.scalar.activation(
                    out=rounded[e][:, b, :].rearrange("p (u m d) -> p u m d", u=2, d=2),
                    in_=banks[b].rearrange("p (m u d) -> p u m d", u=2, d=2),
                    func=COPY,
                )

        def by_pass(e):
            return [(s, b) for s in pass_order(e) for b in range(2)]

        def by_block(e):
            return [(s, b) for b in range(2) for s in pass_order(e)]

        def turn(e, target):
            turned = target.rearrange("p (b u j) -> p b u j", b=2, u=2)
            pairs = rounded[e][:].bitcast(F32)
            for b in range(2):
                for u in range(2):
                    nc.tensor.transpose(turned[:, b, u, :], pairs[:, b, u * P : (u + 1) * P], ident[:])
            nc.scalar.copy(
                out=h_of(e).bitcast(F32).rearrange("p (b j u) -> p b j u", b=2, u=2),
                in_=turned.rearrange("p b u j -> p b j u"),
            )

        def sort_columns(e):
            for s in pass_order(e):
                tile = sbuf([P, 4, P], U16, "sorted_wa%d_%d" % (e, s))
                nc.gpsimd.tensor_copy(out=tile[:], in_=wa_sb[e, s].bitcast(U16).rearrange("p (m d) -> p d m", d=4))
                sorted_wa[e, s] = tile

        def wa_stationary(e, banks, steps):
            for s, b in steps:
                cols = slice(b * P, (b + 1) * P)
                plane = sorted_planes[:, (e - SORTED_FROM) * PASSES + s, :]
                for d in range(4):
                    nc.tensor.matmul_mx(
                        out=banks[b][:, d * P : (d + 1) * P],
                        lhsT=sorted_wa[e, s][:, d, :].bitcast(U8).bitcast(FP4X4),
                        lhsT_scale=plane[:, d * P : (d + 1) * P],
                        rhs=slot_words[e, s][:, cols].bitcast(FP8X4),
                        rhs_scale=slot_planes[e][s][:, cols],
                        start=(s == pass_order(e)[0] and d == 0),
                        stop=(s == pass_order(e)[-1] and d == 3),
                    )
            for b in range(2):
                nc.scalar.activation(
                    out=h_of(e)[:, b * 4 * P : (b + 1) * 4 * P].rearrange("p (j d) -> p j d", d=4),
                    in_=banks[b].rearrange("p (d j) -> p j d", d=4),
                    func=COPY,
                )

        def quantize(first, last):
            e = first // C
            words = sbuf([P, last - first], I32, "h_words%d" % first)
            plane = sbuf([P, last - first], U8, "h_plane%d" % first)
            nc.vector.quantize_mx(
                out=words[:].bitcast(FP8X4),
                scales=plane[:],
                in_=h_pairs[e][:, 4 * (first - e * C) : 4 * (last - e * C)],
            )
            for lo in range(first, last, C):
                cols = slice(lo - first, min(lo + C, last) - first)
                codes[lo] = (words[:, cols], plane[:, cols])

        def second_product(first, last, target, copy_out):
            for lo in range(first, last, C):
                e, hi = lo // C, min(lo + C, last)
                nc.tensor.matmul_mx(
                    out=target[:, lo - first : hi - first],
                    lhsT=wb_sb[:, e, :].bitcast(FP4X4),
                    lhsT_scale=wb_planes[:, e * N : (e + 1) * N],
                    rhs=codes[lo][0].bitcast(FP8X4),
                    rhs_scale=codes[lo][1],
                    start=True,
                    stop=True,
                )
            copy_out(out=y[:, first:last], in_=target[:, 0 : last - first])

        def frozen_layer(half, target):
            for lo, width in ((0, 2 * P), (2 * P, P)):
                cols = slice(half * HALF + lo, half * HALF + lo + width)
                for s in range(PASSES):
                    nc.tensor.matmul_mx(
                        out=target[:, lo : lo + width],
                        lhsT=w_sb[:, s, :].bitcast(FP4X4),
                        lhsT_scale=w_planes[:, s * N : (s + 1) * N],
                        rhs=xw[:, s, cols].bitcast(FP8X4),
                        rhs_scale=(xs, xs_lifted)[s][:, cols],
                        start=(s == 0),
                        stop=(s == PASSES - 1),
                    )
            return target[:, 0:HALF]

        for e in range(SORTED_FROM, E):
            sort_columns(e)
        tokens_stationary(0, [bank(0), bank(1)], by_block(0))
        tokens_stationary(1, [bank(4), bank(5)], by_pass(1))
        tokens_stationary(2, [bank(2), bank(3)], by_pass(2))
        turn(0, bank(4))
        turn(1, bank(5))
        tokens_stationary(3, [bank(6), bank(7)], by_pass(3))
        tokens_stationary(4, [bank(0), bank(1)], by_pass(4))
        wa_stationary(5, [bank(4), bank(5)], by_pass(5))
        turn(2, bank(2))
        turn(3, bank(6))
        turn(4, bank(7))
        wa_stationary(6, [bank(0), bank(1)], by_block(6))
        wa_stationary(7, [bank(4), bank(5)], by_block(7))
        wa_stationary(8, [bank(6), bank(7)], by_block(8))

        last = (E - 1) * C
        for first in range(0, last, 2 * C):
            quantize(first, first + 2 * C)
        for b in range(2):
            quantize(last + b * P, last + (b + 1) * P)
        for k, number in enumerate((0, 2, 1, 3)):
            copy_out = nc.vector.tensor_copy if k == 2 else nc.scalar.copy
            second_product(2 * k * C, (2 * k + 2) * C, bank(number), copy_out)
        for b in range(2):
            second_product(last + b * P, last + (b + 1) * P, bank(4 + b), nc.vector.tensor_copy)
        base = {half: frozen_layer(half, bank(5 - half)) for half in (1, 0)}

        turned_y = {}
        for r, half, number in ((0, 1, 2), (0, 0, 3), (1, 0, 0)):
            picked = keep.tile([P, HALF], F32, name="picked%d_%d" % (r, half))
            nc.scalar.activation(picked[:], y[:].indirect(entries(lists[r], half * HALF, (half + 1) * HALF)), COPY)
            turned_y[r, half] = bank(number)
            for j in range(PER_HALF):
                cols = slice(j * P, (j + 1) * P)
                nc.tensor.transpose(turned_y[r, half][:, cols], picked[:, cols], ident[:])

        def weighted(r, half, gates):
            tile = keep.tile([P, HALF], F32, name="weighted%d_%d" % (r, half))
            nc.vector.tensor_tensor(tile[:], y[:].indirect(entries(lists[r], half * HALF, (half + 1) * HALF)), gates, MULT)
            return tile[:]

        def added(a, b, name):
            tile = keep.tile([P, HALF], F32, name=name)
            nc.vector.tensor_tensor(tile[:], a, b, ADD)
            return tile[:]

        upper_second = weighted(1, 1, gate_second[:])
        upper_third = weighted(2, 1, gate_third[:, HALF:T])
        upper_part = added(base[1], upper_second, "upper_part")
        lower_third = weighted(2, 0, gate_third[:, 0:HALF])
        upper_sum = added(upper_part, upper_third, "upper_sum")
        vector_sums = [added(base[0], lower_third, "lower_sum"), upper_sum]

        for first, last, number, queue in ((HALF, T, 6, nc.sync), (0, 2 * P, 7, nc.sync), (2 * P, HALF, 1, nc.scalar)):
            half = first // HALF
            total = bank(number)
            steps = [(block, r) for block in range(first // P, last // P) for r in range(2 - half)]
            for block, r in steps:
                j = block - half * PER_HALF
                scaled = keep.tile([P, N], F32, name="scaled%d_%d" % (r, block))
                nc.scalar.activation(
                    out=scaled[:],
                    in_=turned_y[r, half][:, j * P : (j + 1) * P],
                    func=COPY,
                    scale=gate_columns[r][:, block : block + 1],
                )
                nc.tensor.matmul(
                    total[:, block * P - first : (block + 1) * P - first],
                    lhsT=scaled[:],
                    rhs=ident[:],
                    is_transpose=True,
                    start=((block, r) == steps[0]),
                    stop=((block, r) == steps[-1]),
                )
            result = keep.tile([P, last - first], F32, name="result%d" % first)
            cols = slice(first - half * HALF, last - half * HALF)
            nc.vector.tensor_tensor(result[:], total[:, 0 : last - first], vector_sums[half][:, cols], ADD)
            queue.dma_start(out=out[:, first:last], in_=result[:])
